import numpy as np, ml_dtypes
CORES = [16,18,20,22]
N = 4
BF = ml_dtypes.bfloat16
W, L, S, T, F = 4096, 256, 1, 5, 256
C = W >> S
LEVELS = np.array([800, 900, 1000, 1050, 1100, 1150, 1250, 1400])
def parts(rng):
    d = {"key": rng.integers(0, 256, (N, 8, 16, W)), "em": rng.integers(0, 256, (N, 8, 16, W)), "cl": rng.integers(0, W, (N, 8, 16, C)), "pl": rng.integers(0, W, (N, 8, 16, L)),
         "q": rng.integers(0, 256, (N, 8, 16, L)), "emb": rng.integers(0, 256, (N, 8, 16, 16)), "w": rng.integers(0, 256, (N, 8, 16, 1))}
    base = np.stack([rng.permutation(LEVELS) for r in range(N)]).reshape(N, 8, 1, 1)
    d["th"] = base + rng.integers(-100, 101, (N, 8, 16, 1))
    return d
def pack(d):
    kinds = {"key": BF, "em": BF, "cl": np.int32, "pl": np.int32, "q": BF, "emb": BF, "w": BF, "th": np.float32}
    return {k: np.ascontiguousarray(d[k].reshape(N, 128, -1)).astype(np.float32).astype(t) for k, t in kinds.items()}
def setup_inputs(rng):
    return pack(parts(rng))
def setup_inputs_ties(rng):
    d = parts(rng); o = rng.permutation(8)
    for k in ("key", "q", "emb"): d[k] = 64 * rng.integers(0, 4, d[k].shape)
    d["th"] = 64 * rng.integers(16, 23, (N, 8, 16, 1)) + rng.integers(0, 2, (N, 8, 16, 1))
    d["em"] = rng.integers(0, 2, (N, 8, 16, W)) * rng.choice(np.array([1, 3, 255]), (N, 8, 1, 1))
    d["em"][:, o[0]] = 7; d["em"][:, o[1]] = 0
    for k in ("key", "q", "emb"):
        d[k][:, o[2]] = 0
        d[k][:, o[3]] = rng.integers(0, 32, d[k][:, o[3]].shape)
    d["th"][:, o[2], :, 0] = rng.permutation(np.arange(16) % 3)
    d["th"][:, o[3]] = rng.integers(1, 256, (N, 16, 1))
    return pack(d)
def setup_inputs_ends(rng):
    d = parts(rng); o = rng.permutation(8); ends = np.array([0, 1, W - 2, W - 1])
    d["pl"][:, o[0]] = rng.choice(ends, (N, 16, L)); d["th"][:, o[0]] = 4096
    d["th"][:, o[1]] = 0
    d["pl"][:, o[2]] = rng.integers(0, W, (N, 1, L))
    d["cl"][:, o[3]] = rng.choice(ends, (N, 16, C)); d["th"][:, o[3]] = 1000
    d["cl"][:, o[4]] = rng.integers(0, W, (N, 1, C))
    d["key"][:, o[5]] = d["key"][:, o[5]][:, :, :1]
    d["pl"][:, o[6]] = rng.choice(ends, (N, 16, L))
    d["th"][:, o[7]] = 0; d["w"][:, o[7]] = 0
    return pack(d)
def setup_inputs_lone(rng):
    d = parts(rng); d["th"] = np.zeros((N, 8, 16, 1), np.int64)
    for r in range(N):
        o = rng.permutation(8)
        d["th"][r, o[1], 0] = 4096; d["th"][r, o[2], 15] = 4096; d["th"][r, o[3], 14:] = 4096
        for g in o[4:]: d["th"][r, g, rng.integers(1, 15)] = 4096
    d["th"][rng.integers(0, N)] = 0
    return pack(d)
def setup_inputs_big(rng):
    d = parts(rng); o = rng.permutation(8)
    for k in ("key", "em", "q", "emb"): d[k] = 255 * rng.integers(0, 2, d[k].shape)
    d["w"] = rng.integers(254, 256, d["w"].shape)
    d["th"] = rng.choice(np.array([1785, 1786, 2040, 2041, 2295, 1020, 4080, 4081]), (N, 8, 16, 1))
    d["key"][:, o[0]] = 0; d["q"][:, o[0]] = 255; d["emb"][:, o[0]] = 255; d["w"][:, o[0]] = 255
    d["th"][:, o[0], :, 0] = 4080 + np.arange(16) % 2
    d["em"][:, o[1]] = 255
    d["th"][:, o[2]] = 0
    d["th"][:, o[3]] = 0; d["q"][:, o[3]] = 255; d["emb"][:, o[3]] = 255; d["w"][:, o[3]] = 255
    d["em"][:, o[4]] = 255 - (rng.random((N, 16, W)) < 0.0625)
    return pack(d)
def setup_inputs_spread(rng):
    d = parts(rng)
    for k in ("key", "em", "q", "emb"):
        s = d[k].shape
        d[k] = np.minimum((np.exp2(10 * rng.random(s[:2] + (1, s[3]))) * rng.random(s)).astype(np.int64), 255)
    d["w"] = np.minimum(np.exp2(8 * rng.random(d["w"].shape)).astype(np.int64), 255)
    d["th"] = np.minimum(np.exp2(8 + 4 * rng.random((N, 8, 16, 1))).astype(np.int64), 4096)
    for k in ("pl", "cl"): d[k] = np.minimum((W * rng.random(d[k].shape) ** 3).astype(np.int64), W - 1)
    return pack(d)
def check_inputs(d):
    bad = []
    for k, hi in (("key", 255), ("em", 255), ("cl", W - 1), ("pl", W - 1), ("q", 255), ("emb", 255), ("w", 255), ("th", 4096)):
        a = np.asarray(d[k]).astype(np.float64)
        if not np.all((a >= 0) & (a <= hi) & (a == np.floor(a))): bad.append("whole numbers and range of " + k)
    return bad
def reference(key, em, cl, pl, q, emb, w, th):
    def ints(a): return a.astype(np.float32).astype(np.int32).reshape(N, 8, 16, -1)
    K, E, CL, B, H, TH = ints(key), ints(em), ints(cl), ints(emb), ints(w), ints(th)
    p, x = ints(pl), ints(q)
    toks = [[] for r in range(N)]
    for t in range(T):
        pn, xn = [], []
        for r in range(N):
            at = np.take_along_axis(K[r], p[r].reshape(8, 1, 16 * L), 2).reshape(8, 16, 16, L)
            dist = np.add.reduce(np.abs(at - x[r][:, :, None, :]), axis=1)
            near = dist < TH[r]
            first = np.argmax(near, axis=1)
            lead = np.take_along_axis(p[r], first[:, None, :], 1)[:, 0]
            h = np.add.reduce(H[r] * x[r], axis=1)
            c = np.where(np.any(near, axis=1), lead >> S, h & (C - 1))
            pr = np.where(near, p[r], np.take_along_axis(CL[r], c[:, None, :], 2))
            v = np.add.reduce(np.take_along_axis(E[r], pr.reshape(8, 1, 16 * L), 2).reshape(8, 16, 16, L), axis=2)
            tok = np.argmax(v, axis=1)
            toks[r].append(tok)
            xn.append((x[r] + np.take_along_axis(B[r], tok[:, :, None], 1).transpose(0, 2, 1)) >> 1); pn.append(pr)
        p = np.stack([np.concatenate([(pn[(r - 1) % N][..., :F] + (1 if r == 0 else 0)) & (W - 1), (pn[(r + 1) % N][..., F:] - (1 if r == N - 1 else 0)) & (W - 1)], axis=2) for r in range(N)])
        x = np.stack([np.concatenate([xn[(r - 1) % N][..., :F], xn[(r + 1) % N][..., F:]], axis=2) for r in range(N)])
    yt = np.stack([np.concatenate(a, axis=1) for a in toks])
    return {"yp": p.reshape(N, 128, L).astype(np.float32), "yq": x.reshape(N, 128, L).astype(np.float32).astype(BF), "yt": yt.astype(np.float32)}

@@ -1,0 +1,457 @@
+from concourse.bass import DstId, RemoteDMATransfer
+from concourse.mybir import AluOpType, ActivationFunctionType
+
+STEPS, CH, NL = 5, 2, 128
+NP = 4
+KB = 4096.0
+MAGIC = 8388608.0
+HUGE = 25769803776.0
+CYC, PEC, GAT, HOP, NET = 1.0, 0.5, 1.6, 60.0, 2200.0
+ITERS, TEMP = 40000, 600.0
+
+SCRATCH = {"e8": ("sbuf", [8, 128], "bfloat16"), "ytb": ("sbuf", [8, 1280], "float32")}
+
+
+def _declare(where, dtype, names, cols, per_chunk=False):
+    for nm in names.split():
+        for x in (range(CH) if per_chunk else [""]):
+            SCRATCH["%s%s" % (nm, x)] = (where, [128, cols], dtype)
+
+
+_declare("sbuf", "bfloat16", "keyt emt", 4112)
+_declare("sbuf", "int32", "clt", 2056)
+_declare("sbuf", "int32", "plt fi fj", 256)
+_declare("sbuf", "float32", "ff", 256)
+_declare("sbuf", "float32", "tht kcf cc wf", 1)
+_declare("sbuf", "int32", "kci kcj", 1)
+_declare("sbuf", "bfloat16", "wt", 1)
+_declare("sbuf", "bfloat16", "embt", 16)
+_declare("sbuf", "float16", "embs", 16)
+_declare("sbuf", "bfloat16", "lq", 1536)
+_declare("sbuf", "float16", "lp", 1536)
+_declare("sbuf", "uint16", "lu", 1536)
+_declare("sbuf", "bfloat16", "sq", 1280)
+_declare("sbuf", "float16", "sp sp1", 1280)
+_declare("sbuf", "uint16", "su su1", 1280)
+_declare("sbuf", "bfloat16", "ones idm bma bm ltm lw nid hid mid sid kid bk bgi bg", 128)
+_declare("sbuf", "bfloat16", "gw gk kv", 8)
+_declare("sbuf", "int32", "mki mkj", 128)
+_declare("sbuf", "float32", "mk z0 z1", 128)
+_declare("sbuf", "float16", "ebk", 128)
+_declare("sbuf", "bfloat16", "sl", 2048)
+_declare("psum", "float32", "x0 x1 x2 x3", 512)
+_declare("psum", "float32", "A B", 512, True)
+_declare("sbuf", "bfloat16", "kg", 4096, True)
+_declare("sbuf", "bfloat16", "ab eg", 2048, True)
+_declare("sbuf", "float32", "hi", 8, True)
+_declare("sbuf", "float16", "hf", 8, True)
+_declare("sbuf", "uint16", "ls", 8, True)
+_declare("sbuf", "bfloat16", "far oh on", 128, True)
+_declare("sbuf", "float16", "sel prd vm", 128, True)
+_declare("sbuf", "float32", "g1 bs", 128, True)
+_declare("sbuf", "float32", "fm", 144, True)
+for _c in range(CH):
+    SCRATCH["def%d" % _c] = ("sbuf", [8, 128], "float16")
+
+SEMAPHORES = ["V", "S", "P", "G", "lsem", "ld_pl", "ld_q", "ld_key", "ld_sm", "ld_cl", "ld_em", "st"]
+for _t in range(STEPS):
+    for _c in range(CH):
+        SEMAPHORES += ["ap%d%d" % (_t, _c), "aq%d%d" % (_t, _c)]
+
+
+def make_ops(g, T, topo, core, rank):
+    A, F = AluOpType, ActivationFunctionType
+    V, S, P = g.vector, g.scalar, g.tensor
+    ops = []
+
+    def op(name, qs, fn, rd, wr, banks=(), cost=100.0, sem=None, lat=0.0, skip=False):
+        ops.append(dict(name=name, qs=qs, fn=fn, rd=list(rd), wr=list(wr), banks=list(banks), cost=cost, sem=sem,
+                        lat=lat, skip=skip, i=len(ops)))
+
+    def vop(name, fn, rd, wr, n, banks=()):
+        op(name, "V", lambda q: [fn()], rd, wr, banks, 55 + max(64, n) * CYC)
+
+    def sop(name, fn, rd, wr, n, banks=()):
+        op(name, "S", lambda q: [fn()], rd, wr, banks, 80 + n * CYC)
+
+    def mm(name, mms, rd, wr, banks):
+        op(name, "P", lambda q: [P.matmul(*m[:5]) for m in mms], rd, wr, banks, 10 + sum(max(64, m[5]) for m in mms) * PEC)
+
+    def gop(name, fn, rd, wr, n):
+        op(name, "G", lambda q: [fn()], rd, wr, (), 170 + 2 * n * CYC)
+
+    def ld(name, q, pairs, wr, sem, lat, rd=()):
+        eng = g.sync if q == "Y" else g.scalar
+        op(name, q, lambda _q: [eng.dma_start(o, i) for o, i in pairs], rd, wr, (), 60.0 * len(pairs), sem, lat)
+
+    ld("ld_pl", "Y", [(T.plt[:], T.pl[:])], ["plt"], "ld_pl", 2000)
+    ld("ld_key", "Y", [(T.keyt[:, 0:4096], T.key[:]), (T.keyt[:, 4096:4098], T.key[:, 0:2])], ["keyt"], "ld_key", 4800)
+    ld("ld_sm", "S", [(T.tht[:], T.th[:]), (T.wt[:], T.w[:]), (T.embt[:], T.emb[:])], ["tht", "wt", "embt"], "ld_sm", 2000)
+    ld("ld_q", "S", [(T.lq[:, 0:256], T.q[:])], ["lq00", "lq01"], "ld_q", 2000)
+    ld("ld_cl", "Y", [(T.clt[:, 0:2048], T.cl[:]), (T.clt[:, 2048:2050], T.cl[:, 0:2])], ["clt"], "ld_cl", 7500)
+    ld("ld_em", "Y", [(T.emt[:, 0:4096], T.em[:]), (T.emt[:, 4096:4098], T.em[:, 0:2])], ["emt"], "ld_em", 10500)
+
+    vop("ones", lambda: V.memset(T.ones[:], 1.0), [], ["ones"], 64)
+    vop("slz", lambda: V.memset(T.sl[:], 0.0), [], ["sl"], 1024)
+    for c in range(CH):
+        a, b = c * NL, c * NL + NL
+        vop("u0_%d" % c, lambda a=a, b=b: V.tensor_copy(T.lu[:, a:b], T.plt[:, a:b]), ["plt"], ["lu0%d" % c], 128)
+        vop("p0_%d" % c, lambda a=a, b=b: V.tensor_scalar(T.lp[:, a:b], T.plt[:, a:b], -2048.0, None, A.add), ["plt"],
+            ["lp0%d" % c], 128)
+
+    def sel(name, src, pattern, cmp, base, cm, rows=128):
+        gop(name, lambda: g.affine_select(T[name][:], T[src][0:rows, :], pattern, cmp, 0.0, base, cm), [src], [name], 128)
+
+    def iota(name, pattern, base, cm, n=128, flag=True):
+        kw = dict(allow_small_or_imprecise_dtypes=True) if flag else {}
+        gop(name, lambda: g.iota(T[name][:], pattern, base, cm, **kw), [], [name], n)
+    sel("idm", "ones", [[-1, 128]], A.is_equal, 0, 1)
+    sel("bma", "ones", [[-16, 8], [0, 16]], A.is_ge, 0, 1)
+    sel("bm", "bma", [[16, 8], [0, 16]], A.is_ge, 15, -1)
+    sel("ltm", "bm", [[1, 128]], A.is_gt, 0, -1)
+    iota("kci", [[0, 1]], 0, 1, 1, False)
+    iota("mki", [[0, 8], [-1, 16]], 16, 1, 128, False)
+    sel("e8", "ones", [[-1, 8], [0, 16]], A.is_equal, 0, 1, 8)
+    iota("bk", [[0, 8], [-1, 16]], 15, 0)
+    iota("bgi", [[1, 8], [0, 16]], 0, 0)
+
+    def scaled(name, src, k):
+        vop(name, lambda: V.tensor_scalar(T[name][:], T[src][:], float(k), None, A.mult), [src], [name], 64)
+    scaled("nid", "idm", -1.0)
+    for j in range(8):
+        vop("sl%d" % j, lambda j=j: V.tensor_copy(T.sl[:, 16 * j:16 * j + 129 * 15 + 1:129], T.bm[:, 16 * j:16 * j + 16]),
+            ["bm", "sl"], ["sl_%d" % j], 16)
+    SLK = ["sl"] + ["sl_%d" % x for x in range(8)]
+    scaled("hid", "idm", 0.5)
+    scaled("mid", "idm", -2048.0)
+    scaled("sid", "idm", 16.0)
+    scaled("kid", "idm", KB)
+    scaled("lw", "ltm", KB)
+    vop("lw1", lambda: V.tensor_tensor(T.lw[:], T.lw[:], T.kid[:], A.subtract), ["lw", "kid"], ["lw"], 256)
+    vop("wf", lambda: V.tensor_copy(T.wf[:], T.wt[:]), ["wt"], ["wf"], 1)
+    vop("gw", lambda: V.tensor_scalar(T.gw[:], T.bm[:, 0::16], T.wf[:], None, A.mult), ["bm", "wf"], ["gw"], 8)
+    vop("gk", lambda: V.tensor_scalar(T.gk[:], T.bm[:, 0::16], KB, None, A.mult), ["bm"], ["gk"], 8)
+    vop("kcj", lambda: V.tensor_scalar(T.kcj[:], T.kci[:], 15, None, A.bitwise_and), ["kci"], ["kcj"], 1)
+    vop("kcf", lambda: V.tensor_copy(T.kcf[:], T.kcj[:]), ["kcj"], ["kcf"], 1)
+    vop("cc", lambda: V.tensor_scalar(T.cc[:], T.kcf[:], -KB, 1023.75, A.mult, A.add), ["kcf"], ["cc"], 1)
+    vop("kv", lambda: V.tensor_scalar(T.kv[:], T.bm[:, 0::16], T.kcf[:], None, A.mult), ["bm", "kcf"], ["kv"], 8)
+    vop("mkj", lambda: V.tensor_scalar(T.mkj[:], T.mki[:], 15, None, A.bitwise_and), ["mki"], ["mkj"], 128)
+    vop("mk", lambda: V.tensor_scalar(T.mk[:], T.mkj[:], 0.0, None, A.is_equal), ["mkj"], ["mk"], 128)
+    scaled("bg", "bgi", 65536.0)
+    vop("embs", lambda: V.tensor_scalar(T.embs[:], T.embt[:], 0.5, -0.25, A.mult, A.add), ["embt"], ["embs"], 16)
+    for j in range(8):
+        vop("ebk%d" % j, lambda j=j: V.tensor_tensor(T.ebk[:, 16 * j:16 * j + 16], T.embs[:], T.bm[:, 16 * j:16 * j + 16],
+                                                     A.mult), ["bm", "embs"], ["ebk_%d" % j], 32)
+    EBK = ["ebk_%d" % x for x in range(8)]
+    vop("z0", lambda: V.memset(T.z0[:], 0.0), [], ["z0"], 128)
+    vop("z1", lambda: V.memset(T.z1[:], 0.0), [], ["z1"], 128)
+    vop("z1b", lambda: V.memset(T.z1[:, 0::16], 4194304.0), ["z1"], ["z1"], 8)
+    for c in range(CH):
+        vop("fmt%d" % c, lambda c=c: V.memset(T["fm%d" % c][:, 128:144], 8388608.0), [], ["fmt%d" % c], 16)
+
+    nxt = T.cores[(rank + 1) % len(T.cores)]
+    rid, pid = topo.addr(nxt)[0], topo.addr(nxt)[1]
+    eng = topo.engines(core, nxt)
+    m_all, m_a, m_b = sum(1 << e for e in eng), sum(1 << e for e in eng[0::2]), sum(1 << e for e in eng[1::2])
+    last_rank = rank == len(T.cores) - 1
+    win_k, win_e, win_c = T.keyt[:, 0:4098], T.emt[:, 0:4098], T.clt[:, 0:2050]
+    LP = NL // NP
+    X = [T.x0, T.x1, T.x2, T.x3]
+
+    def gather(name, dst, win, lst, rd, wr, n):
+        def emit(q):
+            if q == "V":
+                return [V.tensor_copy(dst, win.indirect(lst))]
+            return [S.activation(dst, win.indirect(lst), F.Copy)]
+        op(name, "VS", emit, rd, wr, (), 60 + n * GAT)
+
+    def step(t, c):
+        n, nn = "%d%d" % (t, c), "%d%d" % (t + 1, c)
+        o = t * 256 + c * NL
+        here, dst = slice(o, o + NL), slice(o + 256, o + 256 + NL)
+        p, q = T.lp[:, here], T.lq[:, here]
+        Ab, Bb = T["A%d" % c], T["B%d" % c]
+        bA, bB = "bA%d" % c, "bB%d" % c
+        A1, A2, B0, B1 = "A1%d" % c, "A2%d" % c, "B0%d" % c, "B1%d" % c
+        kg, ab, hi, hf, far, se, prd, vm, ls, g1, eg, fm, bs, oh, on, dfl = (T[x + str(c)] for x in (
+            "kg ab hi hf far sel prd vm ls g1 eg fm bs oh on def".split()))
+
+        def k(x):
+            return "%s%d" % (x, c)
+        ko = (t % 2) * 2048
+        kr = ["kg%d%d_%d" % (c, t % 2, j) for j in range(NP)]
+        for j in range(NP):
+            gather("kg%s_%d" % (n, j), kg[:, ko + 16 * LP * j:ko + 16 * LP * (j + 1)], win_k,
+                   T.lu[:, o + LP * j:o + LP * (j + 1)], ["keyt", "lu" + n], [kr[j]], 16 * LP)
+        mm("h" + n, [(Bb[:, 128:136], q, T.gw[:], True, True, 8)], ["lq" + n, "gw"], [B1], [bB])
+        vop("hi" + n, lambda: V.tensor_scalar(hi[:], Bb[:, 128:136], -1023.5, HUGE, A.add, A.add), [B1], [k("hi")], 8, [bB])
+        vop("hf" + n, lambda: V.tensor_scalar(hf[:], hi[:], -HUGE, 1.0 / 2048.0, A.add, A.mult), [k("hi")], [k("hf")], 8)
+        for b in range(4):
+            mm("xk%s_%d" % (n, b), [(X[b][:, 128 * j:128 * j + 128], T.idm[:], kg[:, ko + 4 * b + j:ko + 2048:16], j == 0,
+                                     False, 128) for j in range(4)], kr + ["idm"], ["x%d" % b], ["bx%d" % b])
+        for b in range(4):
+            mm("xq%s_%d" % (n, b), [(X[b][:, 128 * j:128 * j + 128], T.nid[:], q, False, j == 3, 128) for j in range(4)],
+               ["lq" + n, "nid"], ["x%d" % b], ["bx%d" % b])
+            sop("ab%s_%d" % (n, b), lambda b=b: S.activation(ab[:, 512 * b:512 * b + 512], X[b][:], F.Abs), ["x%d" % b],
+                ["ab%d_%d" % (c, b)], 512, ["bx%d" % b])
+            mm("d%s_%d" % (n, b), [(Ab[:, 0:128], T.sl[:, 128 * s:128 * s + 128], ab[:, 128 * s:128 * s + 128], s == 0,
+                                    s == 15, 128) for s in range(4 * b, 4 * b + 4)], ["ab%d_%d" % (c, b)] + SLK, [k("d")], [bA])
+        vop("far" + n, lambda: V.tensor_scalar(far[:], Ab[:, 0:128], T.tht[:], None, A.is_ge), [k("d"), "tht"], [k("far")],
+            128, [bA])
+        mm("y" + n, [(Bb[:, 0:128], T.hid[:], p, True, False, 128), (Bb[:, 0:128], T.lw[:], far[:], False, True, 128)],
+           [k("far"), "lp" + n, "hid", "lw"], [B0], [bB])
+        y2 = Ab[0:8, 384:512]
+        mm("y2" + n, [(y2, T.gw[:], q, True, False, 128), (y2, hf[:], T.mid[:], False, False, 128),
+                      (y2, T.gk[:], far[:], False, True, 128)],
+           [k("far"), k("hf"), "lq" + n, "gw", "mid", "gk"], [k("y2")], [bA])
+        mm("f2" + n, [(Ab[:, 128:256], T.idm[:], far[:], True, True, 128)], [k("far"), "idm"], [A1], [bA])
+        vop("sel" + n, lambda: V.tensor_scalar(se[:], Bb[:, 0:128], T.cc[:], 0.0, A.add, A.max), [B0, "cc"], [k("sel")],
+            128, [bB])
+        vop("def" + n, lambda: V.tensor_scalar(dfl[:], y2, -16 * KB, 0.0, A.add, A.max), [k("y2")], [k("def")], 128, [bA])
+        mm("ex" + n, [(Bb[:, 128:256], se[:], T.bm[:], True, False, 128), (Bb[:, 128:256], dfl[:], T.e8[:], False, True, 128)],
+           [k("sel"), k("def"), "bm", "e8"], [B1], [bB])
+        vop("prd" + n, lambda: V.tensor_tensor(prd[:], Ab[:, 128:256], p, A.mult), [A1, "lp" + n], [k("prd")], 128, [bA])
+        vop("vm" + n, lambda: V.tensor_tensor(vm[:], Bb[:, 128:256], T.mk[:], A.mult), [B1, "mk"], [k("vm")], 128, [bB])
+        mm("l" + n, [(Bb[:, 0:8], vm[:], T.bm[:, 0::16], True, True, 8)], [k("vm"), "bm"], [B0], [bB])
+        z = Ab[:, 256:384]
+        mm("z" + n, [(z, T.idm[:], p, True, False, 128), (z, T.mid[:], far[:], False, False, 128),
+                     (z, T.nid[:], prd[:], False, True, 128)],
+           ["lp" + n, k("far"), k("prd"), "idm", "mid", "nid"], [A2], [bA])
+        vop("ls" + n, lambda: V.tensor_scalar(ls[:], Bb[:, 0:8], MAGIC, -MAGIC, A.add, A.add), [B0], [k("ls")], 8, [bB])
+        vop("g1" + n, lambda: V.tensor_tensor(g1[:], win_c.indirect(ls[:]), far[:], A.mult), ["clt", k("ls"), k("far")],
+            [k("g1")], 200)
+        sp, su, sp1, su1 = T.sp[:, here], T.su[:, here], T.sp1[:, here], T.su1[:, here]
+        vop("pn" + n, lambda: V.tensor_tensor(sp, g1[:], z, A.add), [k("g1"), A2], ["sp" + n], 128, [bA])
+        vop("un" + n, lambda: V.tensor_scalar(su, sp, 2048.0, None, A.add), ["sp" + n], ["su" + n], 64)
+        last = t == STEPS - 1
+        op("up" + n, "V", lambda _q: [V.tensor_scalar(su1, sp, 2049.0, None, A.add)], ["sp" + n], ["su1" + n], (), 115,
+           skip=not last_rank)
+        if not last:
+            op("pp" + n, "V", lambda _q: [V.tensor_scalar(sp1, sp, 1.0, None, A.add)], ["sp" + n], ["sp1" + n], (), 115,
+               skip=not last_rank)
+        hu, hp = (su1, sp1) if last_rank else (su, sp)
+
+        def send_p(_q):
+            if last:
+                g.remote_dma(T.lu[:, dst], hu, T.sem["ap" + n], T.sem.lsem, pid, rid, m_all)
+                return None
+            g.remote_dma_fused([RemoteDMATransfer(dst_ids=[DstId(rid=rid, pnc=pid)], dma_engine_mask=m,
+                                                  remote_sem=T.sem["ap" + n], src=s, dst=d)
+                                for m, s, d in ((m_a, hu, T.lu[:, dst]), (m_b, hp, T.lp[:, dst]))], local_sem=T.sem.lsem)
+            return None
+        op("sendp" + n, "G", send_p, ["su" + n, "su1" + n] + ([] if last else ["sp" + n, "sp1" + n]),
+           ["lu" + nn] + ([] if last else ["lp" + nn]), (), 150, "ap" + n, NET)
+        if last:
+            r = slice(c * NL, c * NL + NL)
+            vop("fi%d" % c, lambda: V.tensor_copy(T.fi[:, r], T.lu[:, dst]), ["lu" + nn], [k("fi")], 128)
+            vop("fj%d" % c, lambda: V.tensor_scalar(T.fj[:, r], T.fi[:, r], 4095, None, A.bitwise_and), [k("fi")], [k("fj")], 128)
+            vop("ff%d" % c, lambda: V.tensor_copy(T.ff[:, r], T.fj[:, r]), [k("fj")], [k("ff")], 128)
+            ld("stp%d" % c, "Y", [(T.yp[:, r], T.ff[:, r])], ["yp%d" % c], "st", 2000, [k("ff")])
+        for j in range(NP):
+            gather("eg%s_%d" % (n, j), eg[:, 16 * LP * j:16 * LP * (j + 1)], win_e, T.su[:, o + LP * j:o + LP * (j + 1)],
+                   ["emt", "su" + n], ["eg%d_%d" % (c, j)], 16 * LP)
+        v = Ab[:, 128:256]
+        mm("v" + n, [(v, T.ones[0:1, :], T.bk[0:1, :], True, False, 128), (v, T.ones[0:1, :], T.bg[0:1, :], False, False, 128)]
+           + [(v, eg[:, s::16], T.sid[:], False, s == 15, 128) for s in range(16)],
+           ["eg%d_%d" % (c, j) for j in range(NP)] + ["ones", "bk", "bg", "sid"], [A1], [bA])
+        vop("fm" + n, lambda: V.tensor_tensor_scan(fm[:, 0:128], T.z0[:], v, 0.0, A.add, A.max), [A1, "z0"], [k("fm")], 128, [bA])
+        vop("bs" + n, lambda: V.tensor_tensor_scan(bs[:], T.z1[:], fm[:, 15:143], 0.0, A.add, A.min),
+            [k("fm"), k("fmt"), "z1"], [k("bs")], 128)
+        vop("oh" + n, lambda: V.tensor_tensor(oh[:], v, bs[:], A.is_equal), [A1, k("bs")], [k("oh")], 128, [bA])
+        mm("on" + n, [(Bb[:, 256:384], oh[:], T.idm[:], True, True, 128)], [k("oh"), "idm"], [k("onp")], [bB])
+        sop("ons" + n, lambda: S.activation(on[:], Bb[:, 256:384], F.Copy), [k("onp")], [k("on")], 128, [bB])
+        e = Bb[:, 384:512]
+        mm("e" + n, [(e, T.hid[:], q, True, False, 128), (e, T.ebk[:], on[:], False, True, 128)],
+           ["lq" + n, k("on"), "hid"] + EBK, [k("e")], [bB])
+        sq = T.sq[:, here]
+        vop("qn" + n, lambda: V.tensor_scalar(sq, e, MAGIC, -MAGIC, A.add, A.add), [k("e")], ["sq" + n], 128, [bB])
+
+        def send_q(_q):
+            g.remote_dma(T.lq[:, dst], sq, T.sem["aq" + n], T.sem.lsem, pid, rid, m_all)
+            return None
+        op("sendq" + n, "G", send_q, ["sq" + n], ["lq" + nn], (), 150, "aq" + n, NET)
+        mm("tk" + n, [(Ab[0:8, 256:384], T.kv[:], on[:], True, True, 128)], [k("on"), "kv"], [A2], [bA])
+        sop("yt" + n, lambda: S.activation(T.ytb[:, here], Ab[0:8, 256:384], F.Copy), [A2], ["yt" + n], 128, [bA])
+        if last:
+            ld("stq%d" % c, "Y", [(T.yq[:, c * NL:c * NL + NL], T.lq[:, dst])], ["yq%d" % c], "st", 2000, ["lq" + nn])
+            if c == CH - 1:
+                ld("stt", "Y", [(T.yt[:], T.ytb[:])], ["ytd"], "st", 2000,
+                   ["yt%d%d" % (x, y) for x in range(STEPS) for y in range(CH)])
+
+    for t in range(STEPS):
+        for c in range(CH):
+            step(t, c)
+    return ops
+
+
+def depend(ops):
+    wr, rds, bank = {}, {}, {}
+    for o in ops:
+        d = set()
+        for k in o["rd"]:
+            if k in wr:
+                d.add(wr[k])
+        for k in o["wr"]:
+            if k in wr:
+                d.add(wr[k])
+            d.update(rds.get(k, ()))
+        for b in o["banks"]:
+            turn = bank.setdefault(b, ["", [], []])
+            if turn[0] != o["qs"]:
+                turn[0], turn[1], turn[2] = o["qs"], turn[2], []
+            d.update(turn[1])
+            turn[2].append(o["i"])
+        for k in o["rd"]:
+            rds.setdefault(k, []).append(o["i"])
+        for k in o["wr"]:
+            wr[k] = o["i"]
+            rds[k] = []
+        d.discard(o["i"])
+        o["deps"] = sorted(d)
+
+
+def schedule(ops):
+    n = len(ops)
+    succ = [[] for _ in ops]
+    for o in ops:
+        for d in o["deps"]:
+            succ[d].append(o["i"])
+    bl = [0.0] * n
+    for i in range(n - 1, -1, -1):
+        bl[i] = ops[i]["cost"] + ops[i]["lat"] + max([bl[s] + HOP for s in succ[i]] or [0.0])
+    left = [len(o["deps"]) for o in ops]
+    done, ready, free, order = [0.0] * n, {i: 0.0 for i in range(n) if left[i] == 0}, {}, []
+    while ready:
+        st, _, i, q = min((max(r, free.get(q, 0.0)), -bl[i], i, q) for i, r in ready.items() for q in ops[i]["qs"])
+        for j, r in ready.items():
+            if q in ops[j]["qs"] and max(r, free.get(q, 0.0)) <= st + 200.0 and (-bl[j], j) < (-bl[i], i):
+                i = j
+        st = max(ready.pop(i), free.get(q, 0.0))
+        ops[i]["q"] = q
+        free[q] = st + ops[i]["cost"]
+        done[i] = free[q] + ops[i]["lat"]
+        order.append(i)
+        for s in succ[i]:
+            left[s] -= 1
+            if left[s] == 0:
+                ready[s] = max(done[d] for d in ops[s]["deps"]) + HOP
+    return order
+
+
+def improve(ops, order, iters):
+    n = len(ops)
+    cost, lat = [o["cost"] for o in ops], [o["lat"] for o in ops]
+    deps = [o["deps"] for o in ops]
+    qof = [o["q"] for o in ops]
+
+    def run(seq, qs):
+        end, done, pred, free, lastq = [0.0] * n, [0.0] * n, [-1] * n, {}, {}
+        for i in seq:
+            q = qs[i]
+            st, pr = free.get(q, 0.0), lastq.get(q, -1)
+            for d in deps[i]:
+                r = done[d] + HOP
+                if r > st:
+                    st, pr = r, d
+            free[q] = end[i] = st + cost[i]
+            done[i] = end[i] + lat[i]
+            pred[i], lastq[q] = pr, i
+        return done, pred
+    done, pred = run(order, qof)
+    best = cur = max(done)
+    bo, bq = list(order), list(qof)
+    order, seed = list(order), 12345
+    for it in range(iters):
+        seed = (seed * 1103515245 + 12345) % 2147483648
+        path = []
+        i = done.index(max(done))
+        while i >= 0:
+            path.append(i)
+            i = pred[i]
+        cand = [i for i in path if pred[i] >= 0 and pred[i] not in deps[i]] + [i for i in path if len(ops[i]["qs"]) > 1]
+        if not cand:
+            break
+        i = cand[(seed >> 8) % len(cand)]
+        nq, no = qof, list(order)
+        if len(ops[i]["qs"]) > 1 and (seed >> 5) % 3 == 0:
+            nq = list(qof)
+            nq[i] = "S" if qof[i] == "V" else "V"
+        else:
+            j = pred[i]
+            if j < 0 or j in deps[i]:
+                continue
+            a, b = no.index(j), no.index(i)
+            need, head, tail = {i}, [], []
+            for x in reversed(no[a:b + 1]):
+                if x in need:
+                    need.update(deps[x])
+                    head.append(x)
+                else:
+                    tail.append(x)
+            if j in need:
+                continue
+            no[a:b + 1] = head[::-1] + tail[::-1]
+        d2, p2 = run(no, nq)
+        m = max(d2)
+        temp = TEMP * (1.0 - it / iters)
+        if m <= cur or (seed >> 3) % 1000 < 1000.0 * 2.718281828 ** (-(m - cur) / (temp + 0.01)):
+            order, qof, done, pred, cur = no, nq, d2, p2, m
+            if m < best:
+                best, bo, bq = m, list(no), list(nq)
+    for o in ops:
+        o["q"] = bq[o["i"]]
+    return bo, best
+
+
+PLAN = {}
+
+
+def rank_program(g, core, T, topo):
+    rank = T.rank_of(core)
+    if rank is None:
+        return
+    ops = make_ops(g, T, topo, core, rank)
+    depend(ops)
+    if "order" not in PLAN:
+        PLAN["order"], PLAN["best"] = improve(ops, schedule(ops), ITERS)
+        PLAN["q"] = [o["q"] for o in ops]
+    eng = {"V": g.vector, "S": g.scalar, "P": g.tensor, "G": g, "Y": g.sync}
+    known = {q: {} for q in eng}
+    count = {"V": 0, "S": 0, "P": 0, "G": 0}
+    snap, token, stores, lsem = {}, {}, 0, 0
+    for i in PLAN["order"]:
+        o, q = ops[i], PLAN["q"][i]
+        kn, toks = known[q], []
+        for d in o["deps"]:
+            if not (PLAN["q"][d] == "P" and q == "P"):
+                toks += token[d]
+        if o["skip"]:
+            token[i] = toks
+            continue
+        for s, v in sorted(toks, key=lambda x: (-x[1], x[0])):
+            if kn.get(s, 0) < v:
+                eng[q].wait_ge(T.sem[s], v)
+                kn[s] = v
+                for s2, v2 in snap.get((s, v), {}).items():
+                    kn[s2] = max(kn.get(s2, 0), v2)
+        out = o["fn"](q)
+        if out is None:
+            lsem += 16
+            token[i] = [(o["sem"], 16)]
+            continue
+        for x in out:
+            x.then_inc(T.sem[o["sem"] or q], 16 if o["sem"] else 1)
+        if o["sem"] == "st":
+            stores += 16
+            token[i] = []
+            continue
+        if o["sem"]:
+            token[i] = [(o["sem"], 16 * len(out))]
+        else:
+            count[q] += len(out)
+            token[i] = [(q, count[q])]
+        snap[token[i][0]] = dict(kn)
+    for s in sorted(count):
+        g.wait_ge(T.sem[s], count[s])
+    g.wait_ge(T.sem.lsem, lsem)
+    g.wait_ge(T.sem.st, stores)

@@ -2,14 +2,15 @@ from concourse.bass import DstId, RemoteDMATransfer
 from concourse.mybir import AluOpType, ActivationFunctionType
 
 STEPS, CH, NL = 5, 2, 128
-NP = 4
-KB = 4096.0
-MAGIC = 8388608.0
-HUGE = 25769803776.0
-CYC, PEC, GAT, HOP, NET = 1.0, 0.5, 1.6, 60.0, 2200.0
-ITERS, TEMP = 40000, 600.0
+KP = [32, 32, 32, 32]
+EP = [32, 32, 32, 32]
+NABS = 2
+MAGIC = 12582912.0
+MODELS = [(0.87, 1.3, 0.44, 60.0, 1700.0, 330.0), (1.1, 1.7, 0.55, 60.0, 2100.0, 260.0)]
+ITERS, TEMP = 15000, 300.0
 
-SCRATCH = {"e8": ("sbuf", [8, 128], "bfloat16"), "ytb": ("sbuf", [8, 1280], "float32")}
+SCRATCH = {"thr": ("sbuf", [1, 128], "float32"), "thh": ("sbuf", [1, 128], "float16"), "wr": ("sbuf", [1, 128], "bfloat16"),
+           "cb": ("sbuf", [1, 256], "bfloat16"), "cx": ("sbuf", [1, 256], "float16")}
 
 
 def _declare(where, dtype, names, cols, per_chunk=False):
@@ -18,42 +19,41 @@ def _declare(where, dtype, names, cols, per_chunk=False):
             SCRATCH["%s%s" % (nm, x)] = (where, [128, cols], dtype)
 
 
-_declare("sbuf", "bfloat16", "keyt emt", 4112)
+_declare("sbuf", "bfloat16", "keyt", 4128)
+_declare("sbuf", "bfloat16", "emt", 4112)
 _declare("sbuf", "int32", "clt", 2056)
-_declare("sbuf", "int32", "plt fi fj", 256)
-_declare("sbuf", "float32", "ff", 256)
-_declare("sbuf", "float32", "tht kcf cc wf", 1)
+_declare("sbuf", "int32", "plt", 256)
+_declare("sbuf", "float32", "sf lf", 256)
+_declare("sbuf", "float32", "ytb", 512)
+_declare("sbuf", "float32", "kcf", 1)
 _declare("sbuf", "int32", "kci kcj", 1)
-_declare("sbuf", "bfloat16", "wt", 1)
 _declare("sbuf", "bfloat16", "embt", 16)
 _declare("sbuf", "float16", "embs", 16)
 _declare("sbuf", "bfloat16", "lq", 1536)
-_declare("sbuf", "float16", "lp", 1536)
-_declare("sbuf", "uint16", "lu", 1536)
+_declare("sbuf", "float16", "lp sp", 1280)
+_declare("sbuf", "uint16", "lu su", 1280)
 _declare("sbuf", "bfloat16", "sq", 1280)
-_declare("sbuf", "float16", "sp sp1", 1280)
-_declare("sbuf", "uint16", "su su1", 1280)
-_declare("sbuf", "bfloat16", "ones idm bma bm ltm lw nid hid mid sid kid bk bgi bg", 128)
-_declare("sbuf", "bfloat16", "gw gk kv", 8)
-_declare("sbuf", "int32", "mki mkj", 128)
-_declare("sbuf", "float32", "mk z0 z1", 128)
+_declare("sbuf", "bfloat16", "ones idm bma bm nid hid sid kid mid nq", 128)
+_declare("sbuf", "bfloat16", "gw g2 gn", 8)
+_declare("sbuf", "bfloat16", "kv", 32)
+_declare("sbuf", "bfloat16", "ga gb r0 r1", 64)
+_declare("sbuf", "float32", "z8", 64)
+_declare("sbuf", "float32", "zf zb", 128)
 _declare("sbuf", "float16", "ebk", 128)
-_declare("sbuf", "bfloat16", "sl", 2048)
-_declare("psum", "float32", "x0 x1 x2 x3", 512)
-_declare("psum", "float32", "A B", 512, True)
+_declare("sbuf", "bfloat16", "c2k fa", 1024)
+_declare("psum", "float32", "x0 x1 xr tk", 512)
+_declare("psum", "float32", "D B", 512, True)
 _declare("sbuf", "bfloat16", "kg", 4096, True)
 _declare("sbuf", "bfloat16", "ab eg", 2048, True)
-_declare("sbuf", "float32", "hi", 8, True)
-_declare("sbuf", "float16", "hf", 8, True)
+_declare("sbuf", "float16", "qx", 8, True)
 _declare("sbuf", "uint16", "ls", 8, True)
-_declare("sbuf", "bfloat16", "far oh on", 128, True)
-_declare("sbuf", "float16", "sel prd vm", 128, True)
-_declare("sbuf", "float32", "g1 bs", 128, True)
-_declare("sbuf", "float32", "fm", 144, True)
-for _c in range(CH):
-    SCRATCH["def%d" % _c] = ("sbuf", [8, 128], "float16")
+_declare("sbuf", "bfloat16", "sg", 256, True)
+_declare("sbuf", "float16", "sc", 256, True)
+_declare("sbuf", "float32", "s2", 64, True)
+_declare("sbuf", "bfloat16", "yy oh on fl", 128, True)
+_declare("sbuf", "float32", "g1 fm bs", 128, True)
 
-SEMAPHORES = ["V", "S", "P", "G", "lsem", "ld_pl", "ld_q", "ld_key", "ld_sm", "ld_cl", "ld_em", "st"]
+SEMAPHORES = ["V", "S", "P", "G", "lsem", "ld_pl", "ld_q", "ld_key", "ld_th", "ld_w", "ld_emb", "ld_cl", "ld_em", "st"]
 for _t in range(STEPS):
     for _c in range(CH):
         SEMAPHORES += ["ap%d%d" % (_t, _c), "aq%d%d" % (_t, _c)]
@@ -62,221 +62,271 @@ for _t in range(STEPS):
 def make_ops(g, T, topo, core, rank):
     A, F = AluOpType, ActivationFunctionType
     V, S, P = g.vector, g.scalar, g.tensor
-    ops = []
+    ops, groups = [], {}
 
-    def op(name, qs, fn, rd, wr, banks=(), cost=100.0, sem=None, lat=0.0, skip=False):
-        ops.append(dict(name=name, qs=qs, fn=fn, rd=list(rd), wr=list(wr), banks=list(banks), cost=cost, sem=sem,
-                        lat=lat, skip=skip, i=len(ops)))
+    def op(name, qs, fn, rd, wr, banks=(), cost=None, sem=None):
+        ops.append(dict(name=name, qs=qs, fn=fn, rd=list(rd), wr=list(wr), banks=list(banks), cost=cost, sem=sem, i=len(ops)))
 
     def vop(name, fn, rd, wr, n, banks=()):
-        op(name, "V", lambda q: [fn()], rd, wr, banks, 55 + max(64, n) * CYC)
+        op(name, "V", lambda q: [fn()], rd, wr, banks, ("c", n, n))
 
     def sop(name, fn, rd, wr, n, banks=()):
-        op(name, "S", lambda q: [fn()], rd, wr, banks, 80 + n * CYC)
+        op(name, "S", lambda q: [fn()], rd, wr, banks, ("c", n, n))
 
-    def mm(name, mms, rd, wr, banks):
-        op(name, "P", lambda q: [P.matmul(*m[:5]) for m in mms], rd, wr, banks, 10 + sum(max(64, m[5]) for m in mms) * PEC)
+    def vs(name, out, src, scale, bias, rd, wr, n, banks=()):
+        def emit(q):
+            if q == "V":
+                return [V.tensor_scalar(out, src, scale, bias, A.mult, A.add)]
+            return [S.activation(out, src, F.Identity, bias, scale) if bias else S.activation(out, src, F.Copy, 0.0, scale)]
+        op(name, "VS", emit, rd, wr, banks, ("c", n, n))
+
+    def mm(name, grp, mms, rd, wr, banks):
+        st = groups.setdefault(grp, [0, 0])
+        st[0] += len(mms)
+
+        def emit(q):
+            r = []
+            for m in mms:
+                st[1] += 1
+                r.append(P.matmul(m[0], m[1], m[2], st[1] == 1 and grp[0] != "+", st[1] == st[0]))
+            return r
+        op(name, "P", emit, rd, wr, banks, ("p", sum(m[3] for m in mms)))
 
     def gop(name, fn, rd, wr, n):
-        op(name, "G", lambda q: [fn()], rd, wr, (), 170 + 2 * n * CYC)
+        op(name, "G", lambda q: [fn()], rd, wr, (), ("g", n))
 
-    def ld(name, q, pairs, wr, sem, lat, rd=()):
+    def dma(name, q, pairs, rd, wr, sem, nbytes):
         eng = g.sync if q == "Y" else g.scalar
-        op(name, q, lambda _q: [eng.dma_start(o, i) for o, i in pairs], rd, wr, (), 60.0 * len(pairs), sem, lat)
+        op(name, q, lambda _q: [eng.dma_start(o, i) for o, i in pairs], rd, wr, (), ("d", nbytes, len(pairs)), sem)
 
-    ld("ld_pl", "Y", [(T.plt[:], T.pl[:])], ["plt"], "ld_pl", 2000)
-    ld("ld_key", "Y", [(T.keyt[:, 0:4096], T.key[:]), (T.keyt[:, 4096:4098], T.key[:, 0:2])], ["keyt"], "ld_key", 4800)
-    ld("ld_sm", "S", [(T.tht[:], T.th[:]), (T.wt[:], T.w[:]), (T.embt[:], T.emb[:])], ["tht", "wt", "embt"], "ld_sm", 2000)
-    ld("ld_q", "S", [(T.lq[:, 0:256], T.q[:])], ["lq00", "lq01"], "ld_q", 2000)
-    ld("ld_cl", "Y", [(T.clt[:, 0:2048], T.cl[:]), (T.clt[:, 2048:2050], T.cl[:, 0:2])], ["clt"], "ld_cl", 7500)
-    ld("ld_em", "Y", [(T.emt[:, 0:4096], T.em[:]), (T.emt[:, 4096:4098], T.em[:, 0:2])], ["emt"], "ld_em", 10500)
+    first = rank == 0
+    last_rank = rank == len(T.cores) - 1
+    k0 = 15 if first else 16
+
+    vop("kz", lambda: V.memset(T.keyt[:, 0:16], 0.0), [], ["kz"], 16)
+    dma("ld_pl", "Y", [(T.plt[:], T.pl[:])], [], ["plt", "o1"], "ld_pl", 131072)
+    dma("ld_th", "S", [(T.thr[:], T.th[:])], [], ["thr", "o2"], "ld_th", 8192)
+    dma("ld_w", "S", [(T.wr[:], T.w[:])], ["+o2"], ["wr", "o3"], "ld_w", 8192)
+    dma("ld_key", "Y", [(T.keyt[:, k0:k0 + 4096], T.key[:])], ["kz", "+o1", "+o3"], ["keyt", "o4"], "ld_key", 1048576)
+    dma("ld_q", "S", [(T.lq[:, 0:256], T.q[:])], ["+o4"], ["lq00", "lq01", "o5"], "ld_q", 65536)
+    dma("ld_emb", "S", [(T.embt[:], T.emb[:])], ["+o5"], ["embt", "o6"], "ld_emb", 65536)
+    dma("ld_cl", "Y", [(T.clt[:, 0:2048], T.cl[:])], ["+o6"], ["clt0", "o7"], "ld_cl", 1048576)
+    dma("ld_em", "Y", [(T.emt[:, 0:4096], T.em[:])], ["+o7"], ["emt"], "ld_em", 1048576)
 
     vop("ones", lambda: V.memset(T.ones[:], 1.0), [], ["ones"], 64)
-    vop("slz", lambda: V.memset(T.sl[:], 0.0), [], ["sl"], 1024)
+    vop("c2k", lambda: V.memset(T.c2k[:], 2048.0), [], ["c2k"], 512)
     for c in range(CH):
         a, b = c * NL, c * NL + NL
-        vop("u0_%d" % c, lambda a=a, b=b: V.tensor_copy(T.lu[:, a:b], T.plt[:, a:b]), ["plt"], ["lu0%d" % c], 128)
+        vop("u0_%d" % c, lambda a=a, b=b: V.tensor_scalar(T.lu[:, a:b], T.plt[:, a:b], 15.0 if first else 0.0, None, A.add),
+            ["plt"], ["lu0%d" % c], 128)
         vop("p0_%d" % c, lambda a=a, b=b: V.tensor_scalar(T.lp[:, a:b], T.plt[:, a:b], -2048.0, None, A.add), ["plt"],
             ["lp0%d" % c], 128)
+        vop("sga%d" % c, lambda c=c: V.memset(T["sg%d" % c][:], 1.0), [], ["sg%d" % c], 128)
+        vop("sgb%d" % c, lambda c=c: V.memset(T["sg%d" % c][:, 31::32], -1.0), [], ["sg%d" % c], 8)
+    vop("kal", lambda: V.tensor_copy(T.keyt[:, k0 + 4096:k0 + 4097], T.keyt[:, k0:k0 + 1]), ["keyt"], ["kal"], 1)
+    vop("cal", lambda: V.tensor_copy(T.clt[:, 2048:2049], T.clt[:, 0:1]), ["clt0"], ["clt"], 1)
+    vop("eal", lambda: V.tensor_copy(T.emt[:, 4096:4097], T.emt[:, 0:1]), ["emt"], ["eal"], 1)
 
-    def sel(name, src, pattern, cmp, base, cm, rows=128):
-        gop(name, lambda: g.affine_select(T[name][:], T[src][0:rows, :], pattern, cmp, 0.0, base, cm), [src], [name], 128)
+    def sel(name, src, n, pattern, cmp, base, cm):
+        gop(name, lambda: g.affine_select(T[name][:], T[src][:, 0:n], pattern, cmp, 0.0, base, cm), [src], [name], n)
+    sel("idm", "ones", 128, [[-1, 128]], A.is_equal, 0, 1)
+    sel("bma", "ones", 128, [[-16, 8], [0, 16]], A.is_ge, 0, 1)
+    sel("bm", "bma", 128, [[16, 8], [0, 16]], A.is_ge, 15, -1)
+    sel("ga", "ones", 64, [[0, 8], [-16, 8]], A.is_ge, 0, 1)
+    sel("gb", "ga", 64, [[0, 8], [16, 8]], A.is_ge, 15, -1)
+    sel("fa", "c2k", 1024, [[-16, 8], [0, 8], [-1, 16]], A.is_equal, 0, 1)
+    gop("kci", lambda: g.iota(T.kci[:], [[0, 1]], 0, 1), [], ["kci"], 1)
+    g8 = T.gb[:, 0:8]
 
-    def iota(name, pattern, base, cm, n=128, flag=True):
-        kw = dict(allow_small_or_imprecise_dtypes=True) if flag else {}
-        gop(name, lambda: g.iota(T[name][:], pattern, base, cm, **kw), [], [name], n)
-    sel("idm", "ones", [[-1, 128]], A.is_equal, 0, 1)
-    sel("bma", "ones", [[-16, 8], [0, 16]], A.is_ge, 0, 1)
-    sel("bm", "bma", [[16, 8], [0, 16]], A.is_ge, 15, -1)
-    sel("ltm", "bm", [[1, 128]], A.is_gt, 0, -1)
-    iota("kci", [[0, 1]], 0, 1, 1, False)
-    iota("mki", [[0, 8], [-1, 16]], 16, 1, 128, False)
-    sel("e8", "ones", [[-1, 8], [0, 16]], A.is_equal, 0, 1, 8)
-    iota("bk", [[0, 8], [-1, 16]], 15, 0)
-    iota("bgi", [[1, 8], [0, 16]], 0, 0)
-
-    def scaled(name, src, k):
-        vop(name, lambda: V.tensor_scalar(T[name][:], T[src][:], float(k), None, A.mult), [src], [name], 64)
-    scaled("nid", "idm", -1.0)
-    for j in range(8):
-        vop("sl%d" % j, lambda j=j: V.tensor_copy(T.sl[:, 16 * j:16 * j + 129 * 15 + 1:129], T.bm[:, 16 * j:16 * j + 16]),
-            ["bm", "sl"], ["sl_%d" % j], 16)
-    SLK = ["sl"] + ["sl_%d" % x for x in range(8)]
-    scaled("hid", "idm", 0.5)
-    scaled("mid", "idm", -2048.0)
-    scaled("sid", "idm", 16.0)
-    scaled("kid", "idm", KB)
-    scaled("lw", "ltm", KB)
-    vop("lw1", lambda: V.tensor_tensor(T.lw[:], T.lw[:], T.kid[:], A.subtract), ["lw", "kid"], ["lw"], 256)
-    vop("wf", lambda: V.tensor_copy(T.wf[:], T.wt[:]), ["wt"], ["wf"], 1)
-    vop("gw", lambda: V.tensor_scalar(T.gw[:], T.bm[:, 0::16], T.wf[:], None, A.mult), ["bm", "wf"], ["gw"], 8)
-    vop("gk", lambda: V.tensor_scalar(T.gk[:], T.bm[:, 0::16], KB, None, A.mult), ["bm"], ["gk"], 8)
+    def scaled(name, src, k, n):
+        vs(name, T[name][:], T[src][:, 0:n], float(k), 0.0, [src], [name], n // 2)
+    scaled("nid", "idm", -1.0, 128)
+    scaled("hid", "idm", 0.5, 128)
+    scaled("sid", "idm", 1.0 / 4096.0, 128)
+    scaled("kid", "idm", -4096.0, 128)
+    scaled("mid", "idm", -2048.0, 128)
+    scaled("g2", "gb", 2.0, 8)
+    scaled("gn", "gb", -1.0, 8)
+    scaled("nq", "bm", -1.0, 128)
+    for b in range(NABS):
+        vop("nq%d" % b, lambda b=b: V.memset(T.nq[:, b::4], 0.0), [], ["nq"], 16)
+    vs("r0", T.r0[:], T.gb[:], -256.015625, 256.0, ["gb"], ["r0"], 32)
+    vs("r1", T.r1[:], T.gb[:], -255.984375 if first else -256.015625, 256.0, ["gb"], ["r1"], 32)
+    vop("thh", lambda: V.tensor_scalar(T.thh[:], T.thr[:], -1.0, 2048.0, A.mult, A.add), ["thr"], ["thh"], 128)
+    mm("gwp", "gwp", [(T.tk[:, 0:8], T.wr[:], T.c2k[0:1, 0:8], 64)], ["wr", "c2k"], ["gwp"], ["btk"])
+    vop("gw1", lambda: V.tensor_tensor(T.gw[:], T.tk[:, 0:8], g8, A.mult), ["gwp", "gb"], ["gw"], 8, ["btk"])
+    vop("gw", lambda: V.tensor_scalar(T.gw[:], T.gw[:], 1.0 / 4194304.0, None, A.mult), ["gw"], ["gw"], 8)
+    vop("cb", lambda: V.memset(T.cb[:], -1.0), [], ["cb"], 128)
+    vop("cb1", lambda: V.memset(T.cb[:, 31::32], -0.5), [], ["cb"], 8)
+    vop("cx", lambda: V.memset(T.cx[:, 0:128], -2048.0), [], ["cx"], 64)
+    vop("cx1", lambda: V.memset(T.cx[:, 128:256], -2047.0 if first else -2048.0), [], ["cx1"], 64)
     vop("kcj", lambda: V.tensor_scalar(T.kcj[:], T.kci[:], 15, None, A.bitwise_and), ["kci"], ["kcj"], 1)
     vop("kcf", lambda: V.tensor_copy(T.kcf[:], T.kcj[:]), ["kcj"], ["kcf"], 1)
-    vop("cc", lambda: V.tensor_scalar(T.cc[:], T.kcf[:], -KB, 1023.75, A.mult, A.add), ["kcf"], ["cc"], 1)
-    vop("kv", lambda: V.tensor_scalar(T.kv[:], T.bm[:, 0::16], T.kcf[:], None, A.mult), ["bm", "kcf"], ["kv"], 8)
-    vop("mkj", lambda: V.tensor_scalar(T.mkj[:], T.mki[:], 15, None, A.bitwise_and), ["mki"], ["mkj"], 128)
-    vop("mk", lambda: V.tensor_scalar(T.mk[:], T.mkj[:], 0.0, None, A.is_equal), ["mkj"], ["mk"], 128)
-    scaled("bg", "bgi", 65536.0)
+    vop("kv0", lambda: V.memset(T.kv[:, 8:32], 0.0), [], ["kv0"], 16)
+    vop("kv", lambda: V.tensor_scalar(T.kv[:, 0:8], g8, T.kcf[:], None, A.mult), ["gb", "kcf"], ["kv"], 8)
     vop("embs", lambda: V.tensor_scalar(T.embs[:], T.embt[:], 0.5, -0.25, A.mult, A.add), ["embt"], ["embs"], 16)
     for j in range(8):
-        vop("ebk%d" % j, lambda j=j: V.tensor_tensor(T.ebk[:, 16 * j:16 * j + 16], T.embs[:], T.bm[:, 16 * j:16 * j + 16],
-                                                     A.mult), ["bm", "embs"], ["ebk_%d" % j], 32)
+        vop("ebk%d" % j, lambda j=j: V.tensor_scalar(T.ebk[:, 16 * j:16 * j + 16], T.embs[:], T.gb[:, j:j + 1], None, A.mult),
+            ["gb", "embs"], ["ebk_%d" % j], 16)
     EBK = ["ebk_%d" % x for x in range(8)]
-    vop("z0", lambda: V.memset(T.z0[:], 0.0), [], ["z0"], 128)
-    vop("z1", lambda: V.memset(T.z1[:], 0.0), [], ["z1"], 128)
-    vop("z1b", lambda: V.memset(T.z1[:, 0::16], 4194304.0), ["z1"], ["z1"], 8)
-    for c in range(CH):
-        vop("fmt%d" % c, lambda c=c: V.memset(T["fm%d" % c][:, 128:144], 8388608.0), [], ["fmt%d" % c], 16)
+    vop("z8", lambda: V.memset(T.z8[:], 0.0), [], ["z8"], 64)
+    vop("z8b", lambda: V.memset(T.z8[:, 0::8], 16384.0), [], ["z8"], 8)
+    vop("zf", lambda: V.memset(T.zf[:], 0.0625), [], ["zf"], 128)
+    vop("zf1", lambda: V.memset(T.zf[:, 0::16], -16384.0), [], ["zf"], 8)
+    vop("zb", lambda: V.memset(T.zb[:], -0.0625), [], ["zb"], 128)
+    vop("zb1", lambda: V.memset(T.zb[:, 0::16], -16384.0), [], ["zb"], 8)
 
     nxt = T.cores[(rank + 1) % len(T.cores)]
     rid, pid = topo.addr(nxt)[0], topo.addr(nxt)[1]
     eng = topo.engines(core, nxt)
     m_all, m_a, m_b = sum(1 << e for e in eng), sum(1 << e for e in eng[0::2]), sum(1 << e for e in eng[1::2])
-    last_rank = rank == len(T.cores) - 1
-    win_k, win_e, win_c = T.keyt[:, 0:4098], T.emt[:, 0:4098], T.clt[:, 0:2050]
-    LP = NL // NP
-    X = [T.x0, T.x1, T.x2, T.x3]
+    win_c = T.clt[:, 0:2049]
+    X = [T.x0, T.x1]
 
     def gather(name, dst, win, lst, rd, wr, n):
         def emit(q):
             if q == "V":
                 return [V.tensor_copy(dst, win.indirect(lst))]
             return [S.activation(dst, win.indirect(lst), F.Copy)]
-        op(name, "VS", emit, rd, wr, (), 60 + n * GAT)
+        op(name, "VS", emit, rd, wr, (), ("i", n))
 
     def step(t, c):
         n, nn = "%d%d" % (t, c), "%d%d" % (t + 1, c)
         o = t * 256 + c * NL
         here, dst = slice(o, o + NL), slice(o + 256, o + 256 + NL)
         p, q = T.lp[:, here], T.lq[:, here]
-        Ab, Bb = T["A%d" % c], T["B%d" % c]
-        bA, bB = "bA%d" % c, "bB%d" % c
-        A1, A2, B0, B1 = "A1%d" % c, "A2%d" % c, "B0%d" % c, "B1%d" % c
-        kg, ab, hi, hf, far, se, prd, vm, ls, g1, eg, fm, bs, oh, on, dfl = (T[x + str(c)] for x in (
-            "kg ab hi hf far sel prd vm ls g1 eg fm bs oh on def".split()))
+        Db, Bb = T["D%d" % c], T["B%d" % c]
+        bD, bB = "bD%d" % c, "bB%d" % c
+        kg, ab, qx, ls, sg, sc, s2, yy, oh, on, fl, g1, eg, fm, bs = (T[x + str(c)] for x in (
+            "kg ab qx ls sg sc s2 yy oh on fl g1 eg fm bs".split()))
+        last = t == STEPS - 1
 
         def k(x):
             return "%s%d" % (x, c)
+        if t == 0:
+            win_k, kw = (T.keyt[:, 0:4111] if first else T.keyt[:, 16:4112]), ["keyt"]
+            win_e, ew = T.emt[:, 0:4096], ["emt"]
+        else:
+            win_k, kw = T.keyt[:, 16:k0 + 4097], ["kal"]
+            win_e, ew = T.emt[:, 0:4097], ["eal"]
         ko = (t % 2) * 2048
-        kr = ["kg%d%d_%d" % (c, t % 2, j) for j in range(NP)]
-        for j in range(NP):
-            gather("kg%s_%d" % (n, j), kg[:, ko + 16 * LP * j:ko + 16 * LP * (j + 1)], win_k,
-                   T.lu[:, o + LP * j:o + LP * (j + 1)], ["keyt", "lu" + n], [kr[j]], 16 * LP)
-        mm("h" + n, [(Bb[:, 128:136], q, T.gw[:], True, True, 8)], ["lq" + n, "gw"], [B1], [bB])
-        vop("hi" + n, lambda: V.tensor_scalar(hi[:], Bb[:, 128:136], -1023.5, HUGE, A.add, A.add), [B1], [k("hi")], 8, [bB])
-        vop("hf" + n, lambda: V.tensor_scalar(hf[:], hi[:], -HUGE, 1.0 / 2048.0, A.add, A.mult), [k("hi")], [k("hf")], 8)
-        for b in range(4):
-            mm("xk%s_%d" % (n, b), [(X[b][:, 128 * j:128 * j + 128], T.idm[:], kg[:, ko + 4 * b + j:ko + 2048:16], j == 0,
-                                     False, 128) for j in range(4)], kr + ["idm"], ["x%d" % b], ["bx%d" % b])
-        for b in range(4):
-            mm("xq%s_%d" % (n, b), [(X[b][:, 128 * j:128 * j + 128], T.nid[:], q, False, j == 3, 128) for j in range(4)],
-               ["lq" + n, "nid"], ["x%d" % b], ["bx%d" % b])
-            sop("ab%s_%d" % (n, b), lambda b=b: S.activation(ab[:, 512 * b:512 * b + 512], X[b][:], F.Abs), ["x%d" % b],
-                ["ab%d_%d" % (c, b)], 512, ["bx%d" % b])
-            mm("d%s_%d" % (n, b), [(Ab[:, 0:128], T.sl[:, 128 * s:128 * s + 128], ab[:, 128 * s:128 * s + 128], s == 0,
-                                    s == 15, 128) for s in range(4 * b, 4 * b + 4)], ["ab%d_%d" % (c, b)] + SLK, [k("d")], [bA])
-        vop("far" + n, lambda: V.tensor_scalar(far[:], Ab[:, 0:128], T.tht[:], None, A.is_ge), [k("d"), "tht"], [k("far")],
-            128, [bA])
-        mm("y" + n, [(Bb[:, 0:128], T.hid[:], p, True, False, 128), (Bb[:, 0:128], T.lw[:], far[:], False, True, 128)],
-           [k("far"), "lp" + n, "hid", "lw"], [B0], [bB])
-        y2 = Ab[0:8, 384:512]
-        mm("y2" + n, [(y2, T.gw[:], q, True, False, 128), (y2, hf[:], T.mid[:], False, False, 128),
-                      (y2, T.gk[:], far[:], False, True, 128)],
-           [k("far"), k("hf"), "lq" + n, "gw", "mid", "gk"], [k("y2")], [bA])
-        mm("f2" + n, [(Ab[:, 128:256], T.idm[:], far[:], True, True, 128)], [k("far"), "idm"], [A1], [bA])
-        vop("sel" + n, lambda: V.tensor_scalar(se[:], Bb[:, 0:128], T.cc[:], 0.0, A.add, A.max), [B0, "cc"], [k("sel")],
-            128, [bB])
-        vop("def" + n, lambda: V.tensor_scalar(dfl[:], y2, -16 * KB, 0.0, A.add, A.max), [k("y2")], [k("def")], 128, [bA])
-        mm("ex" + n, [(Bb[:, 128:256], se[:], T.bm[:], True, False, 128), (Bb[:, 128:256], dfl[:], T.e8[:], False, True, 128)],
-           [k("sel"), k("def"), "bm", "e8"], [B1], [bB])
-        vop("prd" + n, lambda: V.tensor_tensor(prd[:], Ab[:, 128:256], p, A.mult), [A1, "lp" + n], [k("prd")], 128, [bA])
-        vop("vm" + n, lambda: V.tensor_tensor(vm[:], Bb[:, 128:256], T.mk[:], A.mult), [B1, "mk"], [k("vm")], 128, [bB])
-        mm("l" + n, [(Bb[:, 0:8], vm[:], T.bm[:, 0::16], True, True, 8)], [k("vm"), "bm"], [B0], [bB])
-        z = Ab[:, 256:384]
-        mm("z" + n, [(z, T.idm[:], p, True, False, 128), (z, T.mid[:], far[:], False, False, 128),
-                     (z, T.nid[:], prd[:], False, True, 128)],
-           ["lp" + n, k("far"), k("prd"), "idm", "mid", "nid"], [A2], [bA])
-        vop("ls" + n, lambda: V.tensor_scalar(ls[:], Bb[:, 0:8], MAGIC, -MAGIC, A.add, A.add), [B0], [k("ls")], 8, [bB])
-        vop("g1" + n, lambda: V.tensor_tensor(g1[:], win_c.indirect(ls[:]), far[:], A.mult), ["clt", k("ls"), k("far")],
-            [k("g1")], 200)
-        sp, su, sp1, su1 = T.sp[:, here], T.su[:, here], T.sp1[:, here], T.su1[:, here]
-        vop("pn" + n, lambda: V.tensor_tensor(sp, g1[:], z, A.add), [k("g1"), A2], ["sp" + n], 128, [bA])
+        kr, a = [], 0
+        for j, w in enumerate(KP):
+            kr.append("kg%d%d_%d" % (c, t % 2, j))
+            gather("kg%s_%d" % (n, j), kg[:, ko + 16 * a:ko + 16 * (a + w)], win_k, T.lu[:, o + a:o + a + w],
+                   kw + ["lu" + n], [kr[j]], 16 * w)
+            a += w
+        hcol = Bb[:, 31:256:32]
+        hq = Bb[:, 448:456]
+        mm("h" + n, "H" + n, [(hq, T.ones[0:1, :], T.cb[:, 31::32], 64), (hq, q, T.gw[:], 64)], ["lq" + n, "gw", "ones", "cb"],
+           [k("F")], [bB])
+        vop("qx" + n, lambda: V.tensor_scalar(qx[:], hq, MAGIC, -MAGIC, A.add, A.add), [k("F")], [k("qx")], 8, [bB])
+        mm("bc" + n, "B" + n, [(Bb[:, 0:256], T.ones[0:1, :], T.cb[:], 256), (Bb[:, 0:256:2], p, T.sid[:], 128)],
+           ["lp" + n, "ones", "cb", "sid"], [k("B")], [bB])
+        mm("bq" + n, "B" + n, [(hcol, q, T.gw[:], 64), (hcol, T.nid[:], qx[:], 64)], ["lq" + n, "gw", k("qx"), "nid"], [k("B")],
+           [bB])
+        d = Db[:, 0:128]
+        mm("dt" + n, "D" + n, [(d, T.ones[0:1, :], T.thh[:], 128)], ["ones", "thh"], [k("d")], [bD])
+        parts = []
+
+        def dpart(name, mms, rd):
+            parts.append(k("d") + name)
+            mm(name + n, "D" + n, mms, rd + [k("d")], [parts[-1]], [bD])
+        for b in range(NABS):
+            mm("xk%s_%d" % (n, b), "x%s%d" % (n, b), [(X[b % 2][:, 128 * j:128 * j + 128], T.idm[:],
+               kg[:, ko + 4 * j + b:ko + 2048:16], 128) for j in range(4)], kr + ["idm"], ["x%d" % (b % 2)], ["bx%d" % (b % 2)])
+            mm("xq%s_%d" % (n, b), "x%s%d" % (n, b), [(X[b % 2][:, 128 * j:128 * j + 128], T.nid[:], q, 128) for j in range(4)],
+               ["lq" + n, "nid"], ["x%d" % (b % 2)], ["bx%d" % (b % 2)])
+            sop("ab%s_%d" % (n, b), lambda b=b: S.activation(ab[:, 512 * b:512 * b + 512], X[b % 2][:], F.Abs), ["x%d" % (b % 2)],
+                ["ab%d_%d" % (c, b)], 512, ["bx%d" % (b % 2)])
+            dpart("da%d_" % b, [(Db[:, 4 * j + b:128:16], ab[:, 512 * b + 128 * j:512 * b + 128 * j + 128], g8, 64)
+                                for j in range(4)], ["ab%d_%d" % (c, b), "gb"])
+        if NABS < 4:
+            mm("xr" + n, "xr" + n, [(T.xr[:, j::4], T.idm[:], q, 128) for j in range(4)], ["lq" + n, "idm"], ["xr"], ["bxr"])
+            dpart("dq", [(d, q, T.nq[:], 128)], ["lq" + n, "nq"])
+        for b in range(NABS, 4):
+            dpart("dk%d_" % b, [(Db[:, 4 * j + b:128:16], kg[:, ko + 4 * j + b:ko + 2048:16], T.gn[:], 64) for j in range(4)],
+                  kr + ["gn"])
+            vop("mx%s_%d" % (n, b), lambda b=b: V.tensor_tensor(ab[:, 512 * b:512 * b + 512], kg[:, ko + b:ko + 2048:4], T.xr[:],
+                                                                A.max), kr + ["xr"], ["ab%d_%d" % (c, b)], 512, ["bxr"])
+            dpart("dm%d_" % b, [(Db[:, 4 * j + b:128:16], ab[:, 512 * b + j:512 * b + 512:4], T.g2[:], 64) for j in range(4)],
+                  ["ab%d_%d" % (c, b), "g2"])
+        sge = sg[:, 0:256:2]
+        sop("sg" + n, lambda: S.activation(sge, d, F.Sign, -2047.5), parts, [k("sg"), k("d")], 128, [bD])
+        mm("bs" + n, "B" + n, [(Bb[:, 0:256:2], T.nid[:], sge, 128)], [k("sg"), "nid"], [k("B")], [bB])
+        vop("sc" + n, lambda: V.tensor_tensor_scan(sc[:, ::-1], sg[:, ::-1], Bb[:, 255::-1], 0.0, A.min, A.max),
+            [k("B"), k("sg")], [k("sc")], 256, [bB])
+        mm("nn" + n, "N" + n, [(Db[:, 128:256], sge, T.idm[:], 128)], [k("sg"), "idm"], [k("N")], [bD])
+        x = Db[:, 256:384]
+        cx = T.cx[:, 0:128] if t == 0 else T.cx[:, 128:256]
+        mm("xx" + n, "X" + n, [(x, T.idm[:], p, 128), (x, T.ones[0:1, :], cx, 128), (x, sge, T.mid[:], 128)],
+           [k("sg"), k("N"), "lp" + n, "idm", "ones", "cx", "cx1", "mid"], [k("X")], [bD])
+        vs("yy" + n, yy[:], Db[:, 128:256], 3072.0, -5120.0, [k("N")], [k("yy")], 128, [bD])
+        f = Bb[:, 384:448]
+        mm("fo" + n, "F" + n, [(f, T.bm[:], T.r0[:] if t == 0 else T.r1[:], 64)]
+           + [(Bb[:, 384 + 8 * j:392 + 8 * j], T.fa[:, 128 * j:128 * j + 128], sc[:, 0::32], 64) for j in range(8)],
+           [k("sc"), "bm", "r0", "r1", "fa"], [k("F")], [bB])
+        vop("s2" + n, lambda: V.tensor_tensor_scan(s2[:], T.z8[:], f, 0.0, A.add, A.min), [k("F"), "z8"], [k("s2")], 64, [bB])
+        vop("ls" + n, lambda: V.tensor_scalar(ls[:], s2[:, 7::8], MAGIC + 1024.0, -MAGIC, A.add, A.add), [k("s2")], [k("ls")], 8)
+        op("g1" + n, "V", lambda _q: [V.tensor_tensor(g1[:], win_c.indirect(ls[:]), yy[:], A.add)], ["clt", k("ls"), k("yy")],
+           [k("g1")], (), ("i", 128))
+        sp, su = T.sp[:, here], T.su[:, here]
+        vop("pn" + n, lambda: V.tensor_tensor(sp, g1[:], x, A.max), [k("g1"), k("X")], ["sp" + n], 128, [bD])
         vop("un" + n, lambda: V.tensor_scalar(su, sp, 2048.0, None, A.add), ["sp" + n], ["su" + n], 64)
-        last = t == STEPS - 1
-        op("up" + n, "V", lambda _q: [V.tensor_scalar(su1, sp, 2049.0, None, A.add)], ["sp" + n], ["su1" + n], (), 115,
-           skip=not last_rank)
-        if not last:
-            op("pp" + n, "V", lambda _q: [V.tensor_scalar(sp1, sp, 1.0, None, A.add)], ["sp" + n], ["sp1" + n], (), 115,
-               skip=not last_rank)
-        hu, hp = (su1, sp1) if last_rank else (su, sp)
+        r = slice(c * NL, c * NL + NL)
+        if last:
+            dl = 1.0 if last_rank else 0.0
+            vop(k("fl"), lambda: V.tensor_scalar(fl[:], sp, 2048.0 - dl, None, A.is_ge), ["sp" + n], [k("fl")], 64)
+            mm(k("zz"), k("Z"), [(Db[:, 384:512], T.idm[:], sp, 128), (Db[:, 384:512], T.kid[:], fl[:], 128)],
+               ["sp" + n, k("fl"), "idm", "kid"], [k("Z")], [bD])
+            vs(k("sf"), T.sf[:, r], Db[:, 384:512], 1.0, 2048.0 + dl, [k("Z")], [k("sf")], 128, [bD])
 
         def send_p(_q):
             if last:
-                g.remote_dma(T.lu[:, dst], hu, T.sem["ap" + n], T.sem.lsem, pid, rid, m_all)
+                g.remote_dma(T.lf[:, r], T.sf[:, r], T.sem["ap" + n], T.sem.lsem, pid, rid, m_all)
                 return None
             g.remote_dma_fused([RemoteDMATransfer(dst_ids=[DstId(rid=rid, pnc=pid)], dma_engine_mask=m,
                                                   remote_sem=T.sem["ap" + n], src=s, dst=d)
-                                for m, s, d in ((m_a, hu, T.lu[:, dst]), (m_b, hp, T.lp[:, dst]))], local_sem=T.sem.lsem)
+                                for m, s, d in ((m_a, su, T.lu[:, dst]), (m_b, sp, T.lp[:, dst]))], local_sem=T.sem.lsem)
             return None
-        op("sendp" + n, "G", send_p, ["su" + n, "su1" + n] + ([] if last else ["sp" + n, "sp1" + n]),
-           ["lu" + nn] + ([] if last else ["lp" + nn]), (), 150, "ap" + n, NET)
+        op("sendp" + n, "G", send_p, [k("sf")] if last else ["su" + n, "sp" + n],
+           [k("lf")] if last else ["lu" + nn, "lp" + nn], (), ("r", 1), "ap" + n)
         if last:
-            r = slice(c * NL, c * NL + NL)
-            vop("fi%d" % c, lambda: V.tensor_copy(T.fi[:, r], T.lu[:, dst]), ["lu" + nn], [k("fi")], 128)
-            vop("fj%d" % c, lambda: V.tensor_scalar(T.fj[:, r], T.fi[:, r], 4095, None, A.bitwise_and), [k("fi")], [k("fj")], 128)
-            vop("ff%d" % c, lambda: V.tensor_copy(T.ff[:, r], T.fj[:, r]), [k("fj")], [k("ff")], 128)
-            ld("stp%d" % c, "Y", [(T.yp[:, r], T.ff[:, r])], ["yp%d" % c], "st", 2000, [k("ff")])
-        for j in range(NP):
-            gather("eg%s_%d" % (n, j), eg[:, 16 * LP * j:16 * LP * (j + 1)], win_e, T.su[:, o + LP * j:o + LP * (j + 1)],
-                   ["emt", "su" + n], ["eg%d_%d" % (c, j)], 16 * LP)
-        v = Ab[:, 128:256]
-        mm("v" + n, [(v, T.ones[0:1, :], T.bk[0:1, :], True, False, 128), (v, T.ones[0:1, :], T.bg[0:1, :], False, False, 128)]
-           + [(v, eg[:, s::16], T.sid[:], False, s == 15, 128) for s in range(16)],
-           ["eg%d_%d" % (c, j) for j in range(NP)] + ["ones", "bk", "bg", "sid"], [A1], [bA])
-        vop("fm" + n, lambda: V.tensor_tensor_scan(fm[:, 0:128], T.z0[:], v, 0.0, A.add, A.max), [A1, "z0"], [k("fm")], 128, [bA])
-        vop("bs" + n, lambda: V.tensor_tensor_scan(bs[:], T.z1[:], fm[:, 15:143], 0.0, A.add, A.min),
-            [k("fm"), k("fmt"), "z1"], [k("bs")], 128)
-        vop("oh" + n, lambda: V.tensor_tensor(oh[:], v, bs[:], A.is_equal), [A1, k("bs")], [k("oh")], 128, [bA])
-        mm("on" + n, [(Bb[:, 256:384], oh[:], T.idm[:], True, True, 128)], [k("oh"), "idm"], [k("onp")], [bB])
-        sop("ons" + n, lambda: S.activation(on[:], Bb[:, 256:384], F.Copy), [k("onp")], [k("on")], 128, [bB])
+            dma("stp%d" % c, "Y", [(T.yp[:, r], T.lf[:, r])], [k("lf")], ["yp%d" % c], "st", 65536)
+        er, a = [], 0
+        for j, w in enumerate(EP):
+            er.append("eg%d_%d" % (c, j))
+            gather("eg%s_%d" % (n, j), eg[:, 16 * a:16 * (a + w)], win_e, T.su[:, o + a:o + a + w], ew + ["su" + n], [er[j]], 16 * w)
+            a += w
+        u = Bb[:, 256:384]
+        mm("v" + n, "U" + n, [(u, eg[:, s::16], T.idm[:], 128) for s in range(16)], er + ["idm"], [k("U")], [bB])
+        vop("fm" + n, lambda: V.tensor_tensor_scan(fm[:], T.zf[:], u, 0.0, A.add, A.max), [k("U"), "zf"], [k("fm")], 128, [bB])
+        vop("bw" + n, lambda: V.tensor_tensor_scan(bs[:, ::-1], T.zb[:], fm[:, ::-1], 0.0, A.add, A.max),
+            [k("fm"), "zb"], [k("bs")], 128)
+        vop("oh" + n, lambda: V.tensor_tensor(oh[:], u, bs[:], A.is_equal), [k("U"), k("bs")], [k("oh")], 128, [bB])
+        mm("op" + n, "O" + n, [(u, oh[:], T.idm[:], 128)], [k("oh"), "idm"], [k("U")], [bB])
+        vs("on" + n, on[:], u, 1.0, 0.0, [k("U")], [k("on")], 128, [bB])
         e = Bb[:, 384:512]
-        mm("e" + n, [(e, T.hid[:], q, True, False, 128), (e, T.ebk[:], on[:], False, True, 128)],
-           ["lq" + n, k("on"), "hid"] + EBK, [k("e")], [bB])
+        mm("e" + n, "E" + n, [(e, T.hid[:], q, 128), (e, T.ebk[:], on[:], 128)], ["lq" + n, k("on"), "hid"] + EBK, [k("F")], [bB])
         sq = T.sq[:, here]
-        vop("qn" + n, lambda: V.tensor_scalar(sq, e, MAGIC, -MAGIC, A.add, A.add), [k("e")], ["sq" + n], 128, [bB])
+        vop("qn" + n, lambda: V.tensor_scalar(sq, e, MAGIC, -MAGIC, A.add, A.add), [k("F")], ["sq" + n], 128, [bB])
 
         def send_q(_q):
             g.remote_dma(T.lq[:, dst], sq, T.sem["aq" + n], T.sem.lsem, pid, rid, m_all)
             return None
-        op("sendq" + n, "G", send_q, ["sq" + n], ["lq" + nn], (), 150, "aq" + n, NET)
-        mm("tk" + n, [(Ab[0:8, 256:384], T.kv[:], on[:], True, True, 128)], [k("on"), "kv"], [A2], [bA])
-        sop("yt" + n, lambda: S.activation(T.ytb[:, here], Ab[0:8, 256:384], F.Copy), [A2], ["yt" + n], 128, [bA])
+        op("sendq" + n, "G", send_q, ["sq" + n], ["lq" + nn], (), ("r", 0), "aq" + n)
+        y0, yc = 32 * (t % 4), 256 * (t // 4) + c * NL
+        mm("tk" + n, "T" + n, [(T.tk[y0:y0 + 32, yc:yc + NL], T.kv[:], on[:], 128)], [k("on"), "kv", "kv0"], ["tk" + n], ["btk"])
+        if t == 3 and c == CH - 1:
+            vs("yta", T.ytb[:, 0:256], T.tk[:, 0:256], 1.0, 0.0, ["tk%d%d" % (x, y) for x in range(4) for y in range(CH)],
+               ["yta"], 256, ["btk"])
+            dma("sta", "Y", [(T.yt[:, 256 * x:256 * x + 256], T.ytb[32 * x:32 * x + 8, 0:256]) for x in range(4)], ["yta"],
+                ["ytad"], "st", 32768)
         if last:
-            ld("stq%d" % c, "Y", [(T.yq[:, c * NL:c * NL + NL], T.lq[:, dst])], ["yq%d" % c], "st", 2000, ["lq" + nn])
+            dma("stq%d" % c, "Y", [(T.yq[:, r], T.lq[:, dst])], ["lq" + nn], ["yq%d" % c], "st", 32768)
             if c == CH - 1:
-                ld("stt", "Y", [(T.yt[:], T.ytb[:])], ["ytd"], "st", 2000,
-                   ["yt%d%d" % (x, y) for x in range(STEPS) for y in range(CH)])
+                vs("ytb", T.ytb[0:8, 256:512], T.tk[0:8, 256:512], 1.0, 0.0, ["tk40", "tk41"], ["ytb"], 256, ["btk"])
+                dma("stb", "Y", [(T.yt[:, 1024:1280], T.ytb[0:8, 256:512])], ["ytb"], ["ytbd"], "st", 8192)
 
     for t in range(STEPS):
         for c in range(CH):
@@ -287,9 +337,11 @@ def make_ops(g, T, topo, core, rank):
 def depend(ops):
     wr, rds, bank = {}, {}, {}
     for o in ops:
-        d = set()
+        d, soft = set(), set()
         for k in o["rd"]:
-            if k in wr:
+            if k[0] == "+":
+                soft.add(wr[k[1:]])
+            elif k in wr:
                 d.add(wr[k])
         for k in o["wr"]:
             if k in wr:
@@ -297,7 +349,7 @@ def depend(ops):
             d.update(rds.get(k, ()))
         for b in o["banks"]:
             turn = bank.setdefault(b, ["", [], []])
-            if turn[0] != o["qs"]:
+            if turn[0] != o["qs"] or len(o["qs"]) > 1:
                 turn[0], turn[1], turn[2] = o["qs"], turn[2], []
             d.update(turn[1])
             turn[2].append(o["i"])
@@ -307,79 +359,117 @@ def depend(ops):
             wr[k] = o["i"]
             rds[k] = []
         d.discard(o["i"])
-        o["deps"] = sorted(d)
+        o["deps"], o["soft"] = sorted(d), sorted(soft - d)
 
 
-def schedule(ops):
+def costs(ops, model):
+    cyc, gat, pec, hop, net, bw = model
+    cv, cs, lat, t0 = [], [], [], 1500.0
+    for o in ops:
+        c, l = o["cost"], 0.0
+        if c[0] == "c":
+            a, b = 50 + max(64, c[1]) * cyc, 65 + max(64, c[2]) * cyc
+        elif c[0] == "i":
+            a, b = 50 + c[1] * cyc * gat, 65 + c[1] * cyc * gat
+        elif c[0] == "p":
+            a = b = c[1] * pec
+        elif c[0] == "g":
+            a = b = 170 + 2 * c[1] * cyc
+        elif c[0] == "r":
+            a = b = 150.0
+            l = net + 200.0 * c[1]
+        else:
+            a = b = 60.0 * c[2]
+            if o["sem"] == "st":
+                l = 1600.0 + c[1] / bw
+            else:
+                t0 += c[1] / bw
+                l = t0
+        cv.append(b if o["qs"] == "S" else a)
+        cs.append(b)
+        lat.append(l)
+    dl = [[(d, 0.0 if o["qs"] == "P" and ops[d]["qs"] == "P" else hop) for d in o["deps"]] for o in ops]
+    return cv, cs, lat, dl
+
+
+def timeline(seq, qs, tab):
+    cv, cs, lat, dl = tab
+    n = len(cv)
+    done, pred = [0.0] * n, [-1] * n
+    free = {"V": 0.0, "S": 0.0, "P": 0.0, "G": 0.0, "Y": 0.0}
+    lastq = {"V": -1, "S": -1, "P": -1, "G": -1, "Y": -1}
+    for i in seq:
+        q = qs[i]
+        st, pr = free[q], lastq[q]
+        for d, h in dl[i]:
+            r = done[d] + h
+            if r > st:
+                st, pr = r, d
+        free[q] = e = st + (cs[i] if q == "S" else cv[i])
+        done[i] = e + lat[i]
+        pred[i], lastq[q] = pr, i
+    return done, pred
+
+
+def schedule(ops, tab):
+    cv, cs, lat, dl = tab
     n = len(ops)
     succ = [[] for _ in ops]
     for o in ops:
-        for d in o["deps"]:
+        for d in o["deps"] + o["soft"]:
             succ[d].append(o["i"])
     bl = [0.0] * n
     for i in range(n - 1, -1, -1):
-        bl[i] = ops[i]["cost"] + ops[i]["lat"] + max([bl[s] + HOP for s in succ[i]] or [0.0])
-    left = [len(o["deps"]) for o in ops]
-    done, ready, free, order = [0.0] * n, {i: 0.0 for i in range(n) if left[i] == 0}, {}, []
+        bl[i] = cv[i] + lat[i] + max([bl[s] + 60.0 for s in succ[i]] or [0.0])
+    left = [len(o["deps"] + o["soft"]) for o in ops]
+    done, ready, free, order, qof = [0.0] * n, {i: 0.0 for i in range(n) if left[i] == 0}, {}, [], [""] * n
     while ready:
         st, _, i, q = min((max(r, free.get(q, 0.0)), -bl[i], i, q) for i, r in ready.items() for q in ops[i]["qs"])
         for j, r in ready.items():
             if q in ops[j]["qs"] and max(r, free.get(q, 0.0)) <= st + 200.0 and (-bl[j], j) < (-bl[i], i):
                 i = j
         st = max(ready.pop(i), free.get(q, 0.0))
-        ops[i]["q"] = q
-        free[q] = st + ops[i]["cost"]
-        done[i] = free[q] + ops[i]["lat"]
+        qof[i] = q
+        free[q] = st + (cs[i] if q == "S" else cv[i])
+        done[i] = free[q] + lat[i]
         order.append(i)
         for s in succ[i]:
             left[s] -= 1
             if left[s] == 0:
-                ready[s] = max(done[d] for d in ops[s]["deps"]) + HOP
-    return order
+                ready[s] = max([done[d] + h for d, h in dl[s]] or [0.0])
+    return order, qof
 
 
-def improve(ops, order, iters):
-    n = len(ops)
-    cost, lat = [o["cost"] for o in ops], [o["lat"] for o in ops]
-    deps = [o["deps"] for o in ops]
-    qof = [o["q"] for o in ops]
-
-    def run(seq, qs):
-        end, done, pred, free, lastq = [0.0] * n, [0.0] * n, [-1] * n, {}, {}
-        for i in seq:
-            q = qs[i]
-            st, pr = free.get(q, 0.0), lastq.get(q, -1)
-            for d in deps[i]:
-                r = done[d] + HOP
-                if r > st:
-                    st, pr = r, d
-            free[q] = end[i] = st + cost[i]
-            done[i] = end[i] + lat[i]
-            pred[i], lastq[q] = pr, i
-        return done, pred
-    done, pred = run(order, qof)
-    best = cur = max(done)
-    bo, bq = list(order), list(qof)
-    order, seed = list(order), 12345
+def improve(ops, order, qof, tabs, iters):
+    deps = [o["deps"] + o["soft"] for o in ops]
+    dset = [set(d) for d in deps]
+    flex = [len(o["qs"]) > 1 for o in ops]
+    res = [timeline(order, qof, tb) for tb in tabs]
+    norm = [max(r[0]) for r in res]
+    best = cur = 1.0 * len(tabs)
+    bo, bq, seed = list(order), list(qof), 12345
     for it in range(iters):
         seed = (seed * 1103515245 + 12345) % 2147483648
-        path = []
+        done, pred = res[it % len(tabs)]
         i = done.index(max(done))
+        cand = []
         while i >= 0:
-            path.append(i)
-            i = pred[i]
-        cand = [i for i in path if pred[i] >= 0 and pred[i] not in deps[i]] + [i for i in path if len(ops[i]["qs"]) > 1]
-        if not cand:
-            break
+            j = pred[i]
+            if j >= 0 and j not in dset[i]:
+                cand.append(i)
+                if flex[j]:
+                    cand.append(-j - 1)
+            if flex[i]:
+                cand.append(-i - 1)
+            i = j
         i = cand[(seed >> 8) % len(cand)]
-        nq, no = qof, list(order)
-        if len(ops[i]["qs"]) > 1 and (seed >> 5) % 3 == 0:
+        nq, no = qof, order
+        if i < 0:
             nq = list(qof)
-            nq[i] = "S" if qof[i] == "V" else "V"
+            nq[-i - 1] = "S" if qof[-i - 1] == "V" else "V"
         else:
             j = pred[i]
-            if j < 0 or j in deps[i]:
-                continue
+            no = list(order)
             a, b = no.index(j), no.index(i)
             need, head, tail = {i}, [], []
             for x in reversed(no[a:b + 1]):
@@ -391,16 +481,14 @@ def improve(ops, order, iters):
             if j in need:
                 continue
             no[a:b + 1] = head[::-1] + tail[::-1]
-        d2, p2 = run(no, nq)
-        m = max(d2)
-        temp = TEMP * (1.0 - it / iters)
-        if m <= cur or (seed >> 3) % 1000 < 1000.0 * 2.718281828 ** (-(m - cur) / (temp + 0.01)):
-            order, qof, done, pred, cur = no, nq, d2, p2, m
+        r2 = [timeline(no, nq, tb) for tb in tabs]
+        m = sum(max(r[0]) / z for r, z in zip(r2, norm))
+        temp = TEMP / norm[0] * (1.0 - it / iters) + 1e-7
+        if m <= cur or (seed >> 3) % 1000 < 1000.0 * 2.718281828 ** (-(m - cur) / temp):
+            order, qof, res, cur = no, nq, r2, m
             if m < best:
                 best, bo, bq = m, list(no), list(nq)
-    for o in ops:
-        o["q"] = bq[o["i"]]
-    return bo, best
+    return bo, bq, [max(timeline(bo, bq, tb)[0]) for tb in tabs]
 
 
 PLAN = {}
@@ -413,8 +501,9 @@ def rank_program(g, core, T, topo):
     ops = make_ops(g, T, topo, core, rank)
     depend(ops)
     if "order" not in PLAN:
-        PLAN["order"], PLAN["best"] = improve(ops, schedule(ops), ITERS)
-        PLAN["q"] = [o["q"] for o in ops]
+        tabs = [costs(ops, m) for m in MODELS]
+        order, qof = schedule(ops, tabs[0])
+        PLAN["order"], PLAN["q"], PLAN["best"] = improve(ops, order, qof, tabs, ITERS)
     eng = {"V": g.vector, "S": g.scalar, "P": g.tensor, "G": g, "Y": g.sync}
     known = {q: {} for q in eng}
     count = {"V": 0, "S": 0, "P": 0, "G": 0}
@@ -425,9 +514,6 @@ def rank_program(g, core, T, topo):
         for d in o["deps"]:
             if not (PLAN["q"][d] == "P" and q == "P"):
                 toks += token[d]
-        if o["skip"]:
-            token[i] = toks
-            continue
         for s, v in sorted(toks, key=lambda x: (-x[1], x[0])):
             if kn.get(s, 0) < v:
                 eng[q].wait_ge(T.sem[s], v)
@@ -439,16 +525,17 @@ def rank_program(g, core, T, topo):
             lsem += 16
             token[i] = [(o["sem"], 16)]
             continue
-        for x in out:
-            x.then_inc(T.sem[o["sem"] or q], 16 if o["sem"] else 1)
-        if o["sem"] == "st":
-            stores += 16
-            token[i] = []
-            continue
         if o["sem"]:
+            for x in out:
+                x.then_inc(T.sem[o["sem"]], 16)
+            if o["sem"] == "st":
+                stores += 16 * len(out)
+                token[i] = []
+                continue
             token[i] = [(o["sem"], 16 * len(out))]
         else:
-            count[q] += len(out)
+            out[-1].then_inc(T.sem[q], 1)
+            count[q] += 1
             token[i] = [(q, count[q])]
         snap[token[i][0]] = dict(kn)
     for s in sorted(count):

@@ -7,7 +7,7 @@ EP = [32, 32, 32, 32]
 NABS = 2
 MAGIC = 12582912.0
 MODELS = [(0.87, 1.3, 0.44, 60.0, 1700.0, 330.0), (1.1, 1.7, 0.55, 60.0, 2100.0, 260.0)]
-ITERS, TEMP = 15000, 300.0
+ITERS, TEMP, SOFT, SEED = 15000, 300.0, 0.5, 12345
 
 SCRATCH = {"thr": ("sbuf", [1, 128], "float32"), "thh": ("sbuf", [1, 128], "float16"), "wr": ("sbuf", [1, 128], "bfloat16"),
            "cb": ("sbuf", [1, 256], "bfloat16"), "cx": ("sbuf", [1, 256], "float16")}
@@ -62,10 +62,13 @@ for _t in range(STEPS):
 def make_ops(g, T, topo, core, rank):
     A, F = AluOpType, ActivationFunctionType
     V, S, P = g.vector, g.scalar, g.tensor
-    ops, groups = [], {}
+    ops, groups, cur = [], {}, [""]
 
     def op(name, qs, fn, rd, wr, banks=(), cost=None, sem=None):
-        ops.append(dict(name=name, qs=qs, fn=fn, rd=list(rd), wr=list(wr), banks=list(banks), cost=cost, sem=sem, i=len(ops)))
+        ops.append(dict(name=name, qs=qs, fn=fn, rd=list(rd), wr=list(wr), banks=list(banks), cost=cost, sem=sem, i=len(ops),
+                        tc=(int(cur[0][0]), int(cur[0][1])) if cur[0] else None,
+                        kind=("@".join(name.rsplit(cur[0], 1)) if "_" not in name[-3:] or name[-3] == "_" else
+                              name[:2] + name[-2:], cur[0][1:]) if cur[0] else (name, "")))
 
     def vop(name, fn, rd, wr, n, banks=()):
         op(name, "V", lambda q: [fn()], rd, wr, banks, ("c", n, n))
@@ -108,8 +111,8 @@ def make_ops(g, T, topo, core, rank):
     dma("ld_th", "S", [(T.thr[:], T.th[:])], [], ["thr", "o2"], "ld_th", 8192)
     dma("ld_w", "S", [(T.wr[:], T.w[:])], ["+o2"], ["wr", "o3"], "ld_w", 8192)
     dma("ld_key", "Y", [(T.keyt[:, k0:k0 + 4096], T.key[:])], ["kz", "+o1", "+o3"], ["keyt", "o4"], "ld_key", 1048576)
-    dma("ld_q", "S", [(T.lq[:, 0:256], T.q[:])], ["+o4"], ["lq00", "lq01", "o5"], "ld_q", 65536)
-    dma("ld_emb", "S", [(T.embt[:], T.emb[:])], ["+o5"], ["embt", "o6"], "ld_emb", 65536)
+    dma("ld_q", "Y", [(T.lq[:, 0:256], T.q[:])], ["+o4"], ["lq00", "lq01", "o5"], "ld_q", 65536)
+    dma("ld_emb", "Y", [(T.embt[:], T.emb[:])], ["+o5"], ["embt", "o6"], "ld_emb", 65536)
     dma("ld_cl", "Y", [(T.clt[:, 0:2048], T.cl[:])], ["+o6"], ["clt0", "o7"], "ld_cl", 1048576)
     dma("ld_em", "Y", [(T.emt[:, 0:4096], T.em[:])], ["+o7"], ["emt"], "ld_em", 1048576)
 
@@ -165,10 +168,10 @@ def make_ops(g, T, topo, core, rank):
     vop("kv0", lambda: V.memset(T.kv[:, 8:32], 0.0), [], ["kv0"], 16)
     vop("kv", lambda: V.tensor_scalar(T.kv[:, 0:8], g8, T.kcf[:], None, A.mult), ["gb", "kcf"], ["kv"], 8)
     vop("embs", lambda: V.tensor_scalar(T.embs[:], T.embt[:], 0.5, -0.25, A.mult, A.add), ["embt"], ["embs"], 16)
-    for j in range(8):
-        vop("ebk%d" % j, lambda j=j: V.tensor_scalar(T.ebk[:, 16 * j:16 * j + 16], T.embs[:], T.gb[:, j:j + 1], None, A.mult),
-            ["gb", "embs"], ["ebk_%d" % j], 16)
-    EBK = ["ebk_%d" % x for x in range(8)]
+    mm("ebp", "ebp", [(T.tk[:, 256 + 16 * j:272 + 16 * j], T.idm[:], T.embs[:], 64) for j in range(8)], ["idm", "embs"], ["ebp"],
+       ["btk"])
+    vop("ebk", lambda: V.tensor_tensor(T.ebk[:], T.tk[:, 256:384], T.bm[:], A.mult), ["ebp", "bm"], ["ebk"], 128, ["btk"])
+    EBK = ["ebk"]
     vop("z8", lambda: V.memset(T.z8[:], 0.0), [], ["z8"], 64)
     vop("z8b", lambda: V.memset(T.z8[:, 0::8], 16384.0), [], ["z8"], 8)
     vop("zf", lambda: V.memset(T.zf[:], 0.0625), [], ["zf"], 128)
@@ -193,6 +196,7 @@ def make_ops(g, T, topo, core, rank):
     def step(t, c):
         n, nn = "%d%d" % (t, c), "%d%d" % (t + 1, c)
         o = t * 256 + c * NL
+        cur[0] = n
         here, dst = slice(o, o + NL), slice(o + 256, o + 256 + NL)
         p, q = T.lp[:, here], T.lq[:, here]
         Db, Bb = T["D%d" % c], T["B%d" % c]
@@ -299,7 +303,9 @@ def make_ops(g, T, topo, core, rank):
             gather("eg%s_%d" % (n, j), eg[:, 16 * a:16 * (a + w)], win_e, T.su[:, o + a:o + a + w], ew + ["su" + n], [er[j]], 16 * w)
             a += w
         u = Bb[:, 256:384]
-        mm("v" + n, "U" + n, [(u, eg[:, s::16], T.idm[:], 128) for s in range(16)], er + ["idm"], [k("U")], [bB])
+        for j in range(4):
+            mm("v%d" % j + n, "U" + n, [(u, eg[:, s::16], T.idm[:], 128) for s in range(4 * j, 4 * j + 4)], er + ["idm"],
+               [k("U")], [bB])
         vop("fm" + n, lambda: V.tensor_tensor_scan(fm[:], T.zf[:], u, 0.0, A.add, A.max), [k("U"), "zf"], [k("fm")], 128, [bB])
         vop("bw" + n, lambda: V.tensor_tensor_scan(bs[:, ::-1], T.zb[:], fm[:, ::-1], 0.0, A.add, A.max),
             [k("fm"), "zb"], [k("bs")], 128)
@@ -363,7 +369,7 @@ def depend(ops):
 
 
 def costs(ops, model):
-    cyc, gat, pec, hop, net, bw = model
+    cyc, gat, pec, hop, net, bw = model[:6]
     cv, cs, lat, t0 = [], [], [], 1500.0
     for o in ops:
         c, l = o["cost"], 0.0
@@ -377,7 +383,7 @@ def costs(ops, model):
             a = b = 170 + 2 * c[1] * cyc
         elif c[0] == "r":
             a = b = 150.0
-            l = net + 200.0 * c[1]
+            l = net + 200.0 * c[1] + (1200.0 if o["name"] == "sendp00" else 0.0)
         else:
             a = b = 60.0 * c[2]
             if o["sem"] == "st":
@@ -389,11 +395,11 @@ def costs(ops, model):
         cs.append(b)
         lat.append(l)
     dl = [[(d, 0.0 if o["qs"] == "P" and ops[d]["qs"] == "P" else hop) for d in o["deps"]] for o in ops]
-    return cv, cs, lat, dl
+    return cv, cs, lat, dl, {"V": model[6], "S": model[7]}
 
 
 def timeline(seq, qs, tab):
-    cv, cs, lat, dl = tab
+    cv, cs, lat, dl, ql = tab
     n = len(cv)
     done, pred = [0.0] * n, [-1] * n
     free = {"V": 0.0, "S": 0.0, "P": 0.0, "G": 0.0, "Y": 0.0}
@@ -406,7 +412,7 @@ def timeline(seq, qs, tab):
             if r > st:
                 st, pr = r, d
         free[q] = e = st + (cs[i] if q == "S" else cv[i])
-        done[i] = e + lat[i]
+        done[i] = e + lat[i] + ql.get(q, 0.0)
         pred[i], lastq[q] = pr, i
     return done, pred
 
@@ -491,7 +497,104 @@ def improve(ops, order, qof, tabs, iters):
     return bo, bq, [max(timeline(bo, bq, tb)[0]) for tb in tabs]
 
 
+def improve(ops, order, qof, tabs, iters):
+    n = len(ops)
+    deps = [o["deps"] + o["soft"] for o in ops]
+    dset = [set(d) for d in deps]
+    flex = [len(o["qs"]) > 1 for o in ops]
+    kin, kin2 = {}, {}
+    for o in ops:
+        kin.setdefault(o["kind"], []).append(o["i"])
+        kin2.setdefault(o["kind"][0], []).append(o["i"])
+    same = [kin[o["kind"]] for o in ops]
+    same2 = [kin2[o["kind"][0]] for o in ops]
+    marks = [o["i"] for o in ops if o["cost"][0] == "r"]
+    rnd = [SEED]
+
+    def rand(m):
+        rnd[0] = (rnd[0] * 1103515245 + 12345) % 2147483648
+        return (rnd[0] >> 8) % m
+
+    def score(res):
+        return sum((max(r[0]) + SOFT * sum(r[0][x] for x in marks) / len(marks)) / z for r, z in zip(res, norm))
+    res = [timeline(order, qof, tb) for tb in tabs]
+    norm = [max(r[0]) for r in res]
+    best = cur = score(res)
+    bo, bq = list(order), list(qof)
+    for it in range(iters):
+        done, pred = res[it % len(tabs)]
+        cv, cs, lat, dl = tabs[it % len(tabs)]
+        i = done.index(max(done)) if rand(2) else marks[rand(len(marks))]
+        cand = []
+        while i >= 0:
+            j = pred[i]
+            if j >= 0 and j not in dset[i]:
+                cand.append(i)
+                if flex[j]:
+                    cand.append(-j - 1)
+            if flex[i]:
+                cand.append(-i - 1)
+            i = j
+        if not cand:
+            continue
+        i = cand[rand(len(cand))]
+        w = rand(6)
+        nq, no = qof, order
+        if i < 0:
+            i = -i - 1
+            nq = list(qof)
+            to = "S" if qof[i] == "V" else "V"
+            for x in (same[i] if w < 2 else [i]):
+                nq[x] = to
+        if nq is qof or rand(2):
+            key = [0.0] * n
+            z = 0.0
+            for x in order:
+                z += 0.001
+                key[x] = done[x] - lat[x] - (cs[x] if qof[x] == "S" else cv[x]) + z
+            j = pred[i]
+            if nq is not qof or j < 0:
+                a, dt = i, rand(1200) - 600.0
+            elif rand(2):
+                a, dt = i, key[j] - key[i] - 1.0 - (rand(600) if rand(3) == 0 else 0)
+            else:
+                a, dt = j, key[i] - key[j] + 1.0 + (rand(600) if rand(3) == 0 else 0)
+            for x in (same[a] if w < 2 else same2[a] if w == 2 else [a]):
+                key[x] += dt
+            if dt < 0:
+                for x in range(n - 1, -1, -1):
+                    kx = key[x] - 0.0001
+                    for d in deps[x]:
+                        if key[d] > kx:
+                            key[d] = kx
+            else:
+                for x in range(n):
+                    for d in deps[x]:
+                        if key[d] >= key[x]:
+                            key[x] = key[d] + 0.0001
+            no = sorted(range(n), key=lambda x: key[x])
+        r2 = [timeline(no, nq, tb) for tb in tabs]
+        m = score(r2)
+        temp = TEMP / norm[0] * (1.0 - it / iters) + 1e-7
+        if m <= cur or rand(1000) < 1000.0 * 2.718281828 ** (-(m - cur) / temp):
+            order, qof, res, cur = no, nq, r2, m
+            if m < best:
+                best, bo, bq = m, list(no), list(nq)
+    return bo, bq, [max(timeline(bo, bq, tb)[0]) for tb in tabs]
+
+
 PLAN = {}
+ABC = "0123456789ABCDEFGHIJKLMNOPQRSTUVWXYZabcdefghijklmnopqrstuvwxyz"
+ORDER = "0002040u060E0A0Q0C080G0I1W0k0Y0K0m1S0o0a1B0S1Y0q1C1E1M0i1o1H161J1U1O0s18110M0x150O0z0U131w0W1s1q1y1Q1u1K1a2G421c1g1e27202Y283u2a4M22253m3t2Q2I2K2c2k3p2S2i2A2e2C2E2m2M3q2g2U2O4K1i2W4W4O2o4C2q2u3w2w2s4E2z4Q304G4432460e344I36484U4S4Y383y3A0c4A403C3I1k4a3H5o4g4i4c4e3F3K4m4l4o3M5Z4q3O4s3Q1m4u3S4w7a5f3U4y52573W3Y543a3d513e3k3g5c3i5b585A5C7K5E7R5y5q5G5s5I660g5u5K6A6I606G625M5g6C5w686K5P645i6E5k6M5m7P6O5Q6Q6S6U5S5W6Y6W5U6a7N6c6e6g6i7k6q6k6p7c827w9M7s6m6t7S7e7u7m847g6u6w7y7o6y707U9980727i86747W767Y7q9C78887B8A8E9B7C8G8C7E8K8I7G977I8M8O8Q8S9W8U8d8a8W9o9i9OB89e9E9Q8e8Z9g9Y9k9a8g8i9q9S8k8m9G9cAt8o9U9m8q9s9I8s9KAw8u9u8x9wA0Az8yA29y9490A692A5A8AvAAACAEAGBIARAKAIBUBABaCuBQAOANB0BCBKBSB2BMASBcAUBEAWBWAYCjAaBYB4AcBOAeBeBGCgB6AgBgAjBiBmCfAkBoBkAqAmBsAoBrBuClBwByC0C2D4CCC4C7DMDGCwEgDCC8CBD6CyCmDEDOD0CECGCoD8CIDICKD2ERCMDADQCODKCqCQCsEUCSDSCVDUDYEXCWDaDWCcCYDeCaDdDgETDiDkDmDoEqDzDqDwEiF8F2GWEyDsDvEkEYEsF0FAEuE0E2F4EmE4E6EaEwGNE8F6EoEAFCEcECEeGKEEFEEHFGFKGJFMEIFIEOEKFQEMFPFSGHFUFWFYFaGgFcFfFkGyGsGYISGoFgFjGaGOGqGiH0GcFmFoGuGkFqFsGQIDFuGmGeFwGwH2FyGSIIGUG0H4G3H6HAIFG4HCG6GAH8G8HEHGIHHIHKHMGDHOIuIUHQGEHdIcIkIWIwIoIKImIYIeIqIyIgIaIMIsHgIiIOJ0IQHjJ2J6J8J4JAJCHSHUJEHfJGJIJKJMHXHkJaJdHYHmHoHqJeJZHsJgJOHuHaJiHwJkJmHyJQJoI1JTJqI2I8JsJUI4JuJwI6JyK4K0K8K2KAJWIAK6"
+
+
+ORDER = "0400020u060Q080A0I0C0E1W0G0k0Y0K0m1S0a0o0S1B1Y1C0q1E1o0i1H161M1U1J1O0s18110M0x0O150U0z131w0W1s1q1y1Q1u1K1a2G421c1g1e2720282Y2a3u4M22252A3t3m2I2K2Q3p2S2k2i2c2C2e2m2M3q1i4K2U2g2O2E2W3w4C4W2o4O2q2u2w2s4E2z4Q304G4432460e344I48364U4S4Y383y3A4A0c403C4a4c1k4e5o4g4i3H3I4m3K3F4o4l3M4q3O4s3Q1m4u3S5f4w7a3U4y3W3Y5Z523a3d573e3k3g543i515c5b585A7K5C7R5E5q5G5s0g5I665u5K5y6I60685g626A6C6G5w5M6K5P5i646E5Q6M5k5S7P5m6O6S5U6U6Q5W6W6Y7N6a6c6e7k6g826i7c6p6m6k9M7w7e7S7s6q7m6t7u7y7g6u6w847o6y707U7i99728086747W7Y7q769C88787B8A8E9B7C8G8C7E8K978I7G7I8M8O8Q9O8S9o8UB89W8a8Z8W9i9Q8e8d9e9Y9E9g9q9a8g8i9k9S8k8m9G9cAt8o9U9m8q9s9I8s9KAw9u8u8x9wA0Az8yA29y9490A6A592AvA8AAACAEBIBaAGBUAKAIARBACuBSBCAOANBQBKB0BWBMASAUBcBEAWAYB2BYCjAaBOB4AcBGBeAeB6CgBgAgAjBiBmCfAkBoBkAqAmBsBrAoClBuBwByC0CwDMC2EgD4C4CBCCDGD6C8C7DEDCCmCyCoD0DOCECGD8CIDICKD2ERCMDADQCODKCqCQCsEUDSCSCVDUDYEXCWDaDWCcCYDeDdCaETDgDiDkDmEqF8DoEiDqDwDvGWF2EsDsDzEyEYEkF0FAEuE0E2EaEmE4F4E6EwGNE8EoF6EAFCEcECEeGKFEEEEHFGFKFMGJEIEOFIEKFQFPEMGHFSFUFWFYGYGyFaISGgFcFkFjGsGaFgFfGqGoGOGiGuGcFmFoGQGkFqH0FsGeIDFuGmGwFwH2GSFyGUIIH4G0G3H6HAIFG4HCG6GAH8G8IHHEHGHIHKGDIuHMIcGEHOIUHQHdIkIWIwIKIeIYIoIqImIyIgIaIMIsHgIiIOJ0IQHfJ2J6J8J4JAJCHSHjHUJEJGJIHXHkJKHYHmJMHoJaJZHqJeJdJOHsJgHaJiHuJkHwJmHyJQJoI1JTJqI2I8JUJsI4JuJwI6JyK4K0K8K2KAJWIAK6"
+
+
+ORDER = "0002040u060I080K0A0k0C0E0G0i0Q0S0Y0m0x0z0a111S0o131A151C0q1E0s0O171M190M1H0U1J1K1O2G1Y421Q0W1U1W1a1c1e1g1o1q1s1u1w1y25224M2Y2a3u2621281i3t2I2A2e2K2Q2k2M2S2i1k3o2U2C2c2O2E3r4K3m2g2W2m2o0c4C4W4E2q444G2s2u4O4Q464U48301m4I322w3w0e4S2z344Y4A363y4a40384c4g4i4e5o4l3A4m3C4o4q4s4u4w7a4y3F3G3K3J3O3M52553Q3S3U513W3Y3a5Z5A3c0g3e3k583g5f563i7L5a5E5C5G5d5I5K5M7R5q5O6A665s6C5y5u606I6G5Q626E685S5w5g6K5U5i645k6M5m7N6O6S6U6Q5W6W6Y7P6a6c6e7k6g7w6i826q6k6t7c7s6o6n7e7m7S707y7o6w7u6y847g6u80727q867U7i7W8874769M7Y8A788E977A8C7C7I8G7E9D8K987G8J8M9B8O8Q8S8U9o9W8Y8W8b9O9iB88c8f8g8i9e9Q9k8m9S9Y9q9E8k9a9m8o9g9U9s9c9G8q8s9u9IAx8u9K9w8w9y8yA0A290AtA6Au9294A5A8AzAAACAEBIAGAIAOARBUBaBAAMALAWAYBQBCBWAUBEBKBcASBMBYBSAaB0BeBGBOB2AcAeBgB4ClAgB6BiBmBoAiBkAkCuAqAmBrBsCgCjAoBuCfBwByC0DMC2D4C6C4C9CwDGCACDCGDCD6DICED8CyDOCKD0CICmDKCMDEEgCoD2DQDACOCQCqDSCsCSEVDUCUDWCWCcDYCYDaEXESDeCaDdDgERDiDkDmDoEqDuDqDtF2F8EiGWDwDzE2EyEkF4EYE0EmE6FAE4EsE8F0EaF6EuEoEcEAECFCEEEwFEEGGNEIEeFGEKEOFKFMFIEMGIFPFQGHFSFUGLFWFYFaGgFiFcFlISGyGYGsFeFhGoGiGuGaFqGcH0FsFmGkFoGOGwFuGqGeGQH2GmFwGSFyH4GUG0IJH6G2H8G4GAHAG6HCIEHGG8HFIDHIHKIHHMHOHQHSHdIcHeIoIuIUHjHgHmHkIkIeIqHoIgIWIwIKHqIYImIsHsIiIyIaIMHuHwJ0IOGDHyIQHUJ2I0J6HXJ8GEJ4I2HYJBI8I4JCI6JEJGJIJKJMJOJZJaJQJfJcJiJgJSJkHaJUJmIAJoJqJsJuJwJyK4K0K8K2KAJWK6"
+
+
+ORDER = "0400020u060Q0I081W0A0C0Y0E0G0k0K0m1S0a0S0o1B1Y0q1C0i1H1E1J1o160s1M1U111O0x18150M0z0O130U1w0W1s1q1y1Q1u1K1a2G421c1g1e20252Y4M22272a283u3m3t2I2K2A2k2Q2M2S2i2e2C2U2O2c3q3p4K2W2E1i2m2g2o4W4C2q4E2s444G4Q46302u2w320e4I2z4Y344O483w4U363y404S384A0c4a3A4c3C5o1k4e4g4i4m3H3K3I3F4o4l5f3M4q3O4s3Q5Z1m3S4u3U7a4w3W4y3Y523a3d573e3k3g0g51543i5b5c585A7R7K5C5E5q5G665s6I5y5u606C5g6A626K685w5I6G5i6E5K645k6M5m5M5P6O7N6Q5Q5W6S5S6Y5U6U6a6X6c7P6e6g7c6i9M7k826p6q6k7s7e6m6t7m7u7w7y7g7S6u6w847o6y707U8672997q7i80747W887Y76978A8E8C788G9D7A8I8K7C8M9B7I7E8O7G8Q9O8S9o9i8UB89W8e8W8d8a8Z9e9Q9q9Y9S9g8g9k8i9a8k8mAz9E9s8o9U9G9c9m8q9I9u9KAx8s9wA0A29y8uAt8wA4A68yA8Av9490AA92ACBUBIAEAGCuBABaAOAIANAKARBSBKBQBcBCBMASBWAUBEAWAYCjBeAaB0BGB2BYBOAcB4BgB6ChAeBiBmBkAgBoCfAiBqBsAkBuClAqAmBwAoByDMCwC0D4DGC2EgC4C7C8CCCBCyDCD0D6DICED8CGDOCICKERD2CMCmDKCoDADQCODECqDSCsETCQDUDYDaDWCSEXCUDcDeCWDgEVCcCYDiCaDkF2EqDmEiF8DoGWDwDqDvDsDzEsEyEuF0EkFAE0EmE2F4E4E6GNEwE8EYFCEaEoF6EAEcFEEeGJECFGFKFIEEFMGHEGFOFQEIFSGLEOEKFUEMFWGyGYFYGgGsFaISFkFcFfFgFjGoGiH0GaGkFmGuFoGcFqFsIJGmFuGqGeH2GOFwGwGQH4IHFyGSGUG0H6HAG2HCIDH8G4G6HGIFHEGAG8HIHKIUHMHOHQHgHdIkIWIwIcIYImIeIqIuIgIyIoIKIaIMIsHSGDIiIOJ0IQGEJ2HUJ4J6J8HXHfJAJCHYJEHjJGJIHkJKHmHoJMHqJeJdHaJaJZHsJOJgHuJiJkHwJmJQJoHyJTI1JqJUI2JsI8I4JuJxI6JyK4K0K8K2KAJWIAK6"
 
 
 def rank_program(g, core, T, topo):
@@ -501,9 +604,12 @@ def rank_program(g, core, T, topo):
     ops = make_ops(g, T, topo, core, rank)
     depend(ops)
     if "order" not in PLAN:
-        tabs = [costs(ops, m) for m in MODELS]
-        order, qof = schedule(ops, tabs[0])
-        PLAN["order"], PLAN["q"], PLAN["best"] = improve(ops, order, qof, tabs, ITERS)
+        PLAN["ops"] = ops
+        code = [ABC.index(ORDER[x]) * 62 + ABC.index(ORDER[x + 1]) for x in range(0, len(ORDER), 2)] or range(0, 2 * len(ops), 2)
+        PLAN["order"] = [x // 2 for x in code]
+        PLAN["q"] = [""] * len(ops)
+        for x in code:
+            PLAN["q"][x // 2] = ops[x // 2]["qs"][x % 2]
     eng = {"V": g.vector, "S": g.scalar, "P": g.tensor, "G": g, "Y": g.sync}
     known = {q: {} for q in eng}
     count = {"V": 0, "S": 0, "P": 0, "G": 0}

@@ -2,15 +2,14 @@ from concourse.bass import DstId, RemoteDMATransfer
 from concourse.mybir import AluOpType, ActivationFunctionType
 
 STEPS, CH, NL = 5, 2, 128
-KP = [32, 32, 32, 32]
+KP = [32, 32, 24, 16, 8, 8, 8]
 EP = [32, 32, 32, 32]
-NABS = 2
+NS = [4, 3]
+ALIAS = 3
 MAGIC = 12582912.0
-MODELS = [(0.87, 1.3, 0.44, 60.0, 1700.0, 330.0), (1.1, 1.7, 0.55, 60.0, 2100.0, 260.0)]
-ITERS, TEMP, SOFT, SEED = 15000, 300.0, 0.5, 12345
 
 SCRATCH = {"thr": ("sbuf", [1, 128], "float32"), "thh": ("sbuf", [1, 128], "float16"), "wr": ("sbuf", [1, 128], "bfloat16"),
-           "cb": ("sbuf", [1, 256], "bfloat16"), "cx": ("sbuf", [1, 256], "float16")}
+           "g2w": ("sbuf", [1, 128], "bfloat16"), "cb": ("sbuf", [1, 8], "bfloat16"), "cx": ("sbuf", [1, 128], "bfloat16")}
 
 
 def _declare(where, dtype, names, cols, per_chunk=False):
@@ -19,8 +18,8 @@ def _declare(where, dtype, names, cols, per_chunk=False):
             SCRATCH["%s%s" % (nm, x)] = (where, [128, cols], dtype)
 
 
-_declare("sbuf", "bfloat16", "keyt", 4128)
-_declare("sbuf", "bfloat16", "emt", 4112)
+_declare("sbuf", "bfloat16", "keyt", 8224)
+_declare("sbuf", "bfloat16", "emt", 8208)
 _declare("sbuf", "int32", "clt", 2056)
 _declare("sbuf", "int32", "plt", 256)
 _declare("sbuf", "float32", "sf lf", 256)
@@ -33,7 +32,8 @@ _declare("sbuf", "bfloat16", "lq", 1536)
 _declare("sbuf", "float16", "lp sp", 1280)
 _declare("sbuf", "uint16", "lu su", 1280)
 _declare("sbuf", "bfloat16", "sq", 1280)
-_declare("sbuf", "bfloat16", "ones idm bma bm nid hid sid kid mid nq", 128)
+_declare("sbuf", "bfloat16", "ones idm bma bm nid hid kid aid nq", 128)
+_declare("sbuf", "bfloat16", "sr", 256)
 _declare("sbuf", "bfloat16", "gw g2 gn", 8)
 _declare("sbuf", "bfloat16", "kv", 32)
 _declare("sbuf", "bfloat16", "ga gb r0 r1", 64)
@@ -51,9 +51,9 @@ _declare("sbuf", "bfloat16", "sg", 256, True)
 _declare("sbuf", "float16", "sc", 256, True)
 _declare("sbuf", "float32", "s2", 64, True)
 _declare("sbuf", "bfloat16", "yy oh on fl", 128, True)
-_declare("sbuf", "float32", "g1 fm bs", 128, True)
+_declare("sbuf", "float32", "y4 g1 fm bs", 128, True)
 
-SEMAPHORES = ["V", "S", "P", "G", "lsem", "ld_pl", "ld_q", "ld_key", "ld_th", "ld_w", "ld_emb", "ld_cl", "ld_em", "st"]
+SEMAPHORES = ["V", "S", "P", "G", "lsem", "ld_pl", "ld_p1", "ld_q", "ld_key", "ld_th", "ld_w", "ld_emb", "ld_cl", "ld_em", "st"]
 for _t in range(STEPS):
     for _c in range(CH):
         SEMAPHORES += ["ap%d%d" % (_t, _c), "aq%d%d" % (_t, _c)]
@@ -62,19 +62,13 @@ for _t in range(STEPS):
 def make_ops(g, T, topo, core, rank):
     A, F = AluOpType, ActivationFunctionType
     V, S, P = g.vector, g.scalar, g.tensor
-    ops, groups, cur = [], {}, [""]
+    ops, groups = [], {}
 
     def op(name, qs, fn, rd, wr, banks=(), cost=None, sem=None):
-        ops.append(dict(name=name, qs=qs, fn=fn, rd=list(rd), wr=list(wr), banks=list(banks), cost=cost, sem=sem, i=len(ops),
-                        tc=(int(cur[0][0]), int(cur[0][1])) if cur[0] else None,
-                        kind=("@".join(name.rsplit(cur[0], 1)) if "_" not in name[-3:] or name[-3] == "_" else
-                              name[:2] + name[-2:], cur[0][1:]) if cur[0] else (name, "")))
+        ops.append(dict(name=name, qs=qs, fn=fn, rd=list(rd), wr=list(wr), banks=list(banks), cost=cost, sem=sem, i=len(ops)))
 
     def vop(name, fn, rd, wr, n, banks=()):
         op(name, "V", lambda q: [fn()], rd, wr, banks, ("c", n, n))
-
-    def sop(name, fn, rd, wr, n, banks=()):
-        op(name, "S", lambda q: [fn()], rd, wr, banks, ("c", n, n))
 
     def vs(name, out, src, scale, bias, rd, wr, n, banks=()):
         def emit(q):
@@ -91,7 +85,7 @@ def make_ops(g, T, topo, core, rank):
             r = []
             for m in mms:
                 st[1] += 1
-                r.append(P.matmul(m[0], m[1], m[2], st[1] == 1 and grp[0] != "+", st[1] == st[0]))
+                r.append(P.matmul(m[0], m[1], m[2], st[1] == 1, st[1] == st[0]))
             return r
         op(name, "P", emit, rd, wr, banks, ("p", sum(m[3] for m in mms)))
 
@@ -102,33 +96,44 @@ def make_ops(g, T, topo, core, rank):
         eng = g.sync if q == "Y" else g.scalar
         op(name, q, lambda _q: [eng.dma_start(o, i) for o, i in pairs], rd, wr, (), ("d", nbytes, len(pairs)), sem)
 
+    def copy(out, src, n):
+        return g.affine_select(out, src, [[0, n]], A.is_ge, 0.0, 0, 0)
+
     first = rank == 0
     last_rank = rank == len(T.cores) - 1
     k0 = 15 if first else 16
 
     vop("kz", lambda: V.memset(T.keyt[:, 0:16], 0.0), [], ["kz"], 16)
-    dma("ld_pl", "Y", [(T.plt[:], T.pl[:])], [], ["plt", "o1"], "ld_pl", 131072)
+    dma("ld_pl", "Y", [(T.plt[:, 0:128], T.pl[:, 0:128])], [], ["plt0", "o1"], "ld_pl", 65536)
     dma("ld_th", "S", [(T.thr[:], T.th[:])], [], ["thr", "o2"], "ld_th", 8192)
     dma("ld_w", "S", [(T.wr[:], T.w[:])], ["+o2"], ["wr", "o3"], "ld_w", 8192)
     dma("ld_key", "Y", [(T.keyt[:, k0:k0 + 4096], T.key[:])], ["kz", "+o1", "+o3"], ["keyt", "o4"], "ld_key", 1048576)
-    dma("ld_q", "Y", [(T.lq[:, 0:256], T.q[:])], ["+o4"], ["lq00", "lq01", "o5"], "ld_q", 65536)
-    dma("ld_emb", "Y", [(T.embt[:], T.emb[:])], ["+o5"], ["embt", "o6"], "ld_emb", 65536)
+    dma("ld_p1", "Y", [(T.plt[:, 128:256], T.pl[:, 128:256])], ["+o4"], ["plt1", "o5"], "ld_p1", 65536)
+    dma("ld_q", "Y", [(T.lq[:, 0:256], T.q[:])], ["+o5"], ["lq00", "lq01", "o6"], "ld_q", 65536)
     dma("ld_cl", "Y", [(T.clt[:, 0:2048], T.cl[:])], ["+o6"], ["clt0", "o7"], "ld_cl", 1048576)
-    dma("ld_em", "Y", [(T.emt[:, 0:4096], T.em[:])], ["+o7"], ["emt"], "ld_em", 1048576)
+    dma("ld_em", "Y", [(T.emt[:, 0:4096], T.em[:])], ["+o7"], ["emt", "o8"], "ld_em", 1048576)
+    dma("ld_emb", "Y", [(T.embt[:], T.emb[:])], ["+o8"], ["embt"], "ld_emb", 65536)
 
     vop("ones", lambda: V.memset(T.ones[:], 1.0), [], ["ones"], 64)
     vop("c2k", lambda: V.memset(T.c2k[:], 2048.0), [], ["c2k"], 512)
     for c in range(CH):
         a, b = c * NL, c * NL + NL
         vop("u0_%d" % c, lambda a=a, b=b: V.tensor_scalar(T.lu[:, a:b], T.plt[:, a:b], 15.0 if first else 0.0, None, A.add),
-            ["plt"], ["lu0%d" % c], 128)
-        vop("p0_%d" % c, lambda a=a, b=b: V.tensor_scalar(T.lp[:, a:b], T.plt[:, a:b], -2048.0, None, A.add), ["plt"],
+            ["plt%d" % c], ["lu0%d" % c], 128)
+        vop("p0_%d" % c, lambda a=a, b=b: V.tensor_scalar(T.lp[:, a:b], T.plt[:, a:b], -2048.0, None, A.add), ["plt%d" % c],
             ["lp0%d" % c], 128)
         vop("sga%d" % c, lambda c=c: V.memset(T["sg%d" % c][:], 1.0), [], ["sg%d" % c], 128)
-        vop("sgb%d" % c, lambda c=c: V.memset(T["sg%d" % c][:, 31::32], -1.0), [], ["sg%d" % c], 8)
-    vop("kal", lambda: V.tensor_copy(T.keyt[:, k0 + 4096:k0 + 4097], T.keyt[:, k0:k0 + 1]), ["keyt"], ["kal"], 1)
+        vop("sgb%d" % c, lambda c=c: V.memset(T["sg%d" % c][:, 31::32], 0.0), [], ["sg%d" % c], 8)
+    for j in range(4):
+        a = k0 + 1024 * j
+        gop("ky2_%d" % j, lambda a=a: copy(T.keyt[:, a + 4096:a + 5120], T.keyt[:, a:a + 1024], 1024), ["keyt"],
+            ["ky2_%d" % j], 1024)
+    vop("kal", lambda: V.tensor_copy(T.keyt[:, k0 + 8192:k0 + 8193], T.keyt[:, k0:k0 + 1]), ["keyt"], ["kal"], 1)
     vop("cal", lambda: V.tensor_copy(T.clt[:, 2048:2049], T.clt[:, 0:1]), ["clt0"], ["clt"], 1)
-    vop("eal", lambda: V.tensor_copy(T.emt[:, 4096:4097], T.emt[:, 0:1]), ["emt"], ["eal"], 1)
+    for j in range(8):
+        a = 512 * j
+        gop("em2_%d" % j, lambda a=a: copy(T.emt[:, a + 4096:a + 4608], T.emt[:, a:a + 512], 512), ["emt"], ["em2_%d" % j], 512)
+    vop("eal", lambda: V.tensor_copy(T.emt[:, 8192:8193], T.emt[:, 0:1]), ["emt"], ["eal"], 1)
 
     def sel(name, src, n, pattern, cmp, base, cm):
         gop(name, lambda: g.affine_select(T[name][:], T[src][:, 0:n], pattern, cmp, 0.0, base, cm), [src], [name], n)
@@ -145,33 +150,31 @@ def make_ops(g, T, topo, core, rank):
         vs(name, T[name][:], T[src][:, 0:n], float(k), 0.0, [src], [name], n // 2)
     scaled("nid", "idm", -1.0, 128)
     scaled("hid", "idm", 0.5, 128)
-    scaled("sid", "idm", 1.0 / 4096.0, 128)
+    vs("sid", T.sr[:, 0::2], T.idm[:], 1.0 / 4096.0, 0.0, ["idm"], ["sid"], 64)
+    vs("si1", T.sr[:, 1::2], T.idm[:], -1.0 / 4096.0, 0.0, ["idm"], ["si1"], 64)
     scaled("kid", "idm", -4096.0, 128)
-    scaled("mid", "idm", -2048.0, 128)
     scaled("g2", "gb", 2.0, 8)
     scaled("gn", "gb", -1.0, 8)
     scaled("nq", "bm", -1.0, 128)
-    for b in range(NABS):
+    for b in range(2):
         vop("nq%d" % b, lambda b=b: V.memset(T.nq[:, b::4], 0.0), [], ["nq"], 16)
+        for j in range(NS[b], 4):
+            vop("nq%d%d" % (b, j), lambda s=4 * j + b: V.tensor_scalar(T.nq[:, s::16], g8, -1.0, None, A.mult), ["gb"], ["nq"], 8)
     vs("r0", T.r0[:], T.gb[:], -256.015625, 256.0, ["gb"], ["r0"], 32)
     vs("r1", T.r1[:], T.gb[:], -255.984375 if first else -256.015625, 256.0, ["gb"], ["r1"], 32)
     vop("thh", lambda: V.tensor_scalar(T.thh[:], T.thr[:], -1.0, 2048.0, A.mult, A.add), ["thr"], ["thh"], 128)
     mm("gwp", "gwp", [(T.tk[:, 0:8], T.wr[:], T.c2k[0:1, 0:8], 64)], ["wr", "c2k"], ["gwp"], ["btk"])
     vop("gw1", lambda: V.tensor_tensor(T.gw[:], T.tk[:, 0:8], g8, A.mult), ["gwp", "gb"], ["gw"], 8, ["btk"])
     vop("gw", lambda: V.tensor_scalar(T.gw[:], T.gw[:], 1.0 / 4194304.0, None, A.mult), ["gw"], ["gw"], 8)
-    vop("cb", lambda: V.memset(T.cb[:], -1.0), [], ["cb"], 128)
-    vop("cb1", lambda: V.memset(T.cb[:, 31::32], -0.5), [], ["cb"], 8)
-    vop("cx", lambda: V.memset(T.cx[:, 0:128], -2048.0), [], ["cx"], 64)
-    vop("cx1", lambda: V.memset(T.cx[:, 128:256], -2047.0 if first else -2048.0), [], ["cx1"], 64)
+    vop("cb", lambda: V.memset(T.cb[:], -0.5), [], ["cb"], 8)
+    vop("cx", lambda: V.memset(T.cx[:], 1.0 if first else 0.0), [], ["cx"], 64)
+    vop("g2w", lambda: V.memset(T.g2w[:], 3.0), [], ["g2w"], 64)
+    scaled("aid", "idm", -12288.0, 128)
     vop("kcj", lambda: V.tensor_scalar(T.kcj[:], T.kci[:], 15, None, A.bitwise_and), ["kci"], ["kcj"], 1)
     vop("kcf", lambda: V.tensor_copy(T.kcf[:], T.kcj[:]), ["kcj"], ["kcf"], 1)
     vop("kv0", lambda: V.memset(T.kv[:, 8:32], 0.0), [], ["kv0"], 16)
     vop("kv", lambda: V.tensor_scalar(T.kv[:, 0:8], g8, T.kcf[:], None, A.mult), ["gb", "kcf"], ["kv"], 8)
     vop("embs", lambda: V.tensor_scalar(T.embs[:], T.embt[:], 0.5, -0.25, A.mult, A.add), ["embt"], ["embs"], 16)
-    mm("ebp", "ebp", [(T.tk[:, 256 + 16 * j:272 + 16 * j], T.idm[:], T.embs[:], 64) for j in range(8)], ["idm", "embs"], ["ebp"],
-       ["btk"])
-    vop("ebk", lambda: V.tensor_tensor(T.ebk[:], T.tk[:, 256:384], T.bm[:], A.mult), ["ebp", "bm"], ["ebk"], 128, ["btk"])
-    EBK = ["ebk"]
     vop("z8", lambda: V.memset(T.z8[:], 0.0), [], ["z8"], 64)
     vop("z8b", lambda: V.memset(T.z8[:, 0::8], 16384.0), [], ["z8"], 8)
     vop("zf", lambda: V.memset(T.zf[:], 0.0625), [], ["zf"], 128)
@@ -196,14 +199,14 @@ def make_ops(g, T, topo, core, rank):
     def step(t, c):
         n, nn = "%d%d" % (t, c), "%d%d" % (t + 1, c)
         o = t * 256 + c * NL
-        cur[0] = n
         here, dst = slice(o, o + NL), slice(o + 256, o + 256 + NL)
         p, q = T.lp[:, here], T.lq[:, here]
         Db, Bb = T["D%d" % c], T["B%d" % c]
         bD, bB = "bD%d" % c, "bB%d" % c
-        kg, ab, qx, ls, sg, sc, s2, yy, oh, on, fl, g1, eg, fm, bs = (T[x + str(c)] for x in (
-            "kg ab qx ls sg sc s2 yy oh on fl g1 eg fm bs".split()))
+        kg, ab, qx, ls, sg, sc, s2, yy, y4, oh, on, fl, g1, eg, fm, bs = (T[x + str(c)] for x in (
+            "kg ab qx ls sg sc s2 yy y4 oh on fl g1 eg fm bs".split()))
         last = t == STEPS - 1
+        alias = 2 * t + c >= ALIAS
 
         def k(x):
             return "%s%d" % (x, c)
@@ -211,8 +214,12 @@ def make_ops(g, T, topo, core, rank):
             win_k, kw = (T.keyt[:, 0:4111] if first else T.keyt[:, 16:4112]), ["keyt"]
             win_e, ew = T.emt[:, 0:4096], ["emt"]
         else:
-            win_k, kw = T.keyt[:, 16:k0 + 4097], ["kal"]
-            win_e, ew = T.emt[:, 0:4097], ["eal"]
+            win_k, kw = T.keyt[:, 16:k0 + 4097], ["ky2_0"]
+            if 2 * t - 2 + c >= ALIAS:
+                win_k, kw = T.keyt[:, 16:k0 + 8193], ["kal"] + ["ky2_%d" % j for j in range(4)]
+            win_e, ew = T.emt[:, 0:4097], ["em2_0"]
+            if alias:
+                win_e, ew = T.emt[:, 0:8193], ["eal"] + ["em2_%d" % j for j in range(8)]
         ko = (t % 2) * 2048
         kr, a = [], 0
         for j, w in enumerate(KP):
@@ -221,14 +228,24 @@ def make_ops(g, T, topo, core, rank):
                    kw + ["lu" + n], [kr[j]], 16 * w)
             a += w
         hcol = Bb[:, 31:256:32]
-        hq = Bb[:, 448:456]
-        mm("h" + n, "H" + n, [(hq, T.ones[0:1, :], T.cb[:, 31::32], 64), (hq, q, T.gw[:], 64)], ["lq" + n, "gw", "ones", "cb"],
-           [k("F")], [bB])
-        vop("qx" + n, lambda: V.tensor_scalar(qx[:], hq, MAGIC, -MAGIC, A.add, A.add), [k("F")], [k("qx")], 8, [bB])
-        mm("bc" + n, "B" + n, [(Bb[:, 0:256], T.ones[0:1, :], T.cb[:], 256), (Bb[:, 0:256:2], p, T.sid[:], 128)],
-           ["lp" + n, "ones", "cb", "sid"], [k("B")], [bB])
+        hq = T.tk[:, 256 + 8 * c:264 + 8 * c]
+        mm("h" + n, "H" + n, [(hq, T.ones[0:1, :], T.cb[:], 64), (hq, q, T.gw[:], 64)], ["lq" + n, "gw", "ones", "cb"],
+           [k("H")], ["btk"])
+        vop("qx" + n, lambda: V.tensor_scalar(qx[:], hq, MAGIC, -MAGIC, A.add, A.add), [k("H")], [k("qx")], 8, ["btk"])
+        if t:
+            mm("tk" + n, "T" + n, [(T.tk[32 * t - 32:32 * t, c * NL:c * NL + NL], T.kv[:], on[:], 128)], [k("on"), "kv", "kv0"],
+               ["tk" + n], ["btk"])
+        if last and c == CH - 1:
+            vs("yta", T.ytb[:, 0:256], T.tk[:, 0:256], 1.0, 0.0, ["tk%d%d" % (x, y) for x in range(1, 5) for y in range(CH)],
+               ["yta"], 256, ["btk"])
+            dma("sta", "Y", [(T.yt[:, 256 * x:256 * x + 256], T.ytb[32 * x:32 * x + 8, 0:256]) for x in range(4)], ["yta"],
+                ["ytad"], "st", 32768)
+        mm("bc" + n, "B" + n, [(Bb[:, 0:256], p, T.sr[:], 256), (hcol, T.ones[0:1, :], T.cb[:], 64)],
+           ["lp" + n, "ones", "cb", "sid", "si1"], [k("B")], [bB])
         mm("bq" + n, "B" + n, [(hcol, q, T.gw[:], 64), (hcol, T.nid[:], qx[:], 64)], ["lq" + n, "gw", k("qx"), "nid"], [k("B")],
            [bB])
+        f = Bb[:, 384:448]
+        mm("fe" + n, "F" + n, [(f, T.bm[:], T.r0[:] if t == 0 else T.r1[:], 64)], [k("B"), "bm", "r0", "r1"], [k("F")], [bB])
         d = Db[:, 0:128]
         mm("dt" + n, "D" + n, [(d, T.ones[0:1, :], T.thh[:], 128)], ["ones", "thh"], [k("d")], [bD])
         parts = []
@@ -236,48 +253,68 @@ def make_ops(g, T, topo, core, rank):
         def dpart(name, mms, rd):
             parts.append(k("d") + name)
             mm(name + n, "D" + n, mms, rd + [k("d")], [parts[-1]], [bD])
-        for b in range(NABS):
-            mm("xk%s_%d" % (n, b), "x%s%d" % (n, b), [(X[b % 2][:, 128 * j:128 * j + 128], T.idm[:],
-               kg[:, ko + 4 * j + b:ko + 2048:16], 128) for j in range(4)], kr + ["idm"], ["x%d" % (b % 2)], ["bx%d" % (b % 2)])
-            mm("xq%s_%d" % (n, b), "x%s%d" % (n, b), [(X[b % 2][:, 128 * j:128 * j + 128], T.nid[:], q, 128) for j in range(4)],
-               ["lq" + n, "nid"], ["x%d" % (b % 2)], ["bx%d" % (b % 2)])
-            sop("ab%s_%d" % (n, b), lambda b=b: S.activation(ab[:, 512 * b:512 * b + 512], X[b % 2][:], F.Abs), ["x%d" % (b % 2)],
-                ["ab%d_%d" % (c, b)], 512, ["bx%d" % (b % 2)])
+        for b in range(2):
+            mm("xk%s_%d" % (n, b), "x%s%d" % (n, b), [(X[b][:, 128 * j:128 * j + 128], T.idm[:],
+               kg[:, ko + 4 * j + b:ko + 2048:16], 128) for j in range(NS[b])], kr + ["idm"], ["x%d" % b], ["bx%d" % b])
+            mm("xq%s_%d" % (n, b), "x%s%d" % (n, b), [(X[b][:, 128 * j:128 * j + 128], T.nid[:], q, 128) for j in range(NS[b])],
+               ["lq" + n, "nid"], ["x%d" % b], ["bx%d" % b])
+            op("ab%s_%d" % (n, b), "S", lambda _q, b=b: [S.activation(ab[:, 512 * b:512 * b + 128 * NS[b]],
+                                                                      X[b][:, 0:128 * NS[b]], F.Abs)],
+               ["x%d" % b], ["ab%d_%d" % (c, b)], ["bx%d" % b], ("c", 128 * NS[b], 128 * NS[b]))
             dpart("da%d_" % b, [(Db[:, 4 * j + b:128:16], ab[:, 512 * b + 128 * j:512 * b + 128 * j + 128], g8, 64)
-                                for j in range(4)], ["ab%d_%d" % (c, b), "gb"])
-        if NABS < 4:
-            mm("xr" + n, "xr" + n, [(T.xr[:, j::4], T.idm[:], q, 128) for j in range(4)], ["lq" + n, "idm"], ["xr"], ["bxr"])
-            dpart("dq", [(d, q, T.nq[:], 128)], ["lq" + n, "nq"])
-        for b in range(NABS, 4):
+                                for j in range(NS[b])], ["ab%d_%d" % (c, b), "gb"])
+        mm("xr" + n, "xr" + n, [(T.xr[:, j::4], T.idm[:], q, 128) for j in range(4)], ["lq" + n, "idm"], ["xr"], ["bxr"])
+        dpart("dq", [(d, q, T.nq[:], 128)], ["lq" + n, "nq"])
+        for b in range(2):
+            for j in range(NS[b], 4):
+                s, w = 4 * j + b, 512 * b + 128 * j
+                dpart("dk%d%d_" % (b, j), [(Db[:, s:128:16], kg[:, ko + s:ko + 2048:16], T.gn[:], 64)], kr + ["gn"])
+                vop("my%d%d_%s" % (b, j, n), lambda s=s, w=w: V.tensor_tensor(ab[:, w:w + 128], kg[:, ko + s:ko + 2048:16],
+                                                                              T.xr[:, 0::4], A.max), kr + ["xr"],
+                    ["ab%d_%d%d" % (c, b, j)], 128, ["bxr"])
+                dpart("dm%d%d_" % (b, j), [(Db[:, s:128:16], ab[:, w:w + 128], T.g2[:], 64)], ["ab%d_%d%d" % (c, b, j), "g2"])
+        for b in range(2, 4):
             dpart("dk%d_" % b, [(Db[:, 4 * j + b:128:16], kg[:, ko + 4 * j + b:ko + 2048:16], T.gn[:], 64) for j in range(4)],
                   kr + ["gn"])
             vop("mx%s_%d" % (n, b), lambda b=b: V.tensor_tensor(ab[:, 512 * b:512 * b + 512], kg[:, ko + b:ko + 2048:4], T.xr[:],
                                                                 A.max), kr + ["xr"], ["ab%d_%d" % (c, b)], 512, ["bxr"])
             dpart("dm%d_" % b, [(Db[:, 4 * j + b:128:16], ab[:, 512 * b + j:512 * b + 512:4], T.g2[:], 64) for j in range(4)],
                   ["ab%d_%d" % (c, b), "g2"])
-        sge = sg[:, 0:256:2]
-        sop("sg" + n, lambda: S.activation(sge, d, F.Sign, -2047.5), parts, [k("sg"), k("d")], 128, [bD])
-        mm("bs" + n, "B" + n, [(Bb[:, 0:256:2], T.nid[:], sge, 128)], [k("sg"), "nid"], [k("B")], [bB])
-        vop("sc" + n, lambda: V.tensor_tensor_scan(sc[:, ::-1], sg[:, ::-1], Bb[:, 255::-1], 0.0, A.min, A.max),
+        far = sg[:, 0:256:2]
+        vop("sg" + n, lambda: V.tensor_scalar(far, d, 2047.5, None, A.is_ge), parts, [k("sg"), k("d")], 128, [bD])
+        vop("sc" + n, lambda: V.tensor_tensor_scan(sc[:, ::-1], sg[:, ::-1], Bb[:, 255::-1], 0.0, A.mult, A.add),
             [k("B"), k("sg")], [k("sc")], 256, [bB])
-        mm("nn" + n, "N" + n, [(Db[:, 128:256], sge, T.idm[:], 128)], [k("sg"), "idm"], [k("N")], [bD])
-        x = Db[:, 256:384]
-        cx = T.cx[:, 0:128] if t == 0 else T.cx[:, 128:256]
-        mm("xx" + n, "X" + n, [(x, T.idm[:], p, 128), (x, T.ones[0:1, :], cx, 128), (x, sge, T.mid[:], 128)],
-           [k("sg"), k("N"), "lp" + n, "idm", "ones", "cx", "cx1", "mid"], [k("X")], [bD])
-        vs("yy" + n, yy[:], Db[:, 128:256], 3072.0, -5120.0, [k("N")], [k("yy")], 128, [bD])
-        f = Bb[:, 384:448]
-        mm("fo" + n, "F" + n, [(f, T.bm[:], T.r0[:] if t == 0 else T.r1[:], 64)]
-           + [(Bb[:, 384 + 8 * j:392 + 8 * j], T.fa[:, 128 * j:128 * j + 128], sc[:, 0::32], 64) for j in range(8)],
-           [k("sc"), "bm", "r0", "r1", "fa"], [k("F")], [bB])
+        x, xn = Db[:, 256:384], Db[:, 128:256]
+        if alias:
+            mm("nn" + n, "N" + n, [(xn, T.idm[:], p, 128), (xn, far, T.aid[:], 128)], [k("sg"), "lp" + n, "idm", "aid"], [k("N")],
+               [bD])
+            mm("xx" + n, "X" + n, [(x, T.c2k[0:1, 0:128], T.g2w[:], 128), (x, far, T.kid[:], 128)],
+               [k("sg"), k("N"), "c2k", "g2w", "kid"], [k("X")], [bD])
+            vs("yy" + n, y4[:], xn, 1.0, 6145.0 if first else 6144.0, [k("N")], [k("yy")], 128, [bD])
+        else:
+            mm("nn" + n, "N" + n, [(xn, far, T.idm[:], 128)], [k("sg"), "idm"], [k("N")], [bD])
+            mm("xx" + n, "X" + n, [(x, T.idm[:], p, 128)] + ([(x, T.ones[0:1, :], T.cx[:], 128)] if t else [])
+               + [(x, far, T.kid[:], 128)], [k("sg"), k("N"), "lp" + n, "idm", "ones", "cx", "kid"], [k("X")], [bD])
+            vs("yy" + n, yy[:], xn, 6144.0, -8192.0, [k("N")], [k("yy")], 128, [bD])
+        mm("fo" + n, "F" + n, [(Bb[:, 384 + 8 * j:392 + 8 * j], T.fa[:, 128 * j:128 * j + 128], sc[:, 0::32], 64)
+                               for j in range(8)], [k("sc"), "bm", "r0", "r1", "fa"], [k("F")], [bB])
         vop("s2" + n, lambda: V.tensor_tensor_scan(s2[:], T.z8[:], f, 0.0, A.add, A.min), [k("F"), "z8"], [k("s2")], 64, [bB])
         vop("ls" + n, lambda: V.tensor_scalar(ls[:], s2[:, 7::8], MAGIC + 1024.0, -MAGIC, A.add, A.add), [k("s2")], [k("ls")], 8)
-        op("g1" + n, "V", lambda _q: [V.tensor_tensor(g1[:], win_c.indirect(ls[:]), yy[:], A.add)], ["clt", k("ls"), k("yy")],
-           [k("g1")], (), ("i", 128))
         sp, su = T.sp[:, here], T.su[:, here]
-        vop("pn" + n, lambda: V.tensor_tensor(sp, g1[:], x, A.max), [k("g1"), k("X")], ["sp" + n], 128, [bD])
-        vop("un" + n, lambda: V.tensor_scalar(su, sp, 2048.0, None, A.add), ["sp" + n], ["su" + n], 64)
+        op("g1" + n, "V", lambda _q: [V.tensor_tensor(g1[:], win_c.indirect(ls[:]), y4[:] if alias else yy[:],
+                                                      A.max if alias else A.add)], ["clt", k("ls"), k("yy")], [k("g1")], (),
+           ("i", 128))
+        if alias:
+            vop("ua" + n, lambda: V.tensor_copy(su, g1[:]), [k("g1")], ["su" + n], 128)
+            vop("pn" + n, lambda: V.tensor_tensor(sp, g1[:], x, A.subtract), [k("g1"), k("X")], ["sp" + n], 128, [bD])
+        else:
+            vop("pn" + n, lambda: V.tensor_tensor(sp, g1[:], x, A.max), [k("g1"), k("X")], ["sp" + n], 128, [bD])
+            vop("un" + n, lambda: V.tensor_scalar(su, sp, 2048.0, None, A.add), ["sp" + n], ["su" + n], 64)
         r = slice(c * NL, c * NL + NL)
+        if t == 0 and c == 0:
+            mm("ebp", "ebp", [(T.D0[:, 384 + 16 * j:400 + 16 * j], T.idm[:], T.embs[:], 64) for j in range(8)], ["idm", "embs"],
+               ["ebp"], ["bD0"])
+            vop("ebk", lambda: V.tensor_tensor(T.ebk[:], T.D0[:, 384:512], T.bm[:], A.mult), ["ebp", "bm"], ["ebk"], 128, ["bD0"])
         if last:
             dl = 1.0 if last_rank else 0.0
             vop(k("fl"), lambda: V.tensor_scalar(fl[:], sp, 2048.0 - dl, None, A.is_ge), ["sp" + n], [k("fl")], 64)
@@ -300,7 +337,8 @@ def make_ops(g, T, topo, core, rank):
         er, a = [], 0
         for j, w in enumerate(EP):
             er.append("eg%d_%d" % (c, j))
-            gather("eg%s_%d" % (n, j), eg[:, 16 * a:16 * (a + w)], win_e, T.su[:, o + a:o + a + w], ew + ["su" + n], [er[j]], 16 * w)
+            gather("eg%s_%d" % (n, j), eg[:, 16 * a:16 * (a + w)], win_e, T.su[:, o + a:o + a + w], ew + ["su" + n], [er[j]],
+                   16 * w)
             a += w
         u = Bb[:, 256:384]
         for j in range(4):
@@ -313,7 +351,7 @@ def make_ops(g, T, topo, core, rank):
         mm("op" + n, "O" + n, [(u, oh[:], T.idm[:], 128)], [k("oh"), "idm"], [k("U")], [bB])
         vs("on" + n, on[:], u, 1.0, 0.0, [k("U")], [k("on")], 128, [bB])
         e = Bb[:, 384:512]
-        mm("e" + n, "E" + n, [(e, T.hid[:], q, 128), (e, T.ebk[:], on[:], 128)], ["lq" + n, k("on"), "hid"] + EBK, [k("F")], [bB])
+        mm("e" + n, "E" + n, [(e, T.hid[:], q, 128), (e, T.ebk[:], on[:], 128)], ["lq" + n, k("on"), "hid", "ebk"], [k("F")], [bB])
         sq = T.sq[:, here]
         vop("qn" + n, lambda: V.tensor_scalar(sq, e, MAGIC, -MAGIC, A.add, A.add), [k("F")], ["sq" + n], 128, [bB])
 
@@ -321,18 +359,12 @@ def make_ops(g, T, topo, core, rank):
             g.remote_dma(T.lq[:, dst], sq, T.sem["aq" + n], T.sem.lsem, pid, rid, m_all)
             return None
         op("sendq" + n, "G", send_q, ["sq" + n], ["lq" + nn], (), ("r", 0), "aq" + n)
-        y0, yc = 32 * (t % 4), 256 * (t // 4) + c * NL
-        mm("tk" + n, "T" + n, [(T.tk[y0:y0 + 32, yc:yc + NL], T.kv[:], on[:], 128)], [k("on"), "kv", "kv0"], ["tk" + n], ["btk"])
-        if t == 3 and c == CH - 1:
-            vs("yta", T.ytb[:, 0:256], T.tk[:, 0:256], 1.0, 0.0, ["tk%d%d" % (x, y) for x in range(4) for y in range(CH)],
-               ["yta"], 256, ["btk"])
-            dma("sta", "Y", [(T.yt[:, 256 * x:256 * x + 256], T.ytb[32 * x:32 * x + 8, 0:256]) for x in range(4)], ["yta"],
-                ["ytad"], "st", 32768)
         if last:
+            mm(k("tl"), k("TL"), [(Db[0:8, 0:128], T.kv[:, 0:8], on[:], 128)], [k("on"), "kv"], [k("d")], [bD])
+            vs(k("ytb"), T.ytb[0:8, 256 + c * NL:256 + c * NL + NL], Db[0:8, 0:128], 1.0, 0.0, [k("d")], [k("ytb")], 128, [bD])
             dma("stq%d" % c, "Y", [(T.yq[:, r], T.lq[:, dst])], ["lq" + nn], ["yq%d" % c], "st", 32768)
             if c == CH - 1:
-                vs("ytb", T.ytb[0:8, 256:512], T.tk[0:8, 256:512], 1.0, 0.0, ["tk40", "tk41"], ["ytb"], 256, ["btk"])
-                dma("stb", "Y", [(T.yt[:, 1024:1280], T.ytb[0:8, 256:512])], ["ytb"], ["ytbd"], "st", 8192)
+                dma("stb", "Y", [(T.yt[:, 1024:1280], T.ytb[0:8, 256:512])], ["ytb0", "ytb1"], ["ytbd"], "st", 8192)
 
     for t in range(STEPS):
         for c in range(CH):
@@ -368,233 +400,9 @@ def depend(ops):
         o["deps"], o["soft"] = sorted(d), sorted(soft - d)
 
 
-def costs(ops, model):
-    cyc, gat, pec, hop, net, bw = model[:6]
-    cv, cs, lat, t0 = [], [], [], 1500.0
-    for o in ops:
-        c, l = o["cost"], 0.0
-        if c[0] == "c":
-            a, b = 50 + max(64, c[1]) * cyc, 65 + max(64, c[2]) * cyc
-        elif c[0] == "i":
-            a, b = 50 + c[1] * cyc * gat, 65 + c[1] * cyc * gat
-        elif c[0] == "p":
-            a = b = c[1] * pec
-        elif c[0] == "g":
-            a = b = 170 + 2 * c[1] * cyc
-        elif c[0] == "r":
-            a = b = 150.0
-            l = net + 200.0 * c[1] + (1200.0 if o["name"] == "sendp00" else 0.0)
-        else:
-            a = b = 60.0 * c[2]
-            if o["sem"] == "st":
-                l = 1600.0 + c[1] / bw
-            else:
-                t0 += c[1] / bw
-                l = t0
-        cv.append(b if o["qs"] == "S" else a)
-        cs.append(b)
-        lat.append(l)
-    dl = [[(d, 0.0 if o["qs"] == "P" and ops[d]["qs"] == "P" else hop) for d in o["deps"]] for o in ops]
-    return cv, cs, lat, dl, {"V": model[6], "S": model[7]}
-
-
-def timeline(seq, qs, tab):
-    cv, cs, lat, dl, ql = tab
-    n = len(cv)
-    done, pred = [0.0] * n, [-1] * n
-    free = {"V": 0.0, "S": 0.0, "P": 0.0, "G": 0.0, "Y": 0.0}
-    lastq = {"V": -1, "S": -1, "P": -1, "G": -1, "Y": -1}
-    for i in seq:
-        q = qs[i]
-        st, pr = free[q], lastq[q]
-        for d, h in dl[i]:
-            r = done[d] + h
-            if r > st:
-                st, pr = r, d
-        free[q] = e = st + (cs[i] if q == "S" else cv[i])
-        done[i] = e + lat[i] + ql.get(q, 0.0)
-        pred[i], lastq[q] = pr, i
-    return done, pred
-
-
-def schedule(ops, tab):
-    cv, cs, lat, dl = tab
-    n = len(ops)
-    succ = [[] for _ in ops]
-    for o in ops:
-        for d in o["deps"] + o["soft"]:
-            succ[d].append(o["i"])
-    bl = [0.0] * n
-    for i in range(n - 1, -1, -1):
-        bl[i] = cv[i] + lat[i] + max([bl[s] + 60.0 for s in succ[i]] or [0.0])
-    left = [len(o["deps"] + o["soft"]) for o in ops]
-    done, ready, free, order, qof = [0.0] * n, {i: 0.0 for i in range(n) if left[i] == 0}, {}, [], [""] * n
-    while ready:
-        st, _, i, q = min((max(r, free.get(q, 0.0)), -bl[i], i, q) for i, r in ready.items() for q in ops[i]["qs"])
-        for j, r in ready.items():
-            if q in ops[j]["qs"] and max(r, free.get(q, 0.0)) <= st + 200.0 and (-bl[j], j) < (-bl[i], i):
-                i = j
-        st = max(ready.pop(i), free.get(q, 0.0))
-        qof[i] = q
-        free[q] = st + (cs[i] if q == "S" else cv[i])
-        done[i] = free[q] + lat[i]
-        order.append(i)
-        for s in succ[i]:
-            left[s] -= 1
-            if left[s] == 0:
-                ready[s] = max([done[d] + h for d, h in dl[s]] or [0.0])
-    return order, qof
-
-
-def improve(ops, order, qof, tabs, iters):
-    deps = [o["deps"] + o["soft"] for o in ops]
-    dset = [set(d) for d in deps]
-    flex = [len(o["qs"]) > 1 for o in ops]
-    res = [timeline(order, qof, tb) for tb in tabs]
-    norm = [max(r[0]) for r in res]
-    best = cur = 1.0 * len(tabs)
-    bo, bq, seed = list(order), list(qof), 12345
-    for it in range(iters):
-        seed = (seed * 1103515245 + 12345) % 2147483648
-        done, pred = res[it % len(tabs)]
-        i = done.index(max(done))
-        cand = []
-        while i >= 0:
-            j = pred[i]
-            if j >= 0 and j not in dset[i]:
-                cand.append(i)
-                if flex[j]:
-                    cand.append(-j - 1)
-            if flex[i]:
-                cand.append(-i - 1)
-            i = j
-        i = cand[(seed >> 8) % len(cand)]
-        nq, no = qof, order
-        if i < 0:
-            nq = list(qof)
-            nq[-i - 1] = "S" if qof[-i - 1] == "V" else "V"
-        else:
-            j = pred[i]
-            no = list(order)
-            a, b = no.index(j), no.index(i)
-            need, head, tail = {i}, [], []
-            for x in reversed(no[a:b + 1]):
-                if x in need:
-                    need.update(deps[x])
-                    head.append(x)
-                else:
-                    tail.append(x)
-            if j in need:
-                continue
-            no[a:b + 1] = head[::-1] + tail[::-1]
-        r2 = [timeline(no, nq, tb) for tb in tabs]
-        m = sum(max(r[0]) / z for r, z in zip(r2, norm))
-        temp = TEMP / norm[0] * (1.0 - it / iters) + 1e-7
-        if m <= cur or (seed >> 3) % 1000 < 1000.0 * 2.718281828 ** (-(m - cur) / temp):
-            order, qof, res, cur = no, nq, r2, m
-            if m < best:
-                best, bo, bq = m, list(no), list(nq)
-    return bo, bq, [max(timeline(bo, bq, tb)[0]) for tb in tabs]
-
-
-def improve(ops, order, qof, tabs, iters):
-    n = len(ops)
-    deps = [o["deps"] + o["soft"] for o in ops]
-    dset = [set(d) for d in deps]
-    flex = [len(o["qs"]) > 1 for o in ops]
-    kin, kin2 = {}, {}
-    for o in ops:
-        kin.setdefault(o["kind"], []).append(o["i"])
-        kin2.setdefault(o["kind"][0], []).append(o["i"])
-    same = [kin[o["kind"]] for o in ops]
-    same2 = [kin2[o["kind"][0]] for o in ops]
-    marks = [o["i"] for o in ops if o["cost"][0] == "r"]
-    rnd = [SEED]
-
-    def rand(m):
-        rnd[0] = (rnd[0] * 1103515245 + 12345) % 2147483648
-        return (rnd[0] >> 8) % m
-
-    def score(res):
-        return sum((max(r[0]) + SOFT * sum(r[0][x] for x in marks) / len(marks)) / z for r, z in zip(res, norm))
-    res = [timeline(order, qof, tb) for tb in tabs]
-    norm = [max(r[0]) for r in res]
-    best = cur = score(res)
-    bo, bq = list(order), list(qof)
-    for it in range(iters):
-        done, pred = res[it % len(tabs)]
-        cv, cs, lat, dl = tabs[it % len(tabs)]
-        i = done.index(max(done)) if rand(2) else marks[rand(len(marks))]
-        cand = []
-        while i >= 0:
-            j = pred[i]
-            if j >= 0 and j not in dset[i]:
-                cand.append(i)
-                if flex[j]:
-                    cand.append(-j - 1)
-            if flex[i]:
-                cand.append(-i - 1)
-            i = j
-        if not cand:
-            continue
-        i = cand[rand(len(cand))]
-        w = rand(6)
-        nq, no = qof, order
-        if i < 0:
-            i = -i - 1
-            nq = list(qof)
-            to = "S" if qof[i] == "V" else "V"
-            for x in (same[i] if w < 2 else [i]):
-                nq[x] = to
-        if nq is qof or rand(2):
-            key = [0.0] * n
-            z = 0.0
-            for x in order:
-                z += 0.001
-                key[x] = done[x] - lat[x] - (cs[x] if qof[x] == "S" else cv[x]) + z
-            j = pred[i]
-            if nq is not qof or j < 0:
-                a, dt = i, rand(1200) - 600.0
-            elif rand(2):
-                a, dt = i, key[j] - key[i] - 1.0 - (rand(600) if rand(3) == 0 else 0)
-            else:
-                a, dt = j, key[i] - key[j] + 1.0 + (rand(600) if rand(3) == 0 else 0)
-            for x in (same[a] if w < 2 else same2[a] if w == 2 else [a]):
-                key[x] += dt
-            if dt < 0:
-                for x in range(n - 1, -1, -1):
-                    kx = key[x] - 0.0001
-                    for d in deps[x]:
-                        if key[d] > kx:
-                            key[d] = kx
-            else:
-                for x in range(n):
-                    for d in deps[x]:
-                        if key[d] >= key[x]:
-                            key[x] = key[d] + 0.0001
-            no = sorted(range(n), key=lambda x: key[x])
-        r2 = [timeline(no, nq, tb) for tb in tabs]
-        m = score(r2)
-        temp = TEMP / norm[0] * (1.0 - it / iters) + 1e-7
-        if m <= cur or rand(1000) < 1000.0 * 2.718281828 ** (-(m - cur) / temp):
-            order, qof, res, cur = no, nq, r2, m
-            if m < best:
-                best, bo, bq = m, list(no), list(nq)
-    return bo, bq, [max(timeline(bo, bq, tb)[0]) for tb in tabs]
-
-
-PLAN = {}
 ABC = "0123456789ABCDEFGHIJKLMNOPQRSTUVWXYZabcdefghijklmnopqrstuvwxyz"
-ORDER = "0002040u060E0A0Q0C080G0I1W0k0Y0K0m1S0o0a1B0S1Y0q1C1E1M0i1o1H161J1U1O0s18110M0x150O0z0U131w0W1s1q1y1Q1u1K1a2G421c1g1e27202Y283u2a4M22253m3t2Q2I2K2c2k3p2S2i2A2e2C2E2m2M3q2g2U2O4K1i2W4W4O2o4C2q2u3w2w2s4E2z4Q304G4432460e344I36484U4S4Y383y3A0c4A403C3I1k4a3H5o4g4i4c4e3F3K4m4l4o3M5Z4q3O4s3Q1m4u3S4w7a5f3U4y52573W3Y543a3d513e3k3g5c3i5b585A5C7K5E7R5y5q5G5s5I660g5u5K6A6I606G625M5g6C5w686K5P645i6E5k6M5m7P6O5Q6Q6S6U5S5W6Y6W5U6a7N6c6e6g6i7k6q6k6p7c827w9M7s6m6t7S7e7u7m847g6u6w7y7o6y707U9980727i86747W767Y7q9C78887B8A8E9B7C8G8C7E8K8I7G977I8M8O8Q8S9W8U8d8a8W9o9i9OB89e9E9Q8e8Z9g9Y9k9a8g8i9q9S8k8m9G9cAt8o9U9m8q9s9I8s9KAw8u9u8x9wA0Az8yA29y9490A692A5A8AvAAACAEAGBIARAKAIBUBABaCuBQAOANB0BCBKBSB2BMASBcAUBEAWBWAYCjAaBYB4AcBOAeBeBGCgB6AgBgAjBiBmCfAkBoBkAqAmBsAoBrBuClBwByC0C2D4CCC4C7DMDGCwEgDCC8CBD6CyCmDEDOD0CECGCoD8CIDICKD2ERCMDADQCODKCqCQCsEUCSDSCVDUDYEXCWDaDWCcCYDeCaDdDgETDiDkDmDoEqDzDqDwEiF8F2GWEyDsDvEkEYEsF0FAEuE0E2F4EmE4E6EaEwGNE8F6EoEAFCEcECEeGKEEFEEHFGFKGJFMEIFIEOEKFQEMFPFSGHFUFWFYFaGgFcFfFkGyGsGYISGoFgFjGaGOGqGiH0GcFmFoGuGkFqFsGQIDFuGmGeFwGwH2FyGSIIGUG0H4G3H6HAIFG4HCG6GAH8G8HEHGIHHIHKHMGDHOIuIUHQGEHdIcIkIWIwIoIKImIYIeIqIyIgIaIMIsHgIiIOJ0IQHjJ2J6J8J4JAJCHSHUJEHfJGJIJKJMHXHkJaJdHYHmHoHqJeJZHsJgJOHuHaJiHwJkJmHyJQJoI1JTJqI2I8JsJUI4JuJwI6JyK4K0K8K2KAJWIAK6"
-
-
-ORDER = "0400020u060Q080A0I0C0E1W0G0k0Y0K0m1S0a0o0S1B1Y1C0q1E1o0i1H161M1U1J1O0s18110M0x0O150U0z131w0W1s1q1y1Q1u1K1a2G421c1g1e2720282Y2a3u4M22252A3t3m2I2K2Q3p2S2k2i2c2C2e2m2M3q1i4K2U2g2O2E2W3w4C4W2o4O2q2u2w2s4E2z4Q304G4432460e344I48364U4S4Y383y3A4A0c403C4a4c1k4e5o4g4i3H3I4m3K3F4o4l3M4q3O4s3Q1m4u3S5f4w7a3U4y3W3Y5Z523a3d573e3k3g543i515c5b585A7K5C7R5E5q5G5s0g5I665u5K5y6I60685g626A6C6G5w5M6K5P5i646E5Q6M5k5S7P5m6O6S5U6U6Q5W6W6Y7N6a6c6e7k6g826i7c6p6m6k9M7w7e7S7s6q7m6t7u7y7g6u6w847o6y707U7i99728086747W7Y7q769C88787B8A8E9B7C8G8C7E8K978I7G7I8M8O8Q9O8S9o8UB89W8a8Z8W9i9Q8e8d9e9Y9E9g9q9a8g8i9k9S8k8m9G9cAt8o9U9m8q9s9I8s9KAw9u8u8x9wA0Az8yA29y9490A6A592AvA8AAACAEBIBaAGBUAKAIARBACuBSBCAOANBQBKB0BWBMASAUBcBEAWAYB2BYCjAaBOB4AcBGBeAeB6CgBgAgAjBiBmCfAkBoBkAqAmBsBrAoClBuBwByC0CwDMC2EgD4C4CBCCDGD6C8C7DEDCCmCyCoD0DOCECGD8CIDICKD2ERCMDADQCODKCqCQCsEUDSCSCVDUDYEXCWDaDWCcCYDeDdCaETDgDiDkDmEqF8DoEiDqDwDvGWF2EsDsDzEyEYEkF0FAEuE0E2EaEmE4F4E6EwGNE8EoF6EAFCEcECEeGKFEEEEHFGFKFMGJEIEOFIEKFQFPEMGHFSFUFWFYGYGyFaISGgFcFkFjGsGaFgFfGqGoGOGiGuGcFmFoGQGkFqH0FsGeIDFuGmGwFwH2GSFyGUIIH4G0G3H6HAIFG4HCG6GAH8G8IHHEHGHIHKGDIuHMIcGEHOIUHQHdIkIWIwIKIeIYIoIqImIyIgIaIMIsHgIiIOJ0IQHfJ2J6J8J4JAJCHSHjHUJEJGJIHXHkJKHYHmJMHoJaJZHqJeJdJOHsJgHaJiHuJkHwJmHyJQJoI1JTJqI2I8JUJsI4JuJwI6JyK4K0K8K2KAJWIAK6"
-
-
-ORDER = "0002040u060I080K0A0k0C0E0G0i0Q0S0Y0m0x0z0a111S0o131A151C0q1E0s0O171M190M1H0U1J1K1O2G1Y421Q0W1U1W1a1c1e1g1o1q1s1u1w1y25224M2Y2a3u2621281i3t2I2A2e2K2Q2k2M2S2i1k3o2U2C2c2O2E3r4K3m2g2W2m2o0c4C4W4E2q444G2s2u4O4Q464U48301m4I322w3w0e4S2z344Y4A363y4a40384c4g4i4e5o4l3A4m3C4o4q4s4u4w7a4y3F3G3K3J3O3M52553Q3S3U513W3Y3a5Z5A3c0g3e3k583g5f563i7L5a5E5C5G5d5I5K5M7R5q5O6A665s6C5y5u606I6G5Q626E685S5w5g6K5U5i645k6M5m7N6O6S6U6Q5W6W6Y7P6a6c6e7k6g7w6i826q6k6t7c7s6o6n7e7m7S707y7o6w7u6y847g6u80727q867U7i7W8874769M7Y8A788E977A8C7C7I8G7E9D8K987G8J8M9B8O8Q8S8U9o9W8Y8W8b9O9iB88c8f8g8i9e9Q9k8m9S9Y9q9E8k9a9m8o9g9U9s9c9G8q8s9u9IAx8u9K9w8w9y8yA0A290AtA6Au9294A5A8AzAAACAEBIAGAIAOARBUBaBAAMALAWAYBQBCBWAUBEBKBcASBMBYBSAaB0BeBGBOB2AcAeBgB4ClAgB6BiBmBoAiBkAkCuAqAmBrBsCgCjAoBuCfBwByC0DMC2D4C6C4C9CwDGCACDCGDCD6DICED8CyDOCKD0CICmDKCMDEEgCoD2DQDACOCQCqDSCsCSEVDUCUDWCWCcDYCYDaEXESDeCaDdDgERDiDkDmDoEqDuDqDtF2F8EiGWDwDzE2EyEkF4EYE0EmE6FAE4EsE8F0EaF6EuEoEcEAECFCEEEwFEEGGNEIEeFGEKEOFKFMFIEMGIFPFQGHFSFUGLFWFYFaGgFiFcFlISGyGYGsFeFhGoGiGuGaFqGcH0FsFmGkFoGOGwFuGqGeGQH2GmFwGSFyH4GUG0IJH6G2H8G4GAHAG6HCIEHGG8HFIDHIHKIHHMHOHQHSHdIcHeIoIuIUHjHgHmHkIkIeIqHoIgIWIwIKHqIYImIsHsIiIyIaIMHuHwJ0IOGDHyIQHUJ2I0J6HXJ8GEJ4I2HYJBI8I4JCI6JEJGJIJKJMJOJZJaJQJfJcJiJgJSJkHaJUJmIAJoJqJsJuJwJyK4K0K8K2KAJWK6"
-
-
-ORDER = "0400020u060Q0I081W0A0C0Y0E0G0k0K0m1S0a0S0o1B1Y0q1C0i1H1E1J1o160s1M1U111O0x18150M0z0O130U1w0W1s1q1y1Q1u1K1a2G421c1g1e20252Y4M22272a283u3m3t2I2K2A2k2Q2M2S2i2e2C2U2O2c3q3p4K2W2E1i2m2g2o4W4C2q4E2s444G4Q46302u2w320e4I2z4Y344O483w4U363y404S384A0c4a3A4c3C5o1k4e4g4i4m3H3K3I3F4o4l5f3M4q3O4s3Q5Z1m3S4u3U7a4w3W4y3Y523a3d573e3k3g0g51543i5b5c585A7R7K5C5E5q5G665s6I5y5u606C5g6A626K685w5I6G5i6E5K645k6M5m5M5P6O7N6Q5Q5W6S5S6Y5U6U6a6X6c7P6e6g7c6i9M7k826p6q6k7s7e6m6t7m7u7w7y7g7S6u6w847o6y707U8672997q7i80747W887Y76978A8E8C788G9D7A8I8K7C8M9B7I7E8O7G8Q9O8S9o9i8UB89W8e8W8d8a8Z9e9Q9q9Y9S9g8g9k8i9a8k8mAz9E9s8o9U9G9c9m8q9I9u9KAx8s9wA0A29y8uAt8wA4A68yA8Av9490AA92ACBUBIAEAGCuBABaAOAIANAKARBSBKBQBcBCBMASBWAUBEAWAYCjBeAaB0BGB2BYBOAcB4BgB6ChAeBiBmBkAgBoCfAiBqBsAkBuClAqAmBwAoByDMCwC0D4DGC2EgC4C7C8CCCBCyDCD0D6DICED8CGDOCICKERD2CMCmDKCoDADQCODECqDSCsETCQDUDYDaDWCSEXCUDcDeCWDgEVCcCYDiCaDkF2EqDmEiF8DoGWDwDqDvDsDzEsEyEuF0EkFAE0EmE2F4E4E6GNEwE8EYFCEaEoF6EAEcFEEeGJECFGFKFIEEFMGHEGFOFQEIFSGLEOEKFUEMFWGyGYFYGgGsFaISFkFcFfFgFjGoGiH0GaGkFmGuFoGcFqFsIJGmFuGqGeH2GOFwGwGQH4IHFyGSGUG0H6HAG2HCIDH8G4G6HGIFHEGAG8HIHKIUHMHOHQHgHdIkIWIwIcIYImIeIqIuIgIyIoIKIaIMIsHSGDIiIOJ0IQGEJ2HUJ4J6J8HXHfJAJCHYJEHjJGJIHkJKHmHoJMHqJeJdHaJaJZHsJOJgHuJiJkHwJmJQJoHyJTI1JqJUI2JsI8I4JuJxI6JyK4K0K8K2KAJWIAK6"
+ORDER = "0004021K060S1y080K0A0C1w0E0G0a0I1A0M1C1u0c0U1E1b1G1c181o1X1e1I211g2C1Z1q1j0O1l0Q1R1N2K1T2G1P1V2M2g1m2E2I224m2m1s240g2W2R2O342T362c0W562a2V2Y4U4Z4W4R2o0i3G2q2w2y2s3M3I3E3A302e3O4S544P4c3K380Y320e3C2u4a2i2k3Q4w5M4y4o503S4q5G4s3a3U3W3c5E0m3Z0o5O5K3e5A58525I4u3g5C4g4e3i4i5Q4k3k5S5U5W3q0k5a3v3y2A3t3w3m5Z280s5c26403o425e445g460q6k485i6R4A8i5k6P4C5q5m4E4H5v6S4I4K5s5p6e4M0y6M6L5w5y6U106X608O8J6264726m7K0u6o7C6q7E6u6w7I6Y6y66740w786s7G8T687M6a7A768R707O6A6g6D6i8V7Q7S8N6E7U6G7Y168L6c6I8c7a7W7c7e9G948s7g8k9A7iAg7p7k7q90128m928W8u7m7t14968o9I7u7w8w9C7yAH808q829K8Y9E8y9884AL8e9M8g86AJ9O9Q8a889S8A9W9UAN8C9Y8EAP9aAS8GAa9cAQ9e9gAi9m9pB8B29iAqBE9q9lAyAkB4AsBGAU9sAu9uBAAm9w9yBICFA0B0AwAWBCB6AoA2CeAcBKAeAYCLA4BMBOCJA6BQA8BUCMBTAABWCHACBYCOAEBaCRBcD0CgBeCYBiBlD6BgDCEcCoBmBpCwCiD8CqCkCSBqDEBsCsBuD2BwEPCUDAByEJCyCuEKDGCmC0EDD4CaCcDIC2DKDMEFC4DOC6CWDSDQC8DUEHCADWEMCCEWDYEeEyDaF4FADcEmDiDhDeGaDmDlEQEuEgESF6EoDoEqDqFCDsEiDuF0EsDwGHFEF8GKEwEkDyGFF2EYEaFGE0GJFIFKGBE2EUFME4FQFOE6FSGDE8FUEAFWGMFYFaGwGUGcFeFhFcH2GkH8FiFlGsGeH4GmGgHAGuFmFoGoFqGyFsIBH6FuGOHCGQGiH0GqFwIYI9GWHEGYGSFyHGHIG0HKG2HNHOIKIDG4HQG6HSIFIGG8ISHUIIHWHYIaHhHiJ0IuHaIiJ6HeHdIqIcJ2IkHkImIwHmJ8IeHoHqIMKLHsJAIOIyIoIgHuJ4IsKoKPIUIWHwJCHyKTI0JGKRJEI2JIKNI4JMJKIQJOI6KiKUKXJQJSKqKyJUJmJjL6KsLOKYL0KuLGLILMLAL8LQL2KwLCJlJWLKKaL4LELSKkKmJYKcJpLULWJaLYJcLaLcKfJeLeJqJsKgLgJuLiJwLkLmM3M0JgM4LzJyLoM6K0M8MAK2MCK4LqMEK6MGLsK8KEMIKHLuKAMKMMKCMOMUMQMXMSMaLwKIMY"
+PLAN = {}
 
 
 def rank_program(g, core, T, topo):
@@ -603,22 +411,20 @@ def rank_program(g, core, T, topo):
         return
     ops = make_ops(g, T, topo, core, rank)
     depend(ops)
-    if "order" not in PLAN:
-        PLAN["ops"] = ops
-        code = [ABC.index(ORDER[x]) * 62 + ABC.index(ORDER[x + 1]) for x in range(0, len(ORDER), 2)] or range(0, 2 * len(ops), 2)
-        PLAN["order"] = [x // 2 for x in code]
-        PLAN["q"] = [""] * len(ops)
-        for x in code:
-            PLAN["q"][x // 2] = ops[x // 2]["qs"][x % 2]
+    code = [ABC.index(ORDER[x]) * 62 + ABC.index(ORDER[x + 1]) for x in range(0, len(ORDER), 2)] or range(0, 2 * len(ops), 2)
+    order, qof = [x // 2 for x in code], [""] * len(ops)
+    for x in code:
+        qof[x // 2] = ops[x // 2]["qs"][x % 2]
+    PLAN.update(ops=ops, order=order, q=qof)
     eng = {"V": g.vector, "S": g.scalar, "P": g.tensor, "G": g, "Y": g.sync}
     known = {q: {} for q in eng}
     count = {"V": 0, "S": 0, "P": 0, "G": 0}
     snap, token, stores, lsem = {}, {}, 0, 0
-    for i in PLAN["order"]:
-        o, q = ops[i], PLAN["q"][i]
+    for i in order:
+        o, q = ops[i], qof[i]
         kn, toks = known[q], []
         for d in o["deps"]:
-            if not (PLAN["q"][d] == "P" and q == "P"):
+            if not (qof[d] == "P" and q == "P"):
                 toks += token[d]
         for s, v in sorted(toks, key=lambda x: (-x[1], x[0])):
             if kn.get(s, 0) < v:

from concourse.bass import DstId, RemoteDMATransfer
from concourse.mybir import AluOpType, ActivationFunctionType

STEPS, CH, NL = 5, 2, 128
KP = [32, 32, 24, 16, 8, 8, 8]
EP = [32, 32, 32, 32]
NS = [4, 3]
ALIAS = 3
MAGIC = 12582912.0

SCRATCH = {"thr": ("sbuf", [1, 128], "float32"), "thh": ("sbuf", [1, 128], "float16"), "wr": ("sbuf", [1, 128], "bfloat16"),
           "g2w": ("sbuf", [1, 128], "bfloat16"), "cb": ("sbuf", [1, 8], "bfloat16"), "cx": ("sbuf", [1, 128], "bfloat16")}


def _declare(where, dtype, names, cols, per_chunk=False):
    for nm in names.split():
        for x in (range(CH) if per_chunk else [""]):
            SCRATCH["%s%s" % (nm, x)] = (where, [128, cols], dtype)


_declare("sbuf", "bfloat16", "keyt", 8224)
_declare("sbuf", "bfloat16", "emt", 8208)
_declare("sbuf", "int32", "clt", 2056)
_declare("sbuf", "int32", "plt", 256)
_declare("sbuf", "float32", "sf lf", 256)
_declare("sbuf", "float32", "ytb", 512)
_declare("sbuf", "float32", "kcf", 1)
_declare("sbuf", "int32", "kci kcj", 1)
_declare("sbuf", "bfloat16", "embt", 16)
_declare("sbuf", "float16", "embs", 16)
_declare("sbuf", "bfloat16", "lq", 1536)
_declare("sbuf", "float16", "lp sp", 1280)
_declare("sbuf", "uint16", "lu su", 1280)
_declare("sbuf", "bfloat16", "sq", 1280)
_declare("sbuf", "bfloat16", "ones idm bma bm nid hid kid aid nq", 128)
_declare("sbuf", "bfloat16", "sr", 256)
_declare("sbuf", "bfloat16", "gw g2 gn", 8)
_declare("sbuf", "bfloat16", "kv", 32)
_declare("sbuf", "bfloat16", "ga gb r0 r1", 64)
_declare("sbuf", "float32", "z8", 64)
_declare("sbuf", "float32", "zf zb", 128)
_declare("sbuf", "float16", "ebk", 128)
_declare("sbuf", "bfloat16", "c2k fa", 1024)
_declare("psum", "float32", "x0 x1 xr tk", 512)
_declare("psum", "float32", "D B", 512, True)
_declare("sbuf", "bfloat16", "kg", 4096, True)
_declare("sbuf", "bfloat16", "ab eg", 2048, True)
_declare("sbuf", "float16", "qx", 8, True)
_declare("sbuf", "uint16", "ls", 8, True)
_declare("sbuf", "bfloat16", "sg", 256, True)
_declare("sbuf", "float16", "sc", 256, True)
_declare("sbuf", "float32", "s2", 64, True)
_declare("sbuf", "bfloat16", "yy oh on fl", 128, True)
_declare("sbuf", "float32", "y4 g1 fm bs", 128, True)

SEMAPHORES = ["V", "S", "P", "G", "lsem", "ld_pl", "ld_p1", "ld_q", "ld_key", "ld_th", "ld_w", "ld_emb", "ld_cl", "ld_em", "st"]
for _t in range(STEPS):
    for _c in range(CH):
        SEMAPHORES += ["ap%d%d" % (_t, _c), "aq%d%d" % (_t, _c)]


def make_ops(g, T, topo, core, rank):
    A, F = AluOpType, ActivationFunctionType
    V, S, P = g.vector, g.scalar, g.tensor
    ops, groups = [], {}

    def op(name, qs, fn, rd, wr, banks=(), cost=None, sem=None):
        ops.append(dict(name=name, qs=qs, fn=fn, rd=list(rd), wr=list(wr), banks=list(banks), cost=cost, sem=sem, i=len(ops)))

    def vop(name, fn, rd, wr, n, banks=()):
        op(name, "V", lambda q: [fn()], rd, wr, banks, ("c", n, n))

    def vs(name, out, src, scale, bias, rd, wr, n, banks=()):
        def emit(q):
            if q == "V":
                return [V.tensor_scalar(out, src, scale, bias, A.mult, A.add)]
            return [S.activation(out, src, F.Identity, bias, scale) if bias else S.activation(out, src, F.Copy, 0.0, scale)]
        op(name, "VS", emit, rd, wr, banks, ("c", n, n))

    def mm(name, grp, mms, rd, wr, banks):
        st = groups.setdefault(grp, [0, 0])
        st[0] += len(mms)

        def emit(q):
            r = []
            for m in mms:
                st[1] += 1
                r.append(P.matmul(m[0], m[1], m[2], st[1] == 1, st[1] == st[0]))
            return r
        op(name, "P", emit, rd, wr, banks, ("p", sum(m[3] for m in mms)))

    def gop(name, fn, rd, wr, n):
        op(name, "G", lambda q: [fn()], rd, wr, (), ("g", n))

    def dma(name, q, pairs, rd, wr, sem, nbytes):
        eng = g.sync if q == "Y" else g.scalar
        op(name, q, lambda _q: [eng.dma_start(o, i) for o, i in pairs], rd, wr, (), ("d", nbytes, len(pairs)), sem)

    def copy(out, src, n):
        return g.affine_select(out, src, [[0, n]], A.is_ge, 0.0, 0, 0)

    first = rank == 0
    last_rank = rank == len(T.cores) - 1
    k0 = 15 if first else 16

    vop("kz", lambda: V.memset(T.keyt[:, 0:16], 0.0), [], ["kz"], 16)
    dma("ld_pl", "Y", [(T.plt[:, 0:128], T.pl[:, 0:128])], [], ["plt0", "o1"], "ld_pl", 65536)
    dma("ld_th", "S", [(T.thr[:], T.th[:])], [], ["thr", "o2"], "ld_th", 8192)
    dma("ld_w", "S", [(T.wr[:], T.w[:])], ["+o2"], ["wr", "o3"], "ld_w", 8192)
    dma("ld_key", "Y", [(T.keyt[:, k0:k0 + 4096], T.key[:])], ["kz", "+o1", "+o3"], ["keyt", "o4"], "ld_key", 1048576)
    dma("ld_p1", "Y", [(T.plt[:, 128:256], T.pl[:, 128:256])], ["+o4"], ["plt1", "o5"], "ld_p1", 65536)
    dma("ld_q", "Y", [(T.lq[:, 0:256], T.q[:])], ["+o5"], ["lq00", "lq01", "o6"], "ld_q", 65536)
    dma("ld_cl", "Y", [(T.clt[:, 0:2048], T.cl[:])], ["+o6"], ["clt0", "o7"], "ld_cl", 1048576)
    dma("ld_em", "Y", [(T.emt[:, 0:4096], T.em[:])], ["+o7"], ["emt", "o8"], "ld_em", 1048576)
    dma("ld_emb", "Y", [(T.embt[:], T.emb[:])], ["+o8"], ["embt"], "ld_emb", 65536)

    vop("ones", lambda: V.memset(T.ones[:], 1.0), [], ["ones"], 64)
    vop("c2k", lambda: V.memset(T.c2k[:], 2048.0), [], ["c2k"], 512)
    for c in range(CH):
        a, b = c * NL, c * NL + NL
        vop("u0_%d" % c, lambda a=a, b=b: V.tensor_scalar(T.lu[:, a:b], T.plt[:, a:b], 15.0 if first else 0.0, None, A.add),
            ["plt%d" % c], ["lu0%d" % c], 128)
        vop("p0_%d" % c, lambda a=a, b=b: V.tensor_scalar(T.lp[:, a:b], T.plt[:, a:b], -2048.0, None, A.add), ["plt%d" % c],
            ["lp0%d" % c], 128)
        vop("sga%d" % c, lambda c=c: V.memset(T["sg%d" % c][:], 1.0), [], ["sg%d" % c], 128)
        vop("sgb%d" % c, lambda c=c: V.memset(T["sg%d" % c][:, 31::32], 0.0), [], ["sg%d" % c], 8)
    for j in range(4):
        a = k0 + 1024 * j
        gop("ky2_%d" % j, lambda a=a: copy(T.keyt[:, a + 4096:a + 5120], T.keyt[:, a:a + 1024], 1024), ["keyt"],
            ["ky2_%d" % j], 1024)
    vop("kal", lambda: V.tensor_copy(T.keyt[:, k0 + 8192:k0 + 8193], T.keyt[:, k0:k0 + 1]), ["keyt"], ["kal"], 1)
    vop("cal", lambda: V.tensor_copy(T.clt[:, 2048:2049], T.clt[:, 0:1]), ["clt0"], ["clt"], 1)
    for j in range(8):
        a = 512 * j
        gop("em2_%d" % j, lambda a=a: copy(T.emt[:, a + 4096:a + 4608], T.emt[:, a:a + 512], 512), ["emt"], ["em2_%d" % j], 512)
    vop("eal", lambda: V.tensor_copy(T.emt[:, 8192:8193], T.emt[:, 0:1]), ["emt"], ["eal"], 1)

    def sel(name, src, n, pattern, cmp, base, cm):
        gop(name, lambda: g.affine_select(T[name][:], T[src][:, 0:n], pattern, cmp, 0.0, base, cm), [src], [name], n)
    sel("idm", "ones", 128, [[-1, 128]], A.is_equal, 0, 1)
    sel("bma", "ones", 128, [[-16, 8], [0, 16]], A.is_ge, 0, 1)
    sel("bm", "bma", 128, [[16, 8], [0, 16]], A.is_ge, 15, -1)
    sel("ga", "ones", 64, [[0, 8], [-16, 8]], A.is_ge, 0, 1)
    sel("gb", "ga", 64, [[0, 8], [16, 8]], A.is_ge, 15, -1)
    sel("fa", "c2k", 1024, [[-16, 8], [0, 8], [-1, 16]], A.is_equal, 0, 1)
    gop("kci", lambda: g.iota(T.kci[:], [[0, 1]], 0, 1), [], ["kci"], 1)
    g8 = T.gb[:, 0:8]

    def scaled(name, src, k, n):
        vs(name, T[name][:], T[src][:, 0:n], float(k), 0.0, [src], [name], n // 2)
    scaled("nid", "idm", -1.0, 128)
    scaled("hid", "idm", 0.5, 128)
    vs("sid", T.sr[:, 0::2], T.idm[:], 1.0 / 4096.0, 0.0, ["idm"], ["sid"], 64)
    vs("si1", T.sr[:, 1::2], T.idm[:], -1.0 / 4096.0, 0.0, ["idm"], ["si1"], 64)
    scaled("kid", "idm", -4096.0, 128)
    scaled("g2", "gb", 2.0, 8)
    scaled("gn", "gb", -1.0, 8)
    scaled("nq", "bm", -1.0, 128)
    for b in range(2):
        vop("nq%d" % b, lambda b=b: V.memset(T.nq[:, b::4], 0.0), [], ["nq"], 16)
        for j in range(NS[b], 4):
            vop("nq%d%d" % (b, j), lambda s=4 * j + b: V.tensor_scalar(T.nq[:, s::16], g8, -1.0, None, A.mult), ["gb"], ["nq"], 8)
    vs("r0", T.r0[:], T.gb[:], -256.015625, 256.0, ["gb"], ["r0"], 32)
    vs("r1", T.r1[:], T.gb[:], -255.984375 if first else -256.015625, 256.0, ["gb"], ["r1"], 32)
    vop("thh", lambda: V.tensor_scalar(T.thh[:], T.thr[:], -1.0, 2048.0, A.mult, A.add), ["thr"], ["thh"], 128)
    mm("gwp", "gwp", [(T.tk[:, 0:8], T.wr[:], T.c2k[0:1, 0:8], 64)], ["wr", "c2k"], ["gwp"], ["btk"])
    vop("gw1", lambda: V.tensor_tensor(T.gw[:], T.tk[:, 0:8], g8, A.mult), ["gwp", "gb"], ["gw"], 8, ["btk"])
    vop("gw", lambda: V.tensor_scalar(T.gw[:], T.gw[:], 1.0 / 4194304.0, None, A.mult), ["gw"], ["gw"], 8)
    vop("cb", lambda: V.memset(T.cb[:], -0.5), [], ["cb"], 8)
    vop("cx", lambda: V.memset(T.cx[:], 1.0 if first else 0.0), [], ["cx"], 64)
    vop("g2w", lambda: V.memset(T.g2w[:], 3.0), [], ["g2w"], 64)
    scaled("aid", "idm", -12288.0, 128)
    vop("kcj", lambda: V.tensor_scalar(T.kcj[:], T.kci[:], 15, None, A.bitwise_and), ["kci"], ["kcj"], 1)
    vop("kcf", lambda: V.tensor_copy(T.kcf[:], T.kcj[:]), ["kcj"], ["kcf"], 1)
    vop("kv0", lambda: V.memset(T.kv[:, 8:32], 0.0), [], ["kv0"], 16)
    vop("kv", lambda: V.tensor_scalar(T.kv[:, 0:8], g8, T.kcf[:], None, A.mult), ["gb", "kcf"], ["kv"], 8)
    vop("embs", lambda: V.tensor_scalar(T.embs[:], T.embt[:], 0.5, -0.25, A.mult, A.add), ["embt"], ["embs"], 16)
    vop("z8", lambda: V.memset(T.z8[:], 0.0), [], ["z8"], 64)
    vop("z8b", lambda: V.memset(T.z8[:, 0::8], 16384.0), [], ["z8"], 8)
    vop("zf", lambda: V.memset(T.zf[:], 0.0625), [], ["zf"], 128)
    vop("zf1", lambda: V.memset(T.zf[:, 0::16], -16384.0), [], ["zf"], 8)
    vop("zb", lambda: V.memset(T.zb[:], -0.0625), [], ["zb"], 128)
    vop("zb1", lambda: V.memset(T.zb[:, 0::16], -16384.0), [], ["zb"], 8)

    nxt = T.cores[(rank + 1) % len(T.cores)]
    rid, pid = topo.addr(nxt)[0], topo.addr(nxt)[1]
    eng = topo.engines(core, nxt)
    m_all, m_a, m_b = sum(1 << e for e in eng), sum(1 << e for e in eng[0::2]), sum(1 << e for e in eng[1::2])
    win_c = T.clt[:, 0:2049]
    X = [T.x0, T.x1]

    def gather(name, dst, win, lst, rd, wr, n):
        def emit(q):
            if q == "V":
                return [V.tensor_copy(dst, win.indirect(lst))]
            return [S.activation(dst, win.indirect(lst), F.Copy)]
        op(name, "VS", emit, rd, wr, (), ("i", n))

    def step(t, c):
        n, nn = "%d%d" % (t, c), "%d%d" % (t + 1, c)
        o = t * 256 + c * NL
        here, dst = slice(o, o + NL), slice(o + 256, o + 256 + NL)
        p, q = T.lp[:, here], T.lq[:, here]
        Db, Bb = T["D%d" % c], T["B%d" % c]
        bD, bB = "bD%d" % c, "bB%d" % c
        kg, ab, qx, ls, sg, sc, s2, yy, y4, oh, on, fl, g1, eg, fm, bs = (T[x + str(c)] for x in (
            "kg ab qx ls sg sc s2 yy y4 oh on fl g1 eg fm bs".split()))
        last = t == STEPS - 1
        alias = 2 * t + c >= ALIAS

        def k(x):
            return "%s%d" % (x, c)
        if t == 0:
            win_k, kw = (T.keyt[:, 0:4111] if first else T.keyt[:, 16:4112]), ["keyt"]
            win_e, ew = T.emt[:, 0:4096], ["emt"]
        else:
            win_k, kw = T.keyt[:, 16:k0 + 4097], ["ky2_0"]
            if 2 * t - 2 + c >= ALIAS:
                win_k, kw = T.keyt[:, 16:k0 + 8193], ["kal"] + ["ky2_%d" % j for j in range(4)]
            win_e, ew = T.emt[:, 0:4097], ["em2_0"]
            if alias:
                win_e, ew = T.emt[:, 0:8193], ["eal"] + ["em2_%d" % j for j in range(8)]
        ko = (t % 2) * 2048
        kr, a = [], 0
        for j, w in enumerate(KP):
            kr.append("kg%d%d_%d" % (c, t % 2, j))
            gather("kg%s_%d" % (n, j), kg[:, ko + 16 * a:ko + 16 * (a + w)], win_k, T.lu[:, o + a:o + a + w],
                   kw + ["lu" + n], [kr[j]], 16 * w)
            a += w
        hcol = Bb[:, 31:256:32]
        hq = T.tk[:, 256 + 8 * c:264 + 8 * c]
        mm("h" + n, "H" + n, [(hq, T.ones[0:1, :], T.cb[:], 64), (hq, q, T.gw[:], 64)], ["lq" + n, "gw", "ones", "cb"],
           [k("H")], ["btk"])
        vop("qx" + n, lambda: V.tensor_scalar(qx[:], hq, MAGIC, -MAGIC, A.add, A.add), [k("H")], [k("qx")], 8, ["btk"])
        if t:
            mm("tk" + n, "T" + n, [(T.tk[32 * t - 32:32 * t, c * NL:c * NL + NL], T.kv[:], on[:], 128)], [k("on"), "kv", "kv0"],
               ["tk" + n], ["btk"])
        if last and c == CH - 1:
            vs("yta", T.ytb[:, 0:256], T.tk[:, 0:256], 1.0, 0.0, ["tk%d%d" % (x, y) for x in range(1, 5) for y in range(CH)],
               ["yta"], 256, ["btk"])
            dma("sta", "Y", [(T.yt[:, 256 * x:256 * x + 256], T.ytb[32 * x:32 * x + 8, 0:256]) for x in range(4)], ["yta"],
                ["ytad"], "st", 32768)
        mm("bc" + n, "B" + n, [(Bb[:, 0:256], p, T.sr[:], 256), (hcol, T.ones[0:1, :], T.cb[:], 64)],
           ["lp" + n, "ones", "cb", "sid", "si1"], [k("B")], [bB])
        mm("bq" + n, "B" + n, [(hcol, q, T.gw[:], 64), (hcol, T.nid[:], qx[:], 64)], ["lq" + n, "gw", k("qx"), "nid"], [k("B")],
           [bB])
        f = Bb[:, 384:448]
        mm("fe" + n, "F" + n, [(f, T.bm[:], T.r0[:] if t == 0 else T.r1[:], 64)], [k("B"), "bm", "r0", "r1"], [k("F")], [bB])
        d = Db[:, 0:128]
        mm("dt" + n, "D" + n, [(d, T.ones[0:1, :], T.thh[:], 128)], ["ones", "thh"], [k("d")], [bD])
        parts = []

        def dpart(name, mms, rd):
            parts.append(k("d") + name)
            mm(name + n, "D" + n, mms, rd + [k("d")], [parts[-1]], [bD])
        for b in range(2):
            mm("xk%s_%d" % (n, b), "x%s%d" % (n, b), [(X[b][:, 128 * j:128 * j + 128], T.idm[:],
               kg[:, ko + 4 * j + b:ko + 2048:16], 128) for j in range(NS[b])], kr + ["idm"], ["x%d" % b], ["bx%d" % b])
            mm("xq%s_%d" % (n, b), "x%s%d" % (n, b), [(X[b][:, 128 * j:128 * j + 128], T.nid[:], q, 128) for j in range(NS[b])],
               ["lq" + n, "nid"], ["x%d" % b], ["bx%d" % b])
            op("ab%s_%d" % (n, b), "S", lambda _q, b=b: [S.activation(ab[:, 512 * b:512 * b + 128 * NS[b]],
                                                                      X[b][:, 0:128 * NS[b]], F.Abs)],
               ["x%d" % b], ["ab%d_%d" % (c, b)], ["bx%d" % b], ("c", 128 * NS[b], 128 * NS[b]))
            dpart("da%d_" % b, [(Db[:, 4 * j + b:128:16], ab[:, 512 * b + 128 * j:512 * b + 128 * j + 128], g8, 64)
                                for j in range(NS[b])], ["ab%d_%d" % (c, b), "gb"])
        mm("xr" + n, "xr" + n, [(T.xr[:, j::4], T.idm[:], q, 128) for j in range(4)], ["lq" + n, "idm"], ["xr"], ["bxr"])
        dpart("dq", [(d, q, T.nq[:], 128)], ["lq" + n, "nq"])
        for b in range(2):
            for j in range(NS[b], 4):
                s, w = 4 * j + b, 512 * b + 128 * j
                dpart("dk%d%d_" % (b, j), [(Db[:, s:128:16], kg[:, ko + s:ko + 2048:16], T.gn[:], 64)], kr + ["gn"])
                vop("my%d%d_%s" % (b, j, n), lambda s=s, w=w: V.tensor_tensor(ab[:, w:w + 128], kg[:, ko + s:ko + 2048:16],
                                                                              T.xr[:, 0::4], A.max), kr + ["xr"],
                    ["ab%d_%d%d" % (c, b, j)], 128, ["bxr"])
                dpart("dm%d%d_" % (b, j), [(Db[:, s:128:16], ab[:, w:w + 128], T.g2[:], 64)], ["ab%d_%d%d" % (c, b, j), "g2"])
        for b in range(2, 4):
            dpart("dk%d_" % b, [(Db[:, 4 * j + b:128:16], kg[:, ko + 4 * j + b:ko + 2048:16], T.gn[:], 64) for j in range(4)],
                  kr + ["gn"])
            vop("mx%s_%d" % (n, b), lambda b=b: V.tensor_tensor(ab[:, 512 * b:512 * b + 512], kg[:, ko + b:ko + 2048:4], T.xr[:],
                                                                A.max), kr + ["xr"], ["ab%d_%d" % (c, b)], 512, ["bxr"])
            dpart("dm%d_" % b, [(Db[:, 4 * j + b:128:16], ab[:, 512 * b + j:512 * b + 512:4], T.g2[:], 64) for j in range(4)],
                  ["ab%d_%d" % (c, b), "g2"])
        far = sg[:, 0:256:2]
        vop("sg" + n, lambda: V.tensor_scalar(far, d, 2047.5, None, A.is_ge), parts, [k("sg"), k("d")], 128, [bD])
        vop("sc" + n, lambda: V.tensor_tensor_scan(sc[:, ::-1], sg[:, ::-1], Bb[:, 255::-1], 0.0, A.mult, A.add),
            [k("B"), k("sg")], [k("sc")], 256, [bB])
        x, xn = Db[:, 256:384], Db[:, 128:256]
        if alias:
            mm("nn" + n, "N" + n, [(xn, T.idm[:], p, 128), (xn, far, T.aid[:], 128)], [k("sg"), "lp" + n, "idm", "aid"], [k("N")],
               [bD])
            mm("xx" + n, "X" + n, [(x, T.c2k[0:1, 0:128], T.g2w[:], 128), (x, far, T.kid[:], 128)],
               [k("sg"), k("N"), "c2k", "g2w", "kid"], [k("X")], [bD])
            vs("yy" + n, y4[:], xn, 1.0, 6145.0 if first else 6144.0, [k("N")], [k("yy")], 128, [bD])
        else:
            mm("nn" + n, "N" + n, [(xn, far, T.idm[:], 128)], [k("sg"), "idm"], [k("N")], [bD])
            mm("xx" + n, "X" + n, [(x, T.idm[:], p, 128)] + ([(x, T.ones[0:1, :], T.cx[:], 128)] if t else [])
               + [(x, far, T.kid[:], 128)], [k("sg"), k("N"), "lp" + n, "idm", "ones", "cx", "kid"], [k("X")], [bD])
            vs("yy" + n, yy[:], xn, 6144.0, -8192.0, [k("N")], [k("yy")], 128, [bD])
        mm("fo" + n, "F" + n, [(Bb[:, 384 + 8 * j:392 + 8 * j], T.fa[:, 128 * j:128 * j + 128], sc[:, 0::32], 64)
                               for j in range(8)], [k("sc"), "bm", "r0", "r1", "fa"], [k("F")], [bB])
        vop("s2" + n, lambda: V.tensor_tensor_scan(s2[:], T.z8[:], f, 0.0, A.add, A.min), [k("F"), "z8"], [k("s2")], 64, [bB])
        vop("ls" + n, lambda: V.tensor_scalar(ls[:], s2[:, 7::8], MAGIC + 1024.0, -MAGIC, A.add, A.add), [k("s2")], [k("ls")], 8)
        sp, su = T.sp[:, here], T.su[:, here]
        op("g1" + n, "V", lambda _q: [V.tensor_tensor(g1[:], win_c.indirect(ls[:]), y4[:] if alias else yy[:],
                                                      A.max if alias else A.add)], ["clt", k("ls"), k("yy")], [k("g1")], (),
           ("i", 128))
        if alias:
            vop("ua" + n, lambda: V.tensor_copy(su, g1[:]), [k("g1")], ["su" + n], 128)
            vop("pn" + n, lambda: V.tensor_tensor(sp, g1[:], x, A.subtract), [k("g1"), k("X")], ["sp" + n], 128, [bD])
        else:
            vop("pn" + n, lambda: V.tensor_tensor(sp, g1[:], x, A.max), [k("g1"), k("X")], ["sp" + n], 128, [bD])
            vop("un" + n, lambda: V.tensor_scalar(su, sp, 2048.0, None, A.add), ["sp" + n], ["su" + n], 64)
        r = slice(c * NL, c * NL + NL)
        if t == 0 and c == 0:
            mm("ebp", "ebp", [(T.D0[:, 384 + 16 * j:400 + 16 * j], T.idm[:], T.embs[:], 64) for j in range(8)], ["idm", "embs"],
               ["ebp"], ["bD0"])
            vop("ebk", lambda: V.tensor_tensor(T.ebk[:], T.D0[:, 384:512], T.bm[:], A.mult), ["ebp", "bm"], ["ebk"], 128, ["bD0"])
        if last:
            dl = 1.0 if last_rank else 0.0
            vop(k("fl"), lambda: V.tensor_scalar(fl[:], sp, 2048.0 - dl, None, A.is_ge), ["sp" + n], [k("fl")], 64)
            mm(k("zz"), k("Z"), [(Db[:, 384:512], T.idm[:], sp, 128), (Db[:, 384:512], T.kid[:], fl[:], 128)],
               ["sp" + n, k("fl"), "idm", "kid"], [k("Z")], [bD])
            vs(k("sf"), T.sf[:, r], Db[:, 384:512], 1.0, 2048.0 + dl, [k("Z")], [k("sf")], 128, [bD])

        def send_p(_q):
            if last:
                g.remote_dma(T.lf[:, r], T.sf[:, r], T.sem["ap" + n], T.sem.lsem, pid, rid, m_all)
                return None
            g.remote_dma_fused([RemoteDMATransfer(dst_ids=[DstId(rid=rid, pnc=pid)], dma_engine_mask=m,
                                                  remote_sem=T.sem["ap" + n], src=s, dst=d)
                                for m, s, d in ((m_a, su, T.lu[:, dst]), (m_b, sp, T.lp[:, dst]))], local_sem=T.sem.lsem)
            return None
        op("sendp" + n, "G", send_p, [k("sf")] if last else ["su" + n, "sp" + n],
           [k("lf")] if last else ["lu" + nn, "lp" + nn], (), ("r", 1), "ap" + n)
        if last:
            dma("stp%d" % c, "Y", [(T.yp[:, r], T.lf[:, r])], [k("lf")], ["yp%d" % c], "st", 65536)
        er, a = [], 0
        for j, w in enumerate(EP):
            er.append("eg%d_%d" % (c, j))
            gather("eg%s_%d" % (n, j), eg[:, 16 * a:16 * (a + w)], win_e, T.su[:, o + a:o + a + w], ew + ["su" + n], [er[j]],
                   16 * w)
            a += w
        u = Bb[:, 256:384]
        for j in range(4):
            mm("v%d" % j + n, "U" + n, [(u, eg[:, s::16], T.idm[:], 128) for s in range(4 * j, 4 * j + 4)], er + ["idm"],
               [k("U")], [bB])
        vop("fm" + n, lambda: V.tensor_tensor_scan(fm[:], T.zf[:], u, 0.0, A.add, A.max), [k("U"), "zf"], [k("fm")], 128, [bB])
        vop("bw" + n, lambda: V.tensor_tensor_scan(bs[:, ::-1], T.zb[:], fm[:, ::-1], 0.0, A.add, A.max),
            [k("fm"), "zb"], [k("bs")], 128)
        vop("oh" + n, lambda: V.tensor_tensor(oh[:], u, bs[:], A.is_equal), [k("U"), k("bs")], [k("oh")], 128, [bB])
        mm("op" + n, "O" + n, [(u, oh[:], T.idm[:], 128)], [k("oh"), "idm"], [k("U")], [bB])
        vs("on" + n, on[:], u, 1.0, 0.0, [k("U")], [k("on")], 128, [bB])
        e = Bb[:, 384:512]
        mm("e" + n, "E" + n, [(e, T.hid[:], q, 128), (e, T.ebk[:], on[:], 128)], ["lq" + n, k("on"), "hid", "ebk"], [k("F")], [bB])
        sq = T.sq[:, here]
        vop("qn" + n, lambda: V.tensor_scalar(sq, e, MAGIC, -MAGIC, A.add, A.add), [k("F")], ["sq" + n], 128, [bB])

        def send_q(_q):
            g.remote_dma(T.lq[:, dst], sq, T.sem["aq" + n], T.sem.lsem, pid, rid, m_all)
            return None
        op("sendq" + n, "G", send_q, ["sq" + n], ["lq" + nn], (), ("r", 0), "aq" + n)
        if last:
            mm(k("tl"), k("TL"), [(Db[0:8, 0:128], T.kv[:, 0:8], on[:], 128)], [k("on"), "kv"], [k("d")], [bD])
            vs(k("ytb"), T.ytb[0:8, 256 + c * NL:256 + c * NL + NL], Db[0:8, 0:128], 1.0, 0.0, [k("d")], [k("ytb")], 128, [bD])
            dma("stq%d" % c, "Y", [(T.yq[:, r], T.lq[:, dst])], ["lq" + nn], ["yq%d" % c], "st", 32768)
            if c == CH - 1:
                dma("stb", "Y", [(T.yt[:, 1024:1280], T.ytb[0:8, 256:512])], ["ytb0", "ytb1"], ["ytbd"], "st", 8192)

    for t in range(STEPS):
        for c in range(CH):
            step(t, c)
    return ops


def depend(ops):
    wr, rds, bank = {}, {}, {}
    for o in ops:
        d, soft = set(), set()
        for k in o["rd"]:
            if k[0] == "+":
                soft.add(wr[k[1:]])
            elif k in wr:
                d.add(wr[k])
        for k in o["wr"]:
            if k in wr:
                d.add(wr[k])
            d.update(rds.get(k, ()))
        for b in o["banks"]:
            turn = bank.setdefault(b, ["", [], []])
            if turn[0] != o["qs"] or len(o["qs"]) > 1:
                turn[0], turn[1], turn[2] = o["qs"], turn[2], []
            d.update(turn[1])
            turn[2].append(o["i"])
        for k in o["rd"]:
            rds.setdefault(k, []).append(o["i"])
        for k in o["wr"]:
            wr[k] = o["i"]
            rds[k] = []
        d.discard(o["i"])
        o["deps"], o["soft"] = sorted(d), sorted(soft - d)


ABC = "0123456789ABCDEFGHIJKLMNOPQRSTUVWXYZabcdefghijklmnopqrstuvwxyz"
ORDER = "0004021K060S1y080K0A0C1w0E0G0a0I1A0M1C1u0c0U1E1b1G1c181o1X1e1I211g2C1Z1q1j0O1l0Q1R1N2K1T2G1P1V2M2g1m2E2I224m2m1s240g2W2R2O342T362c0W562a2V2Y4U4Z4W4R2o0i3G2q2w2y2s3M3I3E3A302e3O4S544P4c3K380Y320e3C2u4a2i2k3Q4w5M4y4o503S4q5G4s3a3U3W3c5E0m3Z0o5O5K3e5A58525I4u3g5C4g4e3i4i5Q4k3k5S5U5W3q0k5a3v3y2A3t3w3m5Z280s5c26403o425e445g460q6k485i6R4A8i5k6P4C5q5m4E4H5v6S4I4K5s5p6e4M0y6M6L5w5y6U106X608O8J6264726m7K0u6o7C6q7E6u6w7I6Y6y66740w786s7G8T687M6a7A768R707O6A6g6D6i8V7Q7S8N6E7U6G7Y168L6c6I8c7a7W7c7e9G948s7g8k9A7iAg7p7k7q90128m928W8u7m7t14968o9I7u7w8w9C7yAH808q829K8Y9E8y9884AL8e9M8g86AJ9O9Q8a889S8A9W9UAN8C9Y8EAP9aAS8GAa9cAQ9e9gAi9m9pB8B29iAqBE9q9lAyAkB4AsBGAU9sAu9uBAAm9w9yBICFA0B0AwAWBCB6AoA2CeAcBKAeAYCLA4BMBOCJA6BQA8BUCMBTAABWCHACBYCOAEBaCRBcD0CgBeCYBiBlD6BgDCEcCoBmBpCwCiD8CqCkCSBqDEBsCsBuD2BwEPCUDAByEJCyCuEKDGCmC0EDD4CaCcDIC2DKDMEFC4DOC6CWDSDQC8DUEHCADWEMCCEWDYEeEyDaF4FADcEmDiDhDeGaDmDlEQEuEgESF6EoDoEqDqFCDsEiDuF0EsDwGHFEF8GKEwEkDyGFF2EYEaFGE0GJFIFKGBE2EUFME4FQFOE6FSGDE8FUEAFWGMFYFaGwGUGcFeFhFcH2GkH8FiFlGsGeH4GmGgHAGuFmFoGoFqGyFsIBH6FuGOHCGQGiH0GqFwIYI9GWHEGYGSFyHGHIG0HKG2HNHOIKIDG4HQG6HSIFIGG8ISHUIIHWHYIaHhHiJ0IuHaIiJ6HeHdIqIcJ2IkHkImIwHmJ8IeHoHqIMKLHsJAIOIyIoIgHuJ4IsKoKPIUIWHwJCHyKTI0JGKRJEI2JIKNI4JMJKIQJOI6KiKUKXJQJSKqKyJUJmJjL6KsLOKYL0KuLGLILMLAL8LQL2KwLCJlJWLKKaL4LELSKkKmJYKcJpLULWJaLYJcLaLcKfJeLeJqJsKgLgJuLiJwLkLmM3M0JgM4LzJyLoM6K0M8MAK2MCK4LqMEK6MGLsK8KEMIKHLuKAMKMMKCMOMUMQMXMSMaLwKIMY"
PLAN = {}


def rank_program(g, core, T, topo):
    rank = T.rank_of(core)
    if rank is None:
        return
    ops = make_ops(g, T, topo, core, rank)
    depend(ops)
    code = [ABC.index(ORDER[x]) * 62 + ABC.index(ORDER[x + 1]) for x in range(0, len(ORDER), 2)] or range(0, 2 * len(ops), 2)
    order, qof = [x // 2 for x in code], [""] * len(ops)
    for x in code:
        qof[x // 2] = ops[x // 2]["qs"][x % 2]
    PLAN.update(ops=ops, order=order, q=qof)
    eng = {"V": g.vector, "S": g.scalar, "P": g.tensor, "G": g, "Y": g.sync}
    known = {q: {} for q in eng}
    count = {"V": 0, "S": 0, "P": 0, "G": 0}
    snap, token, stores, lsem = {}, {}, 0, 0
    for i in order:
        o, q = ops[i], qof[i]
        kn, toks = known[q], []
        for d in o["deps"]:
            if not (qof[d] == "P" and q == "P"):
                toks += token[d]
        for s, v in sorted(toks, key=lambda x: (-x[1], x[0])):
            if kn.get(s, 0) < v:
                eng[q].wait_ge(T.sem[s], v)
                kn[s] = v
                for s2, v2 in snap.get((s, v), {}).items():
                    kn[s2] = max(kn.get(s2, 0), v2)
        out = o["fn"](q)
        if out is None:
            lsem += 16
            token[i] = [(o["sem"], 16)]
            continue
        if o["sem"]:
            for x in out:
                x.then_inc(T.sem[o["sem"]], 16)
            if o["sem"] == "st":
                stores += 16 * len(out)
                token[i] = []
                continue
            token[i] = [(o["sem"], 16 * len(out))]
        else:
            out[-1].then_inc(T.sem[q], 1)
            count[q] += 1
            token[i] = [(q, count[q])]
        snap[token[i][0]] = dict(kn)
    for s in sorted(count):
        g.wait_ge(T.sem[s], count[s])
    g.wait_ge(T.sem.lsem, lsem)
    g.wait_ge(T.sem.st, stores)
